import numpy as np
import ml_dtypes


def mxq(x, axis, fmt="e4m3"):
    dtype, down = {"e4m3": (ml_dtypes.float8_e4m3fn, 7), "e5m2": (ml_dtypes.float8_e5m2, 14)}[fmt]
    v = np.moveaxis(np.asarray(x, np.float32).astype(ml_dtypes.bfloat16).astype(np.float64), axis, -1)
    blocks = v.reshape(v.shape[:-1] + (-1, 32))
    amax = np.abs(blocks).max(-1, keepdims=True)
    byte = np.maximum(np.where(amax > 0, np.frexp(amax)[1] - 1 + 127, 0) - down, 1)
    scale = np.exp2(byte - 127.0)
    codes = (blocks / scale).astype(np.float32).astype(dtype).astype(np.float64)
    return np.moveaxis((codes * scale).reshape(v.shape), -1, axis)


WIDE = False


def mx_kscale(k):
    if not WIDE:
        return np.ones(k)
    levels = np.array([10, -10, 5, -5, 0])
    if k % 512:
        return np.exp2(np.random.permutation(np.resize(levels, k // 32))).repeat(32)
    a = np.empty((k // 512, 16))
    for p in range(k // 512):
        a[p, :8] = np.random.permutation(np.resize(levels, 8))
        for g in range(8):
            far = levels[np.abs(levels - a[p, g]) >= 10]
            a[p, g + 8] = far[np.random.randint(len(far))]
    return np.exp2(a.ravel()).repeat(32)


def f64(x):
    return np.asarray(x).astype(np.float64)


def striped(idx):
    return np.tile(idx.reshape(-1, 16).T, (8, 1)).astype(np.uint16)


def unstriped(offs):
    return offs[:16].T.reshape(-1).astype(np.int64)


E2M1 = np.array([0.0, 0.5, 1.0, 1.5, 2.0, 3.0, 4.0, 6.0, -0.0, -0.5, -1.0, -1.5, -2.0, -3.0, -4.0, -6.0])


def pack_fp4(w):
    k, n = w.shape
    w = f64(np.asarray(w, np.float32).astype(ml_dtypes.bfloat16)).reshape(k // 32, 32, n)
    amax = np.abs(w).max(1)
    mant, ex = np.frexp(amax / 6.0)
    byte = np.clip(np.where(amax > 0, np.where(mant > 0.5, ex, ex - 1) + 127, 1), 1, 254)
    scaled = (w * np.exp2(127.0 - byte)[:, None, :]).reshape(k, n).astype(np.float32)
    c = np.ascontiguousarray(scaled.reshape(k // 512, 128, 4, n).transpose(0, 1, 3, 2)).astype(ml_dtypes.float4_e2m1fn).view(np.uint8) & 0xF
    words = (c[..., 0::2] | (c[..., 1::2] << 4)).reshape(k // 512, 128, 2 * n)
    return np.ascontiguousarray(words), np.ascontiguousarray(byte.astype(np.uint8).reshape(k // 512, 16, n))


def unpack_fp4(words, scales):
    g, _, n = scales.shape
    words = np.ascontiguousarray(words).reshape(g, 128, n, 2)
    nib = np.empty((g, 128, n, 4), np.uint8)
    nib[..., 0::2] = words & 0xF
    nib[..., 1::2] = words >> 4
    vals = E2M1[nib] * np.repeat(np.exp2(scales.astype(np.float64) - 127.0), 8, axis=1)[..., None]
    return vals.transpose(0, 1, 3, 2).reshape(g * 512, n)


def planes(y):
    n, m = y.shape
    v = y.astype(np.float32).astype(ml_dtypes.bfloat16).astype(np.float64).reshape(n // 32, 32, m)
    top = np.abs(v).max(1)
    byte = np.clip(np.where(top > 0, np.frexp(top)[1] - 1 + 127 - 7, 1), 1, 254)
    codes = (v * np.exp2(127.0 - byte)[:, None, :]).reshape(n, m).astype(np.float32).astype(ml_dtypes.float8_e4m3fn).view(np.uint8)
    words = codes.reshape(n // 512, 128, 4, m).transpose(0, 1, 3, 2)
    return np.ascontiguousarray(words), np.ascontiguousarray(byte.astype(np.uint8).reshape(n // 512, 16, m))


K, T, N, U = 1024, 1024, 512, 2048
P = 2 ** 7


def setup_inputs():
    n = np.random.standard_normal
    s = mx_kscale(K)[:, None]
    packed_xT = pack_fp4(n((K, T)) * s)
    return {
        "x_words": packed_xT[0],
        "x_scales": packed_xT[1],
        "mem": n((N, U)).astype(np.float32),
        "w1": (n((K, N)) / np.sqrt(K) / s).astype(np.float32),
        "old": np.tile(np.random.uniform(0.5, 0.95, T), (P, 1)).astype(np.float32),
        "new": np.tile(np.random.uniform(0.05, 0.5, T), (P, 1)).astype(np.float32),
        "slot": striped(np.random.permutation(U)[:T]),
    }


def reference(x_words, x_scales, mem, w1, old, new, slot):
    xq = unpack_fp4(x_words, x_scales)
    y = mxq(f64(w1), 0, "e4m3").T @ xq
    out = f64(mem).copy()
    out[:, unstriped(slot)] = f64(mem)[:, unstriped(slot)] * f64(old)[:1] + y * f64(new)[:1]
    return (out,) + planes(out)

@@ -1,0 +1,257 @@
+from contextlib import ExitStack
+
+import concourse.mybir as mybir
+from concourse.masks import make_identity
+
+K, T, N, U = 1024, 1024, 512, 2048
+FLOPS = 2 * K * N * T
+
+F32 = mybir.dt.float32
+BF16 = mybir.dt.bfloat16
+I32 = mybir.dt.int32
+U32 = mybir.dt.uint32
+U16 = mybir.dt.uint16
+U8 = mybir.dt.uint8
+FP8X4 = mybir.dt.float8_e4m3fn_x4
+FP4X4 = mybir.dt.float4_e2m1fn_x4
+COPY = mybir.ActivationFunctionType.Copy
+MULT = mybir.AluOpType.mult
+ADD = mybir.AluOpType.add
+
+P = 128
+PASSES = K // 512
+BLOCKS = T // P
+HALF_T = T // 2
+HALF_N = N // 2
+CHUNKS = 4
+CW = U // CHUNKS
+
+
+def tile_picked_wema_none_lo_kernel(tc, x_words, x_scales, mem, w1, old, new, slot, out_0, out_1, out_2):
+    nc = tc.nc
+
+    def rows_of(ap, t):
+        if t < 2:
+            return ap.rearrange("(h q e) c -> h e q c", h=2, e=2)[t, 0]
+        return ap.rearrange("(l r) c -> r l c", r=4)[2 * (t - 2) + 1]
+
+    with ExitStack() as ctx:
+        keep = ctx.enter_context(tc.tile_pool(name="keep", bufs=1))
+        ps_mx = ctx.enter_context(tc.psum_pool(name="ps_mx", bufs=4))
+        ps_tr = ctx.enter_context(tc.psum_pool(name="ps_tr", bufs=4))
+
+        offs = keep.tile([P, T // 16], U16, name="offs")
+        ident = keep.tile([P, P], F32, name="ident")
+        rows = keep.tile([P, P], F32, name="rows")
+        xs = keep.tile([P, PASSES * T], U8, name="xs", align_bytes=64)
+        nc.gpsimd.memset(rows[:], 0.0)
+        nc.vector.memset(xs[:].bitcast(U32), 0)
+        make_identity(nc, ident[:])
+
+        xw_dram = x_words.bitcast(I32)
+        xs_dram = x_scales.bitcast(I32)
+
+        def load_w(h, z):
+            raw = keep.tile([P, 4, HALF_N], F32, name="wraw%d%d" % (h, z), tag="stage%d" % z, align_bytes=64)
+            src = w1[512 * z : 512 * (z + 1), HALF_N * h : HALF_N * (h + 1)]
+            nc.sync.dma_start(out=raw[:], in_=src.rearrange("(p j) n -> p j n", j=4))
+            return raw
+
+        def load_x(h, tag):
+            xw = keep.tile([P, PASSES, 2 * HALF_T], U8, name="xw%d" % h, tag=tag, align_bytes=64)
+            src = xw_dram[:, :, 256 * h : 256 * (h + 1)].rearrange("z p c -> p z c")
+            nc.sync.dma_start(out=xw[:].bitcast(I32), in_=src)
+            return xw
+
+        def load_mem(t, tag):
+            win = keep.tile([P, U], F32, name="win%d" % t, tag=tag, align_bytes=64)
+            nc.sync.dma_start(out=win[:], in_=rows_of(mem, t))
+            return win
+
+        def group_w(h, z, raw, tag, copy):
+            wg = keep.tile([P, 4 * HALF_N], BF16, name="wg%d%d" % (h, z), tag=tag, align_bytes=64)
+            copy(
+                wg[:].rearrange("p (e c a j) -> p c j a e", e=2, a=2, j=4),
+                raw[:].rearrange("p j (c a e) -> p c j a e", a=2, e=2),
+            )
+            return wg
+
+        def quant_w(h, z, wg):
+            codes = keep.tile([P, HALF_N], U32, name="wc%d%d" % (h, z), align_bytes=64)
+            scales = keep.tile([P, HALF_N], U8, name="ws%d%d" % (h, z), align_bytes=64)
+            nc.vector.quantize_mx(out=codes[:].bitcast(FP8X4), scales=scales[:], in_=wg[:])
+            return codes, scales
+
+        nc.sync.dma_start(offs[:], slot)
+        nc.scalar.dma_start(out=rows[0:BLOCKS, :], in_=old[0:1, :].rearrange("o (b n) -> (o b) n", n=P))
+        nc.scalar.dma_start(out=rows[BLOCKS : 2 * BLOCKS, :], in_=new[0:1, :].rearrange("o (b n) -> (o b) n", n=P))
+        raw = {}
+        raw[0, 0] = load_w(0, 0)
+        raw[0, 1] = load_w(0, 1)
+        for q in range(4):
+            nc.scalar.dma_start(
+                out=xs[32 * q : 32 * q + 4, :].bitcast(I32).rearrange("q (z c) -> q z c", z=PASSES),
+                in_=xs_dram[:, 4 * q : 4 * q + 4, :].rearrange("z q c -> q z c"),
+            )
+        xw = {}
+        xw[0] = load_x(0, "xw0")
+        win = {}
+        win[0] = load_mem(0, "win0")
+
+        cols_ps = ps_tr.tile([P, 512], F32, name="tr")
+        nc.tensor.transpose(cols_ps[:, 0:P], rows[:], ident[:])
+        cols = keep.tile([P, 2 * BLOCKS], F32, name="cols")
+        nc.scalar.copy(cols[:], cols_ps[:, 0 : 2 * BLOCKS])
+        old_b = keep.tile([P, T], F32, name="old_b")
+        for h in range(2):
+            ps = ps_tr.tile([P, 512], F32, name="tr")
+            for i in range(4):
+                b = 4 * h + i
+                nc.tensor.transpose(ps[:, P * i : P * (i + 1)], cols[:, b : b + 1].to_broadcast([P, P]), ident[:])
+            nc.scalar.copy(old_b[:, HALF_T * h : HALF_T * (h + 1)], ps[:])
+
+        wq = {}
+        for z in range(PASSES):
+            wg = group_w(0, z, raw[0, z], "early%d" % z, nc.vector.tensor_copy)
+            wq[0, z] = quant_w(0, z, wg)
+
+        def product(out, b, h, e):
+            for z in range(PASSES):
+                codes, scales = wq[h, z]
+                i = b % 4
+                nc.tensor.matmul_mx(
+                    out=out,
+                    lhsT=xw[b // 4][:, z, 2 * P * i : 2 * P * (i + 1)].bitcast(FP4X4),
+                    lhsT_scale=xs[:, T * z + P * b : T * z + P * (b + 1)],
+                    rhs=codes[:, P * e : P * (e + 1)].bitcast(FP8X4),
+                    rhs_scale=scales[:, P * e : P * (e + 1)],
+                    start=(z == 0),
+                    stop=(z == PASSES - 1),
+                )
+
+        def turn_back(name, srcs, tag):
+            ps = ps_tr.tile([P, 512], F32, name="tr")
+            for i in range(4):
+                nc.tensor.transpose(ps[:, P * i : P * (i + 1)], srcs[i], ident[:])
+            ny = keep.tile([P, HALF_T], F32, name=name, tag=tag)
+            nc.scalar.copy(ny[:], ps[:])
+            return ny
+
+        def even_y(t, s):
+            ps = ps_mx.tile([P, 512], F32, name="mx")
+            for i in range(4):
+                product(ps[:, P * i : P * (i + 1)], 4 * s + i, t, 0)
+            yt = keep.tile([P, 4, P], F32, name="yt%d%d" % (t, s))
+            for i in range(4):
+                b = 4 * s + i
+                nc.scalar.activation(yt[:, i, :], ps[:, P * i : P * (i + 1)], COPY, scale=cols[:, BLOCKS + b : BLOCKS + b + 1])
+            return turn_back("ny%d%d" % (t, s), [yt[:, i, :] for i in range(4)], "ny%d%d" % (t, s))
+
+        def gather(t, s):
+            g = keep.tile([P, HALF_T], F32, name="g%d%d" % (t, s), tag="g%d" % s)
+            nc.vector.tensor_tensor(
+                g[:], win[t][:].indirect(offs[:, 32 * s : 32 * (s + 1)]), old_b[:, HALF_T * s : HALF_T * (s + 1)], MULT
+            )
+            return g
+
+        def scatter(t, s, g, ny):
+            nc.vector.tensor_tensor(win[t][:].indirect(offs[:, 32 * s : 32 * (s + 1)]), g[:], ny[:], ADD)
+
+        def store_rows(t):
+            nc.sync.dma_start(out=rows_of(out_0, t), in_=win[t][:])
+
+        even = [keep.tile([P, 2, CW], F32, name="even%d" % k, tag="even%d" % k) for k in range(CHUNKS)]
+
+        def move_even(t):
+            for k in range(CHUNKS):
+                for a in range(2):
+                    nc.sync.dma_start(out=even[k][64 * t : 64 * (t + 1), a, :], in_=win[t][a:P:2, CW * k : CW * (k + 1)])
+
+        ny = {}
+        g = {}
+        ny[0, 0] = even_y(0, 0)
+        g[0, 0] = gather(0, 0)
+        g[0, 1] = gather(0, 1)
+        scatter(0, 0, g[0, 0], ny[0, 0])
+
+        raw[1, 0] = load_w(1, 0)
+        raw[1, 1] = load_w(1, 1)
+        xw[1] = load_x(1, "early0")
+        win[1] = load_mem(1, "early1")
+        for z in range(PASSES):
+            wg = group_w(1, z, raw[1, z], "late%d" % z, nc.scalar.copy)
+            wq[1, z] = quant_w(1, z, wg)
+        win[2] = load_mem(2, "stage0")
+        win[3] = load_mem(3, "stage1")
+
+        ny[0, 1] = even_y(0, 1)
+        g[1, 0] = gather(1, 0)
+        scatter(0, 1, g[0, 1], ny[0, 1])
+        move_even(0)
+        store_rows(0)
+
+        ny[1, 0] = even_y(1, 0)
+        ny[1, 1] = even_y(1, 1)
+        yo = keep.tile([P, BLOCKS, 2, P], F32, name="yo")
+        for pair in range(BLOCKS // 2):
+            ps = ps_mx.tile([P, 512], F32, name="mx")
+            for i in range(2):
+                for h in range(2):
+                    product(ps[:, P * (2 * i + h) : P * (2 * i + h + 1)], 2 * pair + i, h, 1)
+            for i in range(2):
+                b = 2 * pair + i
+                nc.scalar.activation(
+                    yo[:, b, :, :],
+                    ps[:, 2 * P * i : 2 * P * (i + 1)].rearrange("p (l a) -> p a l", a=2),
+                    COPY,
+                    scale=cols[:, BLOCKS + b : BLOCKS + b + 1],
+                )
+
+        def odd_y(t, s, tag):
+            return turn_back("ny%d%d" % (t, s), [yo[:, 4 * s + i, t - 2, :] for i in range(4)], tag)
+
+        ny[2, 0] = odd_y(2, 0, "ny20")
+        ny[3, 0] = odd_y(3, 0, "ny30")
+
+        g[1, 1] = gather(1, 1)
+        scatter(1, 0, g[1, 0], ny[1, 0])
+        g[2, 0] = gather(2, 0)
+        scatter(1, 1, g[1, 1], ny[1, 1])
+        move_even(1)
+        store_rows(1)
+
+        fin = [keep.tile([P, CW, 4], BF16, name="fin%d" % k, align_bytes=64) for k in range(CHUNKS)]
+        for k in range(CHUNKS):
+            nc.scalar.copy(fin[k][:, :, 0:4:2], even[k][:].rearrange("p a c -> p c a"))
+            if k == 0:
+                ny[2, 1] = odd_y(2, 1, "even0")
+        ny[3, 1] = odd_y(3, 1, "even3")
+
+        g[2, 1] = gather(2, 1)
+        scatter(2, 0, g[2, 0], ny[2, 0])
+        g[3, 0] = gather(3, 0)
+        scatter(2, 1, g[2, 1], ny[2, 1])
+        store_rows(2)
+        for k in range(CHUNKS):
+            nc.scalar.copy(fin[k][:, :, 1], win[2][:, CW * k : CW * (k + 1)])
+        g[3, 1] = gather(3, 1)
+        scatter(3, 0, g[3, 0], ny[3, 0])
+        scatter(3, 1, g[3, 1], ny[3, 1])
+        store_rows(3)
+
+        for k in range(CHUNKS):
+            copy = nc.vector.tensor_copy if k < 2 else nc.scalar.copy
+            copy(fin[k][:, :, 3], win[3][:, CW * k : CW * (k + 1)])
+        osc = keep.tile([P, U], U8, name="osc", align_bytes=64)
+        words_dram = out_1[0].rearrange("p c r -> p (c r)").bitcast(I32)
+        for k in (0, 2, 1, 3):
+            words = keep.tile([P, CW], U32, name="words%d" % k, align_bytes=64)
+            nc.vector.quantize_mx(
+                out=words[:].bitcast(FP8X4),
+                scales=osc[:, CW * k : CW * (k + 1)],
+                in_=fin[k][:].rearrange("p c r -> p (c r)"),
+            )
+            nc.sync.dma_start(out=words_dram[:, CW * k : CW * (k + 1)], in_=words[:].bitcast(I32))
+        scales_dram = out_2[0].bitcast(I32)
+        for q in range(4):
+            nc.scalar.dma_start(out=scales_dram[4 * q : 4 * q + 4, :], in_=osc[32 * q : 32 * q + 4, :].bitcast(I32))

@@ -82,22 +82,27 @@ def tile_picked_wema_none_lo_kernel(tc, x_words, x_scales, mem, w1, old, new, sl
             nc.vector.quantize_mx(out=codes[:].bitcast(FP8X4), scales=scales[:], in_=wg[:])
             return codes, scales
 
-        nc.sync.dma_start(offs[:], slot)
-        nc.scalar.dma_start(out=rows[0:BLOCKS, :], in_=old[0:1, :].rearrange("o (b n) -> (o b) n", n=P))
-        nc.scalar.dma_start(out=rows[BLOCKS : 2 * BLOCKS, :], in_=new[0:1, :].rearrange("o (b n) -> (o b) n", n=P))
+        row_stage = keep.tile([2 * BLOCKS, P], F32, name="row_stage")
+        xs_stage = keep.tile([P, PASSES * T // 4], I32, name="xs_stage")
+        nc.scalar.dma_start(out=row_stage[0:BLOCKS, :], in_=old[0:1, :].rearrange("o (b n) -> (o b) n", n=P))
+        nc.scalar.dma_start(out=row_stage[BLOCKS : 2 * BLOCKS, :], in_=new[0:1, :].rearrange("o (b n) -> (o b) n", n=P))
+        for q in range(4):
+            nc.sync.dma_start(
+                out=xs_stage[32 * q : 32 * q + 4, :].rearrange("q (z c) -> q z c", z=PASSES),
+                in_=xs_dram[:, 4 * q : 4 * q + 4, :].rearrange("z q c -> q z c"),
+            )
         raw = {}
         raw[0, 0] = load_w(0, 0)
         raw[0, 1] = load_w(0, 1)
-        for q in range(4):
-            nc.scalar.dma_start(
-                out=xs[32 * q : 32 * q + 4, :].bitcast(I32).rearrange("q (z c) -> q z c", z=PASSES),
-                in_=xs_dram[:, 4 * q : 4 * q + 4, :].rearrange("z q c -> q z c"),
-            )
         xw = {}
         xw[0] = load_x(0, "xw0")
+        nc.sync.dma_start(offs[:], slot)
         win = {}
         win[0] = load_mem(0, "win0")
 
+        for q in range(4):
+            nc.vector.tensor_copy(xs[32 * q : 32 * q + 4, :].bitcast(I32), xs_stage[32 * q : 32 * q + 4, :])
+        nc.scalar.copy(rows[0 : 2 * BLOCKS, :], row_stage[:])
         cols_ps = ps_tr.tile([P, 512], F32, name="tr")
         nc.tensor.transpose(cols_ps[:, 0:P], rows[:], ident[:])
         cols = keep.tile([P, 2 * BLOCKS], F32, name="cols")
@@ -115,8 +120,8 @@ def tile_picked_wema_none_lo_kernel(tc, x_words, x_scales, mem, w1, old, new, sl
             wg = group_w(0, z, raw[0, z], "early%d" % z, nc.vector.tensor_copy)
             wq[0, z] = quant_w(0, z, wg)
 
-        def product(out, b, h, e):
-            for z in range(PASSES):
+        def product(out, b, h, e, passes=range(PASSES)):
+            for z in passes:
                 codes, scales = wq[h, z]
                 i = b % 4
                 nc.tensor.matmul_mx(
@@ -147,8 +152,18 @@ def tile_picked_wema_none_lo_kernel(tc, x_words, x_scales, mem, w1, old, new, sl
                 nc.scalar.activation(yt[:, i, :], ps[:, P * i : P * (i + 1)], COPY, scale=cols[:, BLOCKS + b : BLOCKS + b + 1])
             return turn_back("ny%d%d" % (t, s), [yt[:, i, :] for i in range(4)], "ny%d%d" % (t, s))
 
-        def gather(t, s):
-            g = keep.tile([P, HALF_T], F32, name="g%d%d" % (t, s), tag="g%d" % s)
+        def first_y():
+            banks = [ps_mx.tile([P, 512], F32, name="mx") for i in range(4)]
+            for z in range(PASSES):
+                for i in range(4):
+                    product(banks[i][:, 0:P], i, 0, 0, [z])
+            yt = keep.tile([P, 4, P], F32, name="yt00")
+            for i in range(4):
+                nc.scalar.activation(yt[:, i, :], banks[i][:, 0:P], COPY, scale=cols[:, BLOCKS + i : BLOCKS + i + 1])
+            return turn_back("ny00", [yt[:, i, :] for i in range(4)], "ny00")
+
+        def gather(t, s, tag):
+            g = keep.tile([P, HALF_T], F32, name="g%d%d" % (t, s), tag=tag)
             nc.vector.tensor_tensor(
                 g[:], win[t][:].indirect(offs[:, 32 * s : 32 * (s + 1)]), old_b[:, HALF_T * s : HALF_T * (s + 1)], MULT
             )
@@ -169,9 +184,9 @@ def tile_picked_wema_none_lo_kernel(tc, x_words, x_scales, mem, w1, old, new, sl
 
         ny = {}
         g = {}
-        ny[0, 0] = even_y(0, 0)
-        g[0, 0] = gather(0, 0)
-        g[0, 1] = gather(0, 1)
+        ny[0, 0] = first_y()
+        g[0, 0] = gather(0, 0, "g0")
+        g[0, 1] = gather(0, 1, "g1")
         scatter(0, 0, g[0, 0], ny[0, 0])
 
         raw[1, 0] = load_w(1, 0)
@@ -185,7 +200,7 @@ def tile_picked_wema_none_lo_kernel(tc, x_words, x_scales, mem, w1, old, new, sl
         win[3] = load_mem(3, "stage1")
 
         ny[0, 1] = even_y(0, 1)
-        g[1, 0] = gather(1, 0)
+        g[1, 0] = gather(1, 0, "g0")
         scatter(0, 1, g[0, 1], ny[0, 1])
         move_even(0)
         store_rows(0)
@@ -211,11 +226,13 @@ def tile_picked_wema_none_lo_kernel(tc, x_words, x_scales, mem, w1, old, new, sl
             return turn_back("ny%d%d" % (t, s), [yo[:, 4 * s + i, t - 2, :] for i in range(4)], tag)
 
         ny[2, 0] = odd_y(2, 0, "ny20")
+        ny[2, 1] = odd_y(2, 1, "ny21")
         ny[3, 0] = odd_y(3, 0, "ny30")
+        ny[3, 1] = odd_y(3, 1, "ny31")
 
-        g[1, 1] = gather(1, 1)
+        g[1, 1] = gather(1, 1, "g1")
         scatter(1, 0, g[1, 0], ny[1, 0])
-        g[2, 0] = gather(2, 0)
+        g[2, 0] = gather(2, 0, "g0")
         scatter(1, 1, g[1, 1], ny[1, 1])
         move_even(1)
         store_rows(1)
@@ -223,18 +240,16 @@ def tile_picked_wema_none_lo_kernel(tc, x_words, x_scales, mem, w1, old, new, sl
         fin = [keep.tile([P, CW, 4], BF16, name="fin%d" % k, align_bytes=64) for k in range(CHUNKS)]
         for k in range(CHUNKS):
             nc.scalar.copy(fin[k][:, :, 0:4:2], even[k][:].rearrange("p a c -> p c a"))
-            if k == 0:
-                ny[2, 1] = odd_y(2, 1, "even0")
-        ny[3, 1] = odd_y(3, 1, "even3")
 
-        g[2, 1] = gather(2, 1)
+
         scatter(2, 0, g[2, 0], ny[2, 0])
-        g[3, 0] = gather(3, 0)
+        g[3, 0] = gather(3, 0, "g0")
+        g[2, 1] = gather(2, 1, "even0")
         scatter(2, 1, g[2, 1], ny[2, 1])
         store_rows(2)
         for k in range(CHUNKS):
             nc.scalar.copy(fin[k][:, :, 1], win[2][:, CW * k : CW * (k + 1)])
-        g[3, 1] = gather(3, 1)
+        g[3, 1] = gather(3, 1, "even1")
         scatter(3, 0, g[3, 0], ny[3, 0])
         scatter(3, 1, g[3, 1], ny[3, 1])
         store_rows(3)
@@ -254,4 +269,5 @@ def tile_picked_wema_none_lo_kernel(tc, x_words, x_scales, mem, w1, old, new, sl
             nc.sync.dma_start(out=words_dram[:, CW * k : CW * (k + 1)], in_=words[:].bitcast(I32))
         scales_dram = out_2[0].bitcast(I32)
         for q in range(4):
-            nc.scalar.dma_start(out=scales_dram[4 * q : 4 * q + 4, :], in_=osc[32 * q : 32 * q + 4, :].bitcast(I32))
+            queue = nc.scalar if q % 2 == 0 else nc.sync
+            queue.dma_start(out=scales_dram[4 * q : 4 * q + 4, :], in_=osc[32 * q : 32 * q + 4, :].bitcast(I32))

@@ -19,21 +19,21 @@ MULT = mybir.AluOpType.mult
 ADD = mybir.AluOpType.add
 
 P = 128
-PASSES = K // 512
+PACK = 4
+PASSES = K // (P * PACK)
 BLOCKS = T // P
+HALF_BLOCKS = BLOCKS // 2
 HALF_T = T // 2
-HALF_N = N // 2
 CHUNKS = 4
 CW = U // CHUNKS
+ORDER = (2, 0, 1, 3)
 
 
 def tile_picked_wema_none_lo_kernel(tc, x_words, x_scales, mem, w1, old, new, slot, out_0, out_1, out_2):
     nc = tc.nc
 
-    def rows_of(ap, t):
-        if t < 2:
-            return ap.rearrange("(h q e) c -> h e q c", h=2, e=2)[t, 0]
-        return ap.rearrange("(l r) c -> r l c", r=4)[2 * (t - 2) + 1]
+    def plane_rows(ap, r):
+        return ap.rearrange("(l r) c -> r l c", r=PACK)[r]
 
     with ExitStack() as ctx:
         keep = ctx.enter_context(tc.tile_pool(name="keep", bufs=1))
@@ -51,54 +51,36 @@ def tile_picked_wema_none_lo_kernel(tc, x_words, x_scales, mem, w1, old, new, sl
         xw_dram = x_words.bitcast(I32)
         xs_dram = x_scales.bitcast(I32)
 
-        def load_w(h, z):
-            raw = keep.tile([P, 4, HALF_N], F32, name="wraw%d%d" % (h, z), tag="stage%d" % z, align_bytes=64)
-            src = w1[512 * z : 512 * (z + 1), HALF_N * h : HALF_N * (h + 1)]
-            nc.sync.dma_start(out=raw[:], in_=src.rearrange("(p j) n -> p j n", j=4))
-            return raw
-
-        def load_x(h, tag):
-            xw = keep.tile([P, PASSES, 2 * HALF_T], U8, name="xw%d" % h, tag=tag, align_bytes=64)
-            src = xw_dram[:, :, 256 * h : 256 * (h + 1)].rearrange("z p c -> p z c")
-            nc.sync.dma_start(out=xw[:].bitcast(I32), in_=src)
-            return xw
-
-        def load_mem(t, tag):
-            win = keep.tile([P, U], F32, name="win%d" % t, tag=tag, align_bytes=64)
-            nc.sync.dma_start(out=win[:], in_=rows_of(mem, t))
-            return win
-
-        def group_w(h, z, raw, tag, copy):
-            wg = keep.tile([P, 4 * HALF_N], BF16, name="wg%d%d" % (h, z), tag=tag, align_bytes=64)
-            copy(
-                wg[:].rearrange("p (e c a j) -> p c j a e", e=2, a=2, j=4),
-                raw[:].rearrange("p j (c a e) -> p c j a e", a=2, e=2),
-            )
-            return wg
-
-        def quant_w(h, z, wg):
-            codes = keep.tile([P, HALF_N], U32, name="wc%d%d" % (h, z), align_bytes=64)
-            scales = keep.tile([P, HALF_N], U8, name="ws%d%d" % (h, z), align_bytes=64)
-            nc.vector.quantize_mx(out=codes[:].bitcast(FP8X4), scales=scales[:], in_=wg[:])
-            return codes, scales
-
         row_stage = keep.tile([2 * BLOCKS, P], F32, name="row_stage")
         xs_stage = keep.tile([P, PASSES * T // 4], I32, name="xs_stage")
         nc.scalar.dma_start(out=row_stage[0:BLOCKS, :], in_=old[0:1, :].rearrange("o (b n) -> (o b) n", n=P))
         nc.scalar.dma_start(out=row_stage[BLOCKS : 2 * BLOCKS, :], in_=new[0:1, :].rearrange("o (b n) -> (o b) n", n=P))
+        raw = [keep.tile([P, PACK, N], F32, name="wraw%d" % z) for z in range(PASSES)]
+
+        def load_w(z):
+            nc.sync.dma_start(out=raw[z][:], in_=w1[512 * z : 512 * (z + 1), :].rearrange("(p j) n -> p j n", j=PACK))
+
+        load_w(0)
         for q in range(4):
             nc.sync.dma_start(
                 out=xs_stage[32 * q : 32 * q + 4, :].rearrange("q (z c) -> q z c", z=PASSES),
                 in_=xs_dram[:, 4 * q : 4 * q + 4, :].rearrange("z q c -> q z c"),
             )
-        raw = {}
-        raw[0, 0] = load_w(0, 0)
-        raw[0, 1] = load_w(0, 1)
-        xw = {}
-        xw[0] = load_x(0, "xw0")
+        load_w(1)
+        xw = [keep.tile([P, PASSES, 2 * HALF_T], U8, name="xw%d" % s, align_bytes=64) for s in range(2)]
+        win = [keep.tile([P, U], F32, name="win%d" % t, tag="win%d" % t) for t in range(PACK)]
+
+        def load_x(s):
+            src = xw_dram[:, :, 256 * s : 256 * (s + 1)].rearrange("z p c -> p z c")
+            nc.sync.dma_start(out=xw[s][:].bitcast(I32), in_=src)
+
+        load_x(0)
         nc.sync.dma_start(offs[:], slot)
-        win = {}
-        win[0] = load_mem(0, "win0")
+        nc.sync.dma_start(out=win[0][:], in_=plane_rows(mem, ORDER[0]))
+        nc.sync.dma_start(out=win[1][:], in_=plane_rows(mem, ORDER[1]))
+        load_x(1)
+        for t in range(2, PACK):
+            nc.sync.dma_start(out=win[t][:], in_=plane_rows(mem, ORDER[t]))
 
         for q in range(4):
             nc.vector.tensor_copy(xs[32 * q : 32 * q + 4, :].bitcast(I32), xs_stage[32 * q : 32 * q + 4, :])
@@ -108,62 +90,64 @@ def tile_picked_wema_none_lo_kernel(tc, x_words, x_scales, mem, w1, old, new, sl
         cols = keep.tile([P, 2 * BLOCKS], F32, name="cols")
         nc.scalar.copy(cols[:], cols_ps[:, 0 : 2 * BLOCKS])
         old_b = keep.tile([P, T], F32, name="old_b")
-        for h in range(2):
+        for s in range(2):
             ps = ps_tr.tile([P, 512], F32, name="tr")
-            for i in range(4):
-                b = 4 * h + i
+            for i in range(HALF_BLOCKS):
+                b = HALF_BLOCKS * s + i
                 nc.tensor.transpose(ps[:, P * i : P * (i + 1)], cols[:, b : b + 1].to_broadcast([P, P]), ident[:])
-            nc.scalar.copy(old_b[:, HALF_T * h : HALF_T * (h + 1)], ps[:])
+            nc.scalar.copy(old_b[:, HALF_T * s : HALF_T * (s + 1)], ps[:])
 
-        wq = {}
+        wq = []
         for z in range(PASSES):
-            wg = group_w(0, z, raw[0, z], "early%d" % z, nc.vector.tensor_copy)
-            wq[0, z] = quant_w(0, z, wg)
+            wg = keep.tile([P, PACK * N], BF16, name="wg%d" % z, align_bytes=64)
+            nc.vector.tensor_copy(
+                wg[:].rearrange("p (r l j) -> p l j r", r=PACK, j=PACK),
+                raw[z][:].rearrange("p j (l r) -> p l j r", r=PACK),
+            )
+            codes = keep.tile([P, N], U32, name="wc%d" % z, align_bytes=64)
+            scales = keep.tile([P, N], U8, name="ws%d" % z, align_bytes=64)
+            nc.vector.quantize_mx(out=codes[:].bitcast(FP8X4), scales=scales[:], in_=wg[:])
+            wq.append((codes, scales))
 
-        def product(out, b, h, e, passes=range(PASSES)):
-            for z in passes:
-                codes, scales = wq[h, z]
-                i = b % 4
-                nc.tensor.matmul_mx(
-                    out=out,
-                    lhsT=xw[b // 4][:, z, 2 * P * i : 2 * P * (i + 1)].bitcast(FP4X4),
-                    lhsT_scale=xs[:, T * z + P * b : T * z + P * (b + 1)],
-                    rhs=codes[:, P * e : P * (e + 1)].bitcast(FP8X4),
-                    rhs_scale=scales[:, P * e : P * (e + 1)],
-                    start=(z == 0),
-                    stop=(z == PASSES - 1),
-                )
+        def mx_pass(out, b, r, z):
+            codes, scales = wq[z]
+            s, i = divmod(b, HALF_BLOCKS)
+            nc.tensor.matmul_mx(
+                out=out,
+                lhsT=xw[s][:, z, 2 * P * i : 2 * P * (i + 1)].bitcast(FP4X4),
+                lhsT_scale=xs[:, T * z + P * b : T * z + P * (b + 1)],
+                rhs=codes[:, P * r : P * (r + 1)].bitcast(FP8X4),
+                rhs_scale=scales[:, P * r : P * (r + 1)],
+                start=(z == 0),
+                stop=(z == PASSES - 1),
+            )
 
-        def turn_back(name, srcs, tag):
+        def new_of(b):
+            return cols[:, BLOCKS + b : BLOCKS + b + 1]
+
+        def turn(srcs):
             ps = ps_tr.tile([P, 512], F32, name="tr")
-            for i in range(4):
+            for i in range(HALF_BLOCKS):
                 nc.tensor.transpose(ps[:, P * i : P * (i + 1)], srcs[i], ident[:])
+            return ps
+
+        def take(ps, name, tag):
             ny = keep.tile([P, HALF_T], F32, name=name, tag=tag)
             nc.scalar.copy(ny[:], ps[:])
             return ny
 
-        def even_y(t, s):
-            ps = ps_mx.tile([P, 512], F32, name="mx")
-            for i in range(4):
-                product(ps[:, P * i : P * (i + 1)], 4 * s + i, t, 0)
-            yt = keep.tile([P, 4, P], F32, name="yt%d%d" % (t, s))
-            for i in range(4):
-                b = 4 * s + i
-                nc.scalar.activation(yt[:, i, :], ps[:, P * i : P * (i + 1)], COPY, scale=cols[:, BLOCKS + b : BLOCKS + b + 1])
-            return turn_back("ny%d%d" % (t, s), [yt[:, i, :] for i in range(4)], "ny%d%d" % (t, s))
-
-        def first_y():
-            banks = [ps_mx.tile([P, 512], F32, name="mx") for i in range(4)]
+        def first_y(s):
+            banks = [ps_mx.tile([P, 512], F32, name="mx") for i in range(HALF_BLOCKS)]
             for z in range(PASSES):
-                for i in range(4):
-                    product(banks[i][:, 0:P], i, 0, 0, [z])
-            yt = keep.tile([P, 4, P], F32, name="yt00")
-            for i in range(4):
-                nc.scalar.activation(yt[:, i, :], banks[i][:, 0:P], COPY, scale=cols[:, BLOCKS + i : BLOCKS + i + 1])
-            return turn_back("ny00", [yt[:, i, :] for i in range(4)], "ny00")
+                for i in range(HALF_BLOCKS):
+                    mx_pass(banks[i][:, 0:P], HALF_BLOCKS * s + i, ORDER[0], z)
+            yt = keep.tile([P, HALF_BLOCKS, P], F32, name="yt%d" % s)
+            for i in range(HALF_BLOCKS):
+                nc.scalar.activation(yt[:, i, :], banks[i][:, 0:P], COPY, scale=new_of(HALF_BLOCKS * s + i))
+            return take(turn([yt[:, i, :] for i in range(HALF_BLOCKS)]), "ny0%d" % s, "ny0%d" % s)
 
-        def gather(t, s, tag):
-            g = keep.tile([P, HALF_T], F32, name="g%d%d" % (t, s), tag=tag)
+        def gather(t, s):
+            g = keep.tile([P, HALF_T], F32, name="g%d%d" % (t, s), tag="g%d%d" % (s, s * t % 2))
             nc.vector.tensor_tensor(
                 g[:], win[t][:].indirect(offs[:, 32 * s : 32 * (s + 1)]), old_b[:, HALF_T * s : HALF_T * (s + 1)], MULT
             )
@@ -172,91 +156,54 @@ def tile_picked_wema_none_lo_kernel(tc, x_words, x_scales, mem, w1, old, new, sl
         def scatter(t, s, g, ny):
             nc.vector.tensor_tensor(win[t][:].indirect(offs[:, 32 * s : 32 * (s + 1)]), g[:], ny[:], ADD)
 
-        def store_rows(t):
-            nc.sync.dma_start(out=rows_of(out_0, t), in_=win[t][:])
-
-        even = [keep.tile([P, 2, CW], F32, name="even%d" % k, tag="even%d" % k) for k in range(CHUNKS)]
-
-        def move_even(t):
-            for k in range(CHUNKS):
-                for a in range(2):
-                    nc.sync.dma_start(out=even[k][64 * t : 64 * (t + 1), a, :], in_=win[t][a:P:2, CW * k : CW * (k + 1)])
-
         ny = {}
-        g = {}
-        ny[0, 0] = first_y()
-        g[0, 0] = gather(0, 0, "g0")
-        g[0, 1] = gather(0, 1, "g1")
-        scatter(0, 0, g[0, 0], ny[0, 0])
-
-        raw[1, 0] = load_w(1, 0)
-        raw[1, 1] = load_w(1, 1)
-        xw[1] = load_x(1, "early0")
-        win[1] = load_mem(1, "early1")
-        for z in range(PASSES):
-            wg = group_w(1, z, raw[1, z], "late%d" % z, nc.scalar.copy)
-            wq[1, z] = quant_w(1, z, wg)
-        win[2] = load_mem(2, "stage0")
-        win[3] = load_mem(3, "stage1")
-
-        ny[0, 1] = even_y(0, 1)
-        g[1, 0] = gather(1, 0, "g0")
-        scatter(0, 1, g[0, 1], ny[0, 1])
-        move_even(0)
-        store_rows(0)
-
-        ny[1, 0] = even_y(1, 0)
-        ny[1, 1] = even_y(1, 1)
-        yo = keep.tile([P, BLOCKS, 2, P], F32, name="yo")
-        for pair in range(BLOCKS // 2):
-            ps = ps_mx.tile([P, 512], F32, name="mx")
-            for i in range(2):
-                for h in range(2):
-                    product(ps[:, P * (2 * i + h) : P * (2 * i + h + 1)], 2 * pair + i, h, 1)
-            for i in range(2):
-                b = 2 * pair + i
+        ny[0, 0] = first_y(0)
+        ny[0, 1] = first_y(1)
+        yrest = keep.tile([P, BLOCKS, PACK - 1, P], F32, name="yrest", tag="yrest", align_bytes=64)
+        turned = {}
+        for s in range(2):
+            for i in range(HALF_BLOCKS):
+                b = HALF_BLOCKS * s + i
+                ps = ps_mx.tile([P, 512], F32, name="mx")
+                for t in range(1, PACK):
+                    for z in range(PASSES):
+                        mx_pass(ps[:, P * (t - 1) : P * t], b, ORDER[t], z)
                 nc.scalar.activation(
-                    yo[:, b, :, :],
-                    ps[:, 2 * P * i : 2 * P * (i + 1)].rearrange("p (l a) -> p a l", a=2),
-                    COPY,
-                    scale=cols[:, BLOCKS + b : BLOCKS + b + 1],
+                    yrest[:, b, :, :].rearrange("p t m -> p (t m)"), ps[:, 0 : P * (PACK - 1)], COPY, scale=new_of(b)
                 )
+            ny[1, s] = take(turn([yrest[:, HALF_BLOCKS * s + i, 0, :] for i in range(HALF_BLOCKS)]), "ny1%d" % s, "ny1%d" % s)
+        for t in range(2, PACK):
+            for s in range(2):
+                turned[t, s] = turn([yrest[:, HALF_BLOCKS * s + i, t - 1, :] for i in range(HALF_BLOCKS)])
+                if t < PACK - 1:
+                    ny[t, s] = take(turned[t, s], "ny%d%d" % (t, s), "ny%d%d" % (t, s))
 
-        def odd_y(t, s, tag):
-            return turn_back("ny%d%d" % (t, s), [yo[:, 4 * s + i, t - 2, :] for i in range(4)], tag)
+        fin = keep.tile([P, U, PACK], BF16, name="fin", tag="yrest", align_bytes=64)
+        g = {}
+        g[0, 0] = gather(0, 0)
+        g[0, 1] = gather(0, 1)
+        last = PACK - 1
+        for t in range(PACK):
+            if t < last:
+                if t + 1 < last:
+                    g[t + 1, 1] = gather(t + 1, 1)
+                scatter(t, 0, g[t, 0], ny[t, 0])
+                if t + 1 < last:
+                    g[t + 1, 0] = gather(t + 1, 0)
+                scatter(t, 1, g[t, 1], ny[t, 1])
+            else:
+                g_last = keep.tile([P, T], F32, name="g_last", tag="g10")
+                nc.vector.tensor_tensor(g_last[:], win[t][:].indirect(offs[:]), old_b[:], MULT)
+                nc.vector.tensor_tensor(win[t][:].indirect(offs[:]), g_last[:], ny_last[:], ADD)
+            nc.sync.dma_start(out=plane_rows(out_0, ORDER[t]), in_=win[t][:])
+            for k in range(CHUNKS):
+                copy = nc.vector.tensor_copy if t == PACK - 1 and k < 2 else nc.scalar.copy
+                copy(fin[:, CW * k : CW * (k + 1), ORDER[t]], win[t][:, CW * k : CW * (k + 1)])
+            if t == 0:
+                ny_last = keep.tile([P, T], F32, name="ny_last", tag="win0")
+                for s in range(2):
+                    nc.scalar.copy(ny_last[:, HALF_T * s : HALF_T * (s + 1)], turned[last, s][:])
 
-        ny[2, 0] = odd_y(2, 0, "ny20")
-        ny[2, 1] = odd_y(2, 1, "ny21")
-        ny[3, 0] = odd_y(3, 0, "ny30")
-        ny[3, 1] = odd_y(3, 1, "ny31")
-
-        g[1, 1] = gather(1, 1, "g1")
-        scatter(1, 0, g[1, 0], ny[1, 0])
-        g[2, 0] = gather(2, 0, "g0")
-        scatter(1, 1, g[1, 1], ny[1, 1])
-        move_even(1)
-        store_rows(1)
-
-        fin = [keep.tile([P, CW, 4], BF16, name="fin%d" % k, align_bytes=64) for k in range(CHUNKS)]
-        for k in range(CHUNKS):
-            nc.scalar.copy(fin[k][:, :, 0:4:2], even[k][:].rearrange("p a c -> p c a"))
-
-
-        scatter(2, 0, g[2, 0], ny[2, 0])
-        g[3, 0] = gather(3, 0, "g0")
-        g[2, 1] = gather(2, 1, "even0")
-        scatter(2, 1, g[2, 1], ny[2, 1])
-        store_rows(2)
-        for k in range(CHUNKS):
-            nc.scalar.copy(fin[k][:, :, 1], win[2][:, CW * k : CW * (k + 1)])
-        g[3, 1] = gather(3, 1, "even1")
-        scatter(3, 0, g[3, 0], ny[3, 0])
-        scatter(3, 1, g[3, 1], ny[3, 1])
-        store_rows(3)
-
-        for k in range(CHUNKS):
-            copy = nc.vector.tensor_copy if k < 2 else nc.scalar.copy
-            copy(fin[k][:, :, 3], win[3][:, CW * k : CW * (k + 1)])
         osc = keep.tile([P, U], U8, name="osc", align_bytes=64)
         words_dram = out_1[0].rearrange("p c r -> p (c r)").bitcast(I32)
         for k in (0, 2, 1, 3):
@@ -264,7 +211,7 @@ def tile_picked_wema_none_lo_kernel(tc, x_words, x_scales, mem, w1, old, new, sl
             nc.vector.quantize_mx(
                 out=words[:].bitcast(FP8X4),
                 scales=osc[:, CW * k : CW * (k + 1)],
-                in_=fin[k][:].rearrange("p c r -> p (c r)"),
+                in_=fin[:, CW * k : CW * (k + 1), :].rearrange("p c r -> p (c r)"),
             )
             nc.sync.dma_start(out=words_dram[:, CW * k : CW * (k + 1)], in_=words[:].bitcast(I32))
         scales_dram = out_2[0].bitcast(I32)

@@ -53,8 +53,8 @@ def tile_picked_wema_none_lo_kernel(tc, x_words, x_scales, mem, w1, old, new, sl
 
         row_stage = keep.tile([2 * BLOCKS, P], F32, name="row_stage")
         xs_stage = keep.tile([P, PASSES * T // 4], I32, name="xs_stage")
-        nc.scalar.dma_start(out=row_stage[0:BLOCKS, :], in_=old[0:1, :].rearrange("o (b n) -> (o b) n", n=P))
-        nc.scalar.dma_start(out=row_stage[BLOCKS : 2 * BLOCKS, :], in_=new[0:1, :].rearrange("o (b n) -> (o b) n", n=P))
+        nc.sync.dma_start(out=row_stage[0:BLOCKS, :], in_=old[0:1, :].rearrange("o (b n) -> (o b) n", n=P))
+        nc.sync.dma_start(out=row_stage[BLOCKS : 2 * BLOCKS, :], in_=new[0:1, :].rearrange("o (b n) -> (o b) n", n=P))
         raw = [keep.tile([P, PACK, N], F32, name="wraw%d" % z) for z in range(PASSES)]
 
         def load_w(z):
@@ -78,9 +78,9 @@ def tile_picked_wema_none_lo_kernel(tc, x_words, x_scales, mem, w1, old, new, sl
         nc.sync.dma_start(offs[:], slot)
         nc.sync.dma_start(out=win[0][:], in_=plane_rows(mem, ORDER[0]))
         nc.sync.dma_start(out=win[1][:], in_=plane_rows(mem, ORDER[1]))
+        nc.sync.dma_start(out=win[2][:], in_=plane_rows(mem, ORDER[2]))
         load_x(1)
-        for t in range(2, PACK):
-            nc.sync.dma_start(out=win[t][:], in_=plane_rows(mem, ORDER[t]))
+        nc.sync.dma_start(out=win[3][:], in_=plane_rows(mem, ORDER[3]))
 
         for q in range(4):
             nc.vector.tensor_copy(xs[32 * q : 32 * q + 4, :].bitcast(I32), xs_stage[32 * q : 32 * q + 4, :])
@@ -100,24 +100,21 @@ def tile_picked_wema_none_lo_kernel(tc, x_words, x_scales, mem, w1, old, new, sl
         wq = []
         for z in range(PASSES):
             wg = keep.tile([P, PACK * N], BF16, name="wg%d" % z, align_bytes=64)
-            nc.vector.tensor_copy(
-                wg[:].rearrange("p (r l j) -> p l j r", r=PACK, j=PACK),
-                raw[z][:].rearrange("p j (l r) -> p l j r", r=PACK),
-            )
+            nc.vector.tensor_copy(wg[:].rearrange("p (n j) -> p n j", j=PACK), raw[z][:].rearrange("p j n -> p n j"))
             codes = keep.tile([P, N], U32, name="wc%d" % z, align_bytes=64)
             scales = keep.tile([P, N], U8, name="ws%d" % z, align_bytes=64)
             nc.vector.quantize_mx(out=codes[:].bitcast(FP8X4), scales=scales[:], in_=wg[:])
             wq.append((codes, scales))
 
-        def mx_pass(out, b, r, z):
+        def mx_pass(out, b, z):
             codes, scales = wq[z]
             s, i = divmod(b, HALF_BLOCKS)
             nc.tensor.matmul_mx(
                 out=out,
                 lhsT=xw[s][:, z, 2 * P * i : 2 * P * (i + 1)].bitcast(FP4X4),
                 lhsT_scale=xs[:, T * z + P * b : T * z + P * (b + 1)],
-                rhs=codes[:, P * r : P * (r + 1)].bitcast(FP8X4),
-                rhs_scale=scales[:, P * r : P * (r + 1)],
+                rhs=codes[:].bitcast(FP8X4),
+                rhs_scale=scales[:],
                 start=(z == 0),
                 stop=(z == PASSES - 1),
             )
@@ -125,84 +122,64 @@ def tile_picked_wema_none_lo_kernel(tc, x_words, x_scales, mem, w1, old, new, sl
         def new_of(b):
             return cols[:, BLOCKS + b : BLOCKS + b + 1]
 
-        def turn(srcs):
-            ps = ps_tr.tile([P, 512], F32, name="tr")
-            for i in range(HALF_BLOCKS):
-                nc.tensor.transpose(ps[:, P * i : P * (i + 1)], srcs[i], ident[:])
-            return ps
+        yt = keep.tile([P, BLOCKS, PACK, P], F32, name="yt", tag="yt", align_bytes=64)
 
-        def take(ps, name, tag):
-            ny = keep.tile([P, HALF_T], F32, name=name, tag=tag)
-            nc.scalar.copy(ny[:], ps[:])
-            return ny
-
-        def first_y(s):
-            banks = [ps_mx.tile([P, 512], F32, name="mx") for i in range(HALF_BLOCKS)]
+        def project(s):
+            banks = [ps_mx.tile([P, N], F32, name="mx") for i in range(HALF_BLOCKS)]
             for z in range(PASSES):
                 for i in range(HALF_BLOCKS):
-                    mx_pass(banks[i][:, 0:P], HALF_BLOCKS * s + i, ORDER[0], z)
-            yt = keep.tile([P, HALF_BLOCKS, P], F32, name="yt%d" % s)
-            for i in range(HALF_BLOCKS):
-                nc.scalar.activation(yt[:, i, :], banks[i][:, 0:P], COPY, scale=new_of(HALF_BLOCKS * s + i))
-            return take(turn([yt[:, i, :] for i in range(HALF_BLOCKS)]), "ny0%d" % s, "ny0%d" % s)
-
-        def gather(t, s):
-            g = keep.tile([P, HALF_T], F32, name="g%d%d" % (t, s), tag="g%d%d" % (s, s * t % 2))
-            nc.vector.tensor_tensor(
-                g[:], win[t][:].indirect(offs[:, 32 * s : 32 * (s + 1)]), old_b[:, HALF_T * s : HALF_T * (s + 1)], MULT
-            )
-            return g
-
-        def scatter(t, s, g, ny):
-            nc.vector.tensor_tensor(win[t][:].indirect(offs[:, 32 * s : 32 * (s + 1)]), g[:], ny[:], ADD)
-
-        ny = {}
-        ny[0, 0] = first_y(0)
-        ny[0, 1] = first_y(1)
-        yrest = keep.tile([P, BLOCKS, PACK - 1, P], F32, name="yrest", tag="yrest", align_bytes=64)
-        turned = {}
-        for s in range(2):
+                    mx_pass(banks[i][:], HALF_BLOCKS * s + i, z)
             for i in range(HALF_BLOCKS):
                 b = HALF_BLOCKS * s + i
-                ps = ps_mx.tile([P, 512], F32, name="mx")
-                for t in range(1, PACK):
-                    for z in range(PASSES):
-                        mx_pass(ps[:, P * (t - 1) : P * t], b, ORDER[t], z)
-                nc.scalar.activation(
-                    yrest[:, b, :, :].rearrange("p t m -> p (t m)"), ps[:, 0 : P * (PACK - 1)], COPY, scale=new_of(b)
-                )
-            ny[1, s] = take(turn([yrest[:, HALF_BLOCKS * s + i, 0, :] for i in range(HALF_BLOCKS)]), "ny1%d" % s, "ny1%d" % s)
-        for t in range(2, PACK):
-            for s in range(2):
-                turned[t, s] = turn([yrest[:, HALF_BLOCKS * s + i, t - 1, :] for i in range(HALF_BLOCKS)])
-                if t < PACK - 1:
-                    ny[t, s] = take(turned[t, s], "ny%d%d" % (t, s), "ny%d%d" % (t, s))
+                nc.scalar.activation(yt[:, b, :, :], banks[i][:].rearrange("p (l r) -> p r l", r=PACK), COPY, scale=new_of(b))
 
-        fin = keep.tile([P, U, PACK], BF16, name="fin", tag="yrest", align_bytes=64)
-        g = {}
-        g[0, 0] = gather(0, 0)
-        g[0, 1] = gather(0, 1)
+        def turn(t, s):
+            ps = ps_tr.tile([P, 512], F32, name="tr")
+            for i in range(HALF_BLOCKS):
+                nc.tensor.transpose(ps[:, P * i : P * (i + 1)], yt[:, HALF_BLOCKS * s + i, ORDER[t], :], ident[:])
+            return ps
+
+        def half(s):
+            return slice(HALF_T * s, HALF_T * (s + 1))
+
         last = PACK - 1
-        for t in range(PACK):
-            if t < last:
-                if t + 1 < last:
-                    g[t + 1, 1] = gather(t + 1, 1)
-                scatter(t, 0, g[t, 0], ny[t, 0])
-                if t + 1 < last:
-                    g[t + 1, 0] = gather(t + 1, 0)
-                scatter(t, 1, g[t, 1], ny[t, 1])
-            else:
-                g_last = keep.tile([P, T], F32, name="g_last", tag="g10")
-                nc.vector.tensor_tensor(g_last[:], win[t][:].indirect(offs[:]), old_b[:], MULT)
-                nc.vector.tensor_tensor(win[t][:].indirect(offs[:]), g_last[:], ny_last[:], ADD)
+        ny = [keep.tile([P, T], F32, name="ny%d" % t) for t in range(last)]
+        for s in range(2):
+            project(s)
+            nc.scalar.copy(ny[0][:, half(s)], turn(0, s)[:])
+        for t in range(1, last):
+            for s in range(2):
+                nc.scalar.copy(ny[t][:, half(s)], turn(t, s)[:])
+        turned_last = [turn(last, s) for s in range(2)]
+
+        def gather(t, tag):
+            g = keep.tile([P, T], F32, name="g%d" % t, tag=tag)
+            nc.vector.tensor_tensor(g[:], win[t][:].indirect(offs[:]), old_b[:], MULT)
+            return g
+
+        fin = keep.tile([P, U, PACK], BF16, name="fin", tag="yt", align_bytes=64)
+
+        def finish(t):
             nc.sync.dma_start(out=plane_rows(out_0, ORDER[t]), in_=win[t][:])
             for k in range(CHUNKS):
-                copy = nc.vector.tensor_copy if t == PACK - 1 and k < 2 else nc.scalar.copy
+                copy = nc.vector.tensor_copy if t == last and k < 2 else nc.scalar.copy
                 copy(fin[:, CW * k : CW * (k + 1), ORDER[t]], win[t][:, CW * k : CW * (k + 1)])
-            if t == 0:
-                ny_last = keep.tile([P, T], F32, name="ny_last", tag="win0")
-                for s in range(2):
-                    nc.scalar.copy(ny_last[:, HALF_T * s : HALF_T * (s + 1)], turned[last, s][:])
+
+        g = [gather(0, "g0"), gather(1, "g1")]
+        nc.vector.tensor_tensor(win[0][:].indirect(offs[:, 0:32]), g[0][:, half(0)], ny[0][:, half(0)], ADD)
+        g.append(gather(2, "g2"))
+        nc.vector.tensor_tensor(win[0][:].indirect(offs[:, 32:64]), g[0][:, half(1)], ny[0][:, half(1)], ADD)
+        finish(0)
+        ny_last = keep.tile([P, T], F32, name="ny_last", tag="win0")
+        for s in range(2):
+            nc.scalar.copy(ny_last[:, half(s)], turned_last[s][:])
+        ny.append(ny_last)
+        nc.vector.tensor_tensor(win[1][:].indirect(offs[:]), g[1][:], ny[1][:], ADD)
+        finish(1)
+        g.append(gather(3, "g1"))
+        for t in (2, 3):
+            nc.vector.tensor_tensor(win[t][:].indirect(offs[:]), g[t][:], ny[t][:], ADD)
+            finish(t)
 
         osc = keep.tile([P, U], U8, name="osc", align_bytes=64)
         words_dram = out_1[0].rearrange("p c r -> p (c r)").bitcast(I32)

@@ -20,20 +20,35 @@ ADD = mybir.AluOpType.add
 
 P = 128
 PACK = 4
-PASSES = K // (P * PACK)
+K_PASS = P * PACK
+PASSES = K // K_PASS
+QUADRANTS = 4
+BANK = 512
 BLOCKS = T // P
 HALF_BLOCKS = BLOCKS // 2
 HALF_T = T // 2
+LIST_HALF = HALF_T // 16
 CHUNKS = 4
-CW = U // CHUNKS
+CHUNK = U // CHUNKS
+VECTOR_CHUNKS = 2
 ORDER = (2, 0, 1, 3)
+LAST = PACK - 1
 
 
 def tile_picked_wema_none_lo_kernel(tc, x_words, x_scales, mem, w1, old, new, slot, out_0, out_1, out_2):
     nc = tc.nc
 
     def plane_rows(ap, r):
-        return ap.rearrange("(l r) c -> r l c", r=PACK)[r]
+        return ap.rearrange("(p r) c -> r p c", r=PACK)[r]
+
+    def half(s):
+        return slice(HALF_T * s, HALF_T * (s + 1))
+
+    def blocks(s):
+        return range(HALF_BLOCKS * s, HALF_BLOCKS * (s + 1))
+
+    def chunk(c):
+        return slice(CHUNK * c, CHUNK * (c + 1))
 
     with ExitStack() as ctx:
         keep = ctx.enter_context(tc.tile_pool(name="keep", bufs=1))
@@ -42,156 +57,161 @@ def tile_picked_wema_none_lo_kernel(tc, x_words, x_scales, mem, w1, old, new, sl
 
         offs = keep.tile([P, T // 16], U16, name="offs")
         ident = keep.tile([P, P], F32, name="ident")
-        rows = keep.tile([P, P], F32, name="rows")
-        xs = keep.tile([P, PASSES * T], U8, name="xs", align_bytes=64)
-        nc.gpsimd.memset(rows[:], 0.0)
-        nc.vector.memset(xs[:].bitcast(U32), 0)
+        weight_rows = keep.tile([P, P], F32, name="weight_rows")
+        x_scale = keep.tile([P, PASSES * T], U8, name="x_scale", align_bytes=64)
+        nc.gpsimd.memset(weight_rows[:], 0.0)
+        nc.vector.memset(x_scale[:].bitcast(U32), 0)
         make_identity(nc, ident[:])
 
         xw_dram = x_words.bitcast(I32)
         xs_dram = x_scales.bitcast(I32)
 
         row_stage = keep.tile([2 * BLOCKS, P], F32, name="row_stage")
-        xs_stage = keep.tile([P, PASSES * T // 4], I32, name="xs_stage")
+        scale_stage = keep.tile([P, PASSES * T // 4], I32, name="scale_stage")
         nc.sync.dma_start(out=row_stage[0:BLOCKS, :], in_=old[0:1, :].rearrange("o (b n) -> (o b) n", n=P))
         nc.sync.dma_start(out=row_stage[BLOCKS : 2 * BLOCKS, :], in_=new[0:1, :].rearrange("o (b n) -> (o b) n", n=P))
-        raw = [keep.tile([P, PACK, N], F32, name="wraw%d" % z) for z in range(PASSES)]
+        w_raw = [keep.tile([P, PACK, N], F32, name="w_raw%d" % z) for z in range(PASSES)]
 
         def load_w(z):
-            nc.sync.dma_start(out=raw[z][:], in_=w1[512 * z : 512 * (z + 1), :].rearrange("(p j) n -> p j n", j=PACK))
+            rows = w1[K_PASS * z : K_PASS * (z + 1), :]
+            nc.sync.dma_start(out=w_raw[z][:], in_=rows.rearrange("(p i) n -> p i n", i=PACK))
 
         load_w(0)
-        for q in range(4):
+        for q in range(QUADRANTS):
             nc.sync.dma_start(
-                out=xs_stage[32 * q : 32 * q + 4, :].rearrange("q (z c) -> q z c", z=PASSES),
+                out=scale_stage[32 * q : 32 * q + 4, :].rearrange("q (z c) -> q z c", z=PASSES),
                 in_=xs_dram[:, 4 * q : 4 * q + 4, :].rearrange("z q c -> q z c"),
             )
         load_w(1)
-        xw = [keep.tile([P, PASSES, 2 * HALF_T], U8, name="xw%d" % s, align_bytes=64) for s in range(2)]
-        win = [keep.tile([P, U], F32, name="win%d" % t, tag="win%d" % t) for t in range(PACK)]
+        x_word = [keep.tile([P, PASSES, 2 * HALF_T], U8, name="x_word%d" % s, align_bytes=64) for s in range(2)]
+        window = [keep.tile([P, U], F32, name="window%d" % t, tag="window%d" % t) for t in range(PACK)]
 
         def load_x(s):
-            src = xw_dram[:, :, 256 * s : 256 * (s + 1)].rearrange("z p c -> p z c")
-            nc.sync.dma_start(out=xw[s][:].bitcast(I32), in_=src)
+            ints = HALF_T // 2
+            src = xw_dram[:, :, ints * s : ints * (s + 1)].rearrange("z p c -> p z c")
+            nc.sync.dma_start(out=x_word[s][:].bitcast(I32), in_=src)
 
-        load_x(0)
         nc.sync.dma_start(offs[:], slot)
-        nc.sync.dma_start(out=win[0][:], in_=plane_rows(mem, ORDER[0]))
-        nc.sync.dma_start(out=win[1][:], in_=plane_rows(mem, ORDER[1]))
-        nc.sync.dma_start(out=win[2][:], in_=plane_rows(mem, ORDER[2]))
-        load_x(1)
-        nc.sync.dma_start(out=win[3][:], in_=plane_rows(mem, ORDER[3]))
+        for t in range(PACK):
+            nc.sync.dma_start(out=window[t][:], in_=plane_rows(mem, ORDER[t]))
+            if t < 2:
+                load_x(t)
 
-        for q in range(4):
-            nc.vector.tensor_copy(xs[32 * q : 32 * q + 4, :].bitcast(I32), xs_stage[32 * q : 32 * q + 4, :])
-        nc.scalar.copy(rows[0 : 2 * BLOCKS, :], row_stage[:])
-        cols_ps = ps_tr.tile([P, 512], F32, name="tr")
-        nc.tensor.transpose(cols_ps[:, 0:P], rows[:], ident[:])
-        cols = keep.tile([P, 2 * BLOCKS], F32, name="cols")
-        nc.scalar.copy(cols[:], cols_ps[:, 0 : 2 * BLOCKS])
-        old_b = keep.tile([P, T], F32, name="old_b")
+        for q in range(QUADRANTS):
+            nc.vector.tensor_copy(x_scale[32 * q : 32 * q + 4, :].bitcast(I32), scale_stage[32 * q : 32 * q + 4, :])
+
+        nc.scalar.copy(weight_rows[0 : 2 * BLOCKS, :], row_stage[:])
+        cols_bank = ps_tr.tile([P, BANK], F32, name="tr")
+        nc.tensor.transpose(cols_bank[:, 0:P], weight_rows[:], ident[:])
+        weight_cols = keep.tile([P, 2 * BLOCKS], F32, name="weight_cols")
+        nc.scalar.copy(weight_cols[:], cols_bank[:, 0 : 2 * BLOCKS])
+        old_all = keep.tile([P, T], F32, name="old_all")
         for s in range(2):
-            ps = ps_tr.tile([P, 512], F32, name="tr")
-            for i in range(HALF_BLOCKS):
-                b = HALF_BLOCKS * s + i
-                nc.tensor.transpose(ps[:, P * i : P * (i + 1)], cols[:, b : b + 1].to_broadcast([P, P]), ident[:])
-            nc.scalar.copy(old_b[:, HALF_T * s : HALF_T * (s + 1)], ps[:])
+            bank = ps_tr.tile([P, BANK], F32, name="tr")
+            for i, b in enumerate(blocks(s)):
+                nc.tensor.transpose(bank[:, P * i : P * (i + 1)], weight_cols[:, b : b + 1].to_broadcast([P, P]), ident[:])
+            nc.scalar.copy(old_all[:, half(s)], bank[:])
 
-        wq = []
+        w_mx = []
         for z in range(PASSES):
-            wg = keep.tile([P, PACK * N], BF16, name="wg%d" % z, align_bytes=64)
-            nc.vector.tensor_copy(wg[:].rearrange("p (n j) -> p n j", j=PACK), raw[z][:].rearrange("p j n -> p n j"))
-            codes = keep.tile([P, N], U32, name="wc%d" % z, align_bytes=64)
-            scales = keep.tile([P, N], U8, name="ws%d" % z, align_bytes=64)
-            nc.vector.quantize_mx(out=codes[:].bitcast(FP8X4), scales=scales[:], in_=wg[:])
-            wq.append((codes, scales))
+            w_grouped = keep.tile([P, PACK * N], BF16, name="w_grouped%d" % z, align_bytes=64)
+            nc.vector.tensor_copy(
+                w_grouped[:].rearrange("p (r l i) -> p l i r", r=PACK, i=PACK),
+                w_raw[z][:].rearrange("p i (l r) -> p l i r", r=PACK),
+            )
+            codes = keep.tile([P, N], U32, name="w_codes%d" % z, align_bytes=64)
+            scales = keep.tile([P, N], U8, name="w_scales%d" % z, align_bytes=64)
+            nc.vector.quantize_mx(out=codes[:].bitcast(FP8X4), scales=scales[:], in_=w_grouped[:])
+            w_mx.append((codes, scales))
 
-        def mx_pass(out, b, z):
-            codes, scales = wq[z]
+        def mx_pass(out, b, r, z):
+            codes, scales = w_mx[z]
             s, i = divmod(b, HALF_BLOCKS)
             nc.tensor.matmul_mx(
                 out=out,
-                lhsT=xw[s][:, z, 2 * P * i : 2 * P * (i + 1)].bitcast(FP4X4),
-                lhsT_scale=xs[:, T * z + P * b : T * z + P * (b + 1)],
-                rhs=codes[:].bitcast(FP8X4),
-                rhs_scale=scales[:],
+                lhsT=x_word[s][:, z, 2 * P * i : 2 * P * (i + 1)].bitcast(FP4X4),
+                lhsT_scale=x_scale[:, T * z + P * b : T * z + P * (b + 1)],
+                rhs=codes[:, P * r : P * (r + 1)].bitcast(FP8X4),
+                rhs_scale=scales[:, P * r : P * (r + 1)],
                 start=(z == 0),
                 stop=(z == PASSES - 1),
             )
 
         def new_of(b):
-            return cols[:, BLOCKS + b : BLOCKS + b + 1]
+            return weight_cols[:, BLOCKS + b : BLOCKS + b + 1]
 
-        yt = keep.tile([P, BLOCKS, PACK, P], F32, name="yt", tag="yt", align_bytes=64)
-
-        def project(s):
-            banks = [ps_mx.tile([P, N], F32, name="mx") for i in range(HALF_BLOCKS)]
-            for z in range(PASSES):
-                for i in range(HALF_BLOCKS):
-                    mx_pass(banks[i][:], HALF_BLOCKS * s + i, z)
+        def turn(sources):
+            bank = ps_tr.tile([P, BANK], F32, name="tr")
             for i in range(HALF_BLOCKS):
-                b = HALF_BLOCKS * s + i
-                nc.scalar.activation(yt[:, b, :, :], banks[i][:].rearrange("p (l r) -> p r l", r=PACK), COPY, scale=new_of(b))
+                nc.tensor.transpose(bank[:, P * i : P * (i + 1)], sources[i], ident[:])
+            return bank
 
-        def turn(t, s):
-            ps = ps_tr.tile([P, 512], F32, name="tr")
-            for i in range(HALF_BLOCKS):
-                nc.tensor.transpose(ps[:, P * i : P * (i + 1)], yt[:, HALF_BLOCKS * s + i, ORDER[t], :], ident[:])
-            return ps
-
-        def half(s):
-            return slice(HALF_T * s, HALF_T * (s + 1))
-
-        last = PACK - 1
-        ny = [keep.tile([P, T], F32, name="ny%d" % t) for t in range(last)]
+        new_y = [keep.tile([P, T], F32, name="new_y%d" % t) for t in range(LAST)]
         for s in range(2):
-            project(s)
-            nc.scalar.copy(ny[0][:, half(s)], turn(0, s)[:])
-        for t in range(1, last):
+            banks = [ps_mx.tile([P, BANK], F32, name="mx") for b in blocks(s)]
+            for z in range(PASSES):
+                for i, b in enumerate(blocks(s)):
+                    mx_pass(banks[i][:, 0:P], b, ORDER[0], z)
+            y_first = keep.tile([P, HALF_BLOCKS, P], F32, name="y_first%d" % s)
+            for i, b in enumerate(blocks(s)):
+                nc.scalar.activation(y_first[:, i, :], banks[i][:, 0:P], COPY, scale=new_of(b))
+            nc.scalar.copy(new_y[0][:, half(s)], turn([y_first[:, i, :] for i in range(HALF_BLOCKS)])[:])
+
+        y_rest = keep.tile([P, BLOCKS, LAST, P], F32, name="y_rest", tag="y_rest", align_bytes=64)
+        for b in range(BLOCKS):
+            bank = ps_mx.tile([P, BANK], F32, name="mx")
+            for t in range(1, PACK):
+                for z in range(PASSES):
+                    mx_pass(bank[:, P * (t - 1) : P * t], b, ORDER[t], z)
+            nc.scalar.activation(y_rest[:, b, :, :].rearrange("p t l -> p (t l)"), bank[:, 0 : P * LAST], COPY, scale=new_of(b))
+        for t in range(1, LAST):
             for s in range(2):
-                nc.scalar.copy(ny[t][:, half(s)], turn(t, s)[:])
-        turned_last = [turn(last, s) for s in range(2)]
+                nc.scalar.copy(new_y[t][:, half(s)], turn([y_rest[:, b, t - 1, :] for b in blocks(s)])[:])
+        last_banks = [turn([y_rest[:, b, LAST - 1, :] for b in blocks(s)]) for s in range(2)]
 
         def gather(t, tag):
-            g = keep.tile([P, T], F32, name="g%d" % t, tag=tag)
-            nc.vector.tensor_tensor(g[:], win[t][:].indirect(offs[:]), old_b[:], MULT)
-            return g
+            old_mem = keep.tile([P, T], F32, name="old_mem%d" % t, tag=tag)
+            nc.vector.tensor_tensor(old_mem[:], window[t][:].indirect(offs[:]), old_all[:], MULT)
+            return old_mem
 
-        fin = keep.tile([P, U, PACK], BF16, name="fin", tag="yt", align_bytes=64)
+        grouped = keep.tile([P, U, PACK], BF16, name="grouped", tag="y_rest", align_bytes=64)
 
         def finish(t):
-            nc.sync.dma_start(out=plane_rows(out_0, ORDER[t]), in_=win[t][:])
-            for k in range(CHUNKS):
-                copy = nc.vector.tensor_copy if t == last and k < 2 else nc.scalar.copy
-                copy(fin[:, CW * k : CW * (k + 1), ORDER[t]], win[t][:, CW * k : CW * (k + 1)])
+            nc.sync.dma_start(out=plane_rows(out_0, ORDER[t]), in_=window[t][:])
+            for c in range(CHUNKS):
+                copy = nc.vector.tensor_copy if t == LAST and c < VECTOR_CHUNKS else nc.scalar.copy
+                copy(grouped[:, chunk(c), ORDER[t]], window[t][:, chunk(c)])
 
-        g = [gather(0, "g0"), gather(1, "g1")]
-        nc.vector.tensor_tensor(win[0][:].indirect(offs[:, 0:32]), g[0][:, half(0)], ny[0][:, half(0)], ADD)
-        g.append(gather(2, "g2"))
-        nc.vector.tensor_tensor(win[0][:].indirect(offs[:, 32:64]), g[0][:, half(1)], ny[0][:, half(1)], ADD)
+        old_mem = [gather(0, "old_mem0"), gather(1, "old_mem1")]
+        nc.vector.tensor_tensor(window[0][:].indirect(offs[:, 0:LIST_HALF]), old_mem[0][:, half(0)], new_y[0][:, half(0)], ADD)
+        old_mem.append(gather(2, "old_mem2"))
+        nc.vector.tensor_tensor(
+            window[0][:].indirect(offs[:, LIST_HALF : 2 * LIST_HALF]), old_mem[0][:, half(1)], new_y[0][:, half(1)], ADD
+        )
         finish(0)
-        ny_last = keep.tile([P, T], F32, name="ny_last", tag="win0")
+        new_y_last = keep.tile([P, T], F32, name="new_y_last", tag="window0")
         for s in range(2):
-            nc.scalar.copy(ny_last[:, half(s)], turned_last[s][:])
-        ny.append(ny_last)
-        nc.vector.tensor_tensor(win[1][:].indirect(offs[:]), g[1][:], ny[1][:], ADD)
+            nc.scalar.copy(new_y_last[:, half(s)], last_banks[s][:])
+        new_y.append(new_y_last)
+        nc.vector.tensor_tensor(window[1][:].indirect(offs[:]), old_mem[1][:], new_y[1][:], ADD)
         finish(1)
-        g.append(gather(3, "g1"))
-        for t in (2, 3):
-            nc.vector.tensor_tensor(win[t][:].indirect(offs[:]), g[t][:], ny[t][:], ADD)
+        old_mem.append(gather(LAST, "old_mem1"))
+        for t in range(2, PACK):
+            nc.vector.tensor_tensor(window[t][:].indirect(offs[:]), old_mem[t][:], new_y[t][:], ADD)
             finish(t)
 
-        osc = keep.tile([P, U], U8, name="osc", align_bytes=64)
+        out_scale = keep.tile([P, U], U8, name="out_scale", align_bytes=64)
         words_dram = out_1[0].rearrange("p c r -> p (c r)").bitcast(I32)
-        for k in (0, 2, 1, 3):
-            words = keep.tile([P, CW], U32, name="words%d" % k, align_bytes=64)
-            nc.vector.quantize_mx(
-                out=words[:].bitcast(FP8X4),
-                scales=osc[:, CW * k : CW * (k + 1)],
-                in_=fin[:, CW * k : CW * (k + 1), :].rearrange("p c r -> p (c r)"),
-            )
-            nc.sync.dma_start(out=words_dram[:, CW * k : CW * (k + 1)], in_=words[:].bitcast(I32))
+        for first in range(VECTOR_CHUNKS):
+            for c in (first, VECTOR_CHUNKS + first):
+                words = keep.tile([P, CHUNK], U32, name="words%d" % c, align_bytes=64)
+                nc.vector.quantize_mx(
+                    out=words[:].bitcast(FP8X4),
+                    scales=out_scale[:, chunk(c)],
+                    in_=grouped[:, chunk(c), :].rearrange("p c r -> p (c r)"),
+                )
+                nc.sync.dma_start(out=words_dram[:, chunk(c)], in_=words[:].bitcast(I32))
         scales_dram = out_2[0].bitcast(I32)
-        for q in range(4):
+        for q in range(QUADRANTS):
             queue = nc.scalar if q % 2 == 0 else nc.sync
-            queue.dma_start(out=scales_dram[4 * q : 4 * q + 4, :], in_=osc[32 * q : 32 * q + 4, :].bitcast(I32))
+            queue.dma_start(out=scales_dram[4 * q : 4 * q + 4, :], in_=out_scale[32 * q : 32 * q + 4, :].bitcast(I32))

@@ -32,6 +32,7 @@ CHUNKS = 4
 CHUNK = U // CHUNKS
 VECTOR_CHUNKS = 2
 ORDER = (2, 0, 1, 3)
+LOADS = (1, 0, 2, 3)
 LAST = PACK - 1
 
 
@@ -92,10 +93,10 @@ def tile_picked_wema_none_lo_kernel(tc, x_words, x_scales, mem, w1, old, new, sl
             nc.sync.dma_start(out=x_word[s][:].bitcast(I32), in_=src)
 
         nc.sync.dma_start(offs[:], slot)
-        for t in range(PACK):
+        for t in LOADS:
             nc.sync.dma_start(out=window[t][:], in_=plane_rows(mem, ORDER[t]))
-            if t < 2:
-                load_x(t)
+            if t > 0 and t < LAST:
+                load_x(t - 1)
 
         for q in range(QUADRANTS):
             nc.vector.tensor_copy(x_scale[32 * q : 32 * q + 4, :].bitcast(I32), scale_stage[32 * q : 32 * q + 4, :])
@@ -146,11 +147,11 @@ def tile_picked_wema_none_lo_kernel(tc, x_words, x_scales, mem, w1, old, new, sl
                 nc.tensor.transpose(bank[:, P * i : P * (i + 1)], sources[i], ident[:])
             return bank
 
-        new_y = [keep.tile([P, T], F32, name="new_y%d" % t) for t in range(LAST)]
+        new_y = [keep.tile([P, T], F32, name="new_y%d" % t) for t in range(PACK)]
         for s in range(2):
             banks = [ps_mx.tile([P, BANK], F32, name="mx") for b in blocks(s)]
-            for z in range(PASSES):
-                for i, b in enumerate(blocks(s)):
+            for i, b in enumerate(blocks(s)):
+                for z in range(PASSES):
                     mx_pass(banks[i][:, 0:P], b, ORDER[0], z)
             y_first = keep.tile([P, HALF_BLOCKS, P], F32, name="y_first%d" % s)
             for i, b in enumerate(blocks(s)):
@@ -164,10 +165,9 @@ def tile_picked_wema_none_lo_kernel(tc, x_words, x_scales, mem, w1, old, new, sl
                 for z in range(PASSES):
                     mx_pass(bank[:, P * (t - 1) : P * t], b, ORDER[t], z)
             nc.scalar.activation(y_rest[:, b, :, :].rearrange("p t l -> p (t l)"), bank[:, 0 : P * LAST], COPY, scale=new_of(b))
-        for t in range(1, LAST):
+        for t in range(1, PACK):
             for s in range(2):
                 nc.scalar.copy(new_y[t][:, half(s)], turn([y_rest[:, b, t - 1, :] for b in blocks(s)])[:])
-        last_banks = [turn([y_rest[:, b, LAST - 1, :] for b in blocks(s)]) for s in range(2)]
 
         def gather(t, tag):
             old_mem = keep.tile([P, T], F32, name="old_mem%d" % t, tag=tag)
@@ -182,23 +182,20 @@ def tile_picked_wema_none_lo_kernel(tc, x_words, x_scales, mem, w1, old, new, sl
                 copy = nc.vector.tensor_copy if t == LAST and c < VECTOR_CHUNKS else nc.scalar.copy
                 copy(grouped[:, chunk(c), ORDER[t]], window[t][:, chunk(c)])
 
-        old_mem = [gather(0, "old_mem0"), gather(1, "old_mem1")]
+        second = gather(1, "old_mem1")
+        old_mem = [gather(0, "old_mem0"), second]
         nc.vector.tensor_tensor(window[0][:].indirect(offs[:, 0:LIST_HALF]), old_mem[0][:, half(0)], new_y[0][:, half(0)], ADD)
         old_mem.append(gather(2, "old_mem2"))
         nc.vector.tensor_tensor(
             window[0][:].indirect(offs[:, LIST_HALF : 2 * LIST_HALF]), old_mem[0][:, half(1)], new_y[0][:, half(1)], ADD
         )
         finish(0)
-        new_y_last = keep.tile([P, T], F32, name="new_y_last", tag="window0")
-        for s in range(2):
-            nc.scalar.copy(new_y_last[:, half(s)], last_banks[s][:])
-        new_y.append(new_y_last)
-        nc.vector.tensor_tensor(window[1][:].indirect(offs[:]), old_mem[1][:], new_y[1][:], ADD)
-        finish(1)
-        old_mem.append(gather(LAST, "old_mem1"))
-        for t in range(2, PACK):
+        for t in range(1, LAST):
             nc.vector.tensor_tensor(window[t][:].indirect(offs[:]), old_mem[t][:], new_y[t][:], ADD)
             finish(t)
+        old_mem.append(gather(LAST, "window0"))
+        nc.vector.tensor_tensor(window[LAST][:].indirect(offs[:]), old_mem[LAST][:], new_y[LAST][:], ADD)
+        finish(LAST)
 
         out_scale = keep.tile([P, U], U8, name="out_scale", align_bytes=64)
         words_dram = out_1[0].rearrange("p c r -> p (c r)").bitcast(I32)

@@ -27,13 +27,14 @@ BANK = 512
 BLOCKS = T // P
 HALF_BLOCKS = BLOCKS // 2
 HALF_T = T // 2
-LIST_HALF = HALF_T // 16
+EARLY = 2
+PIECES = (range(0, EARLY), range(EARLY, BLOCKS))
 CHUNKS = 4
 CHUNK = U // CHUNKS
 VECTOR_CHUNKS = 2
 ORDER = (2, 0, 1, 3)
-LOADS = (1, 0, 2, 3)
 LAST = PACK - 1
+W_VECTOR = 96
 
 
 def tile_picked_wema_none_lo_kernel(tc, x_words, x_scales, mem, w1, old, new, slot, out_0, out_1, out_2):
@@ -59,67 +60,70 @@ def tile_picked_wema_none_lo_kernel(tc, x_words, x_scales, mem, w1, old, new, sl
         offs = keep.tile([P, T // 16], U16, name="offs")
         ident = keep.tile([P, P], F32, name="ident")
         weight_rows = keep.tile([P, P], F32, name="weight_rows")
-        x_scale = keep.tile([P, PASSES * T], U8, name="x_scale", align_bytes=64)
         nc.gpsimd.memset(weight_rows[:], 0.0)
-        nc.vector.memset(x_scale[:].bitcast(U32), 0)
         make_identity(nc, ident[:])
 
         xw_dram = x_words.bitcast(I32)
         xs_dram = x_scales.bitcast(I32)
 
-        row_stage = keep.tile([2 * BLOCKS, P], F32, name="row_stage")
-        scale_stage = keep.tile([P, PASSES * T // 4], I32, name="scale_stage")
-        nc.sync.dma_start(out=row_stage[0:BLOCKS, :], in_=old[0:1, :].rearrange("o (b n) -> (o b) n", n=P))
-        nc.sync.dma_start(out=row_stage[BLOCKS : 2 * BLOCKS, :], in_=new[0:1, :].rearrange("o (b n) -> (o b) n", n=P))
+        row_stage = keep.tile([BLOCKS, P], F32, name="row_stage")
+        old_cols = keep.tile([P, BLOCKS], F32, name="old_cols")
         w_raw = [keep.tile([P, PACK, N], F32, name="w_raw%d" % z) for z in range(PASSES)]
 
         def load_w(z):
             rows = w1[K_PASS * z : K_PASS * (z + 1), :]
             nc.sync.dma_start(out=w_raw[z][:], in_=rows.rearrange("(p i) n -> p i n", i=PACK))
 
-        load_w(0)
-        for q in range(QUADRANTS):
-            nc.sync.dma_start(
-                out=scale_stage[32 * q : 32 * q + 4, :].rearrange("q (z c) -> q z c", z=PASSES),
-                in_=xs_dram[:, 4 * q : 4 * q + 4, :].rearrange("z q c -> q z c"),
-            )
-        load_w(1)
-        x_word = [keep.tile([P, PASSES, 2 * HALF_T], U8, name="x_word%d" % s, align_bytes=64) for s in range(2)]
+        x_word = [keep.tile([P, PASSES, 2 * P * len(PIECES[s])], U8, name="x_word%d" % s, align_bytes=64) for s in range(2)]
+        x_scale = [keep.tile([P, PASSES, P * len(PIECES[s])], U8, name="x_scale%d" % s, align_bytes=64) for s in range(2)]
         window = [keep.tile([P, U], F32, name="window%d" % t, tag="window%d" % t) for t in range(PACK)]
 
-        def load_x(s):
-            ints = HALF_T // 2
-            src = xw_dram[:, :, ints * s : ints * (s + 1)].rearrange("z p c -> p z c")
+        def load_x_words(s):
+            ints = P // 2
+            src = xw_dram[:, :, ints * PIECES[s].start : ints * PIECES[s].stop].rearrange("z p c -> p z c")
             nc.sync.dma_start(out=x_word[s][:].bitcast(I32), in_=src)
 
+        def load_x_scales(s):
+            ints = P // 4
+            for q in range(QUADRANTS):
+                src = xs_dram[:, q:16:4, ints * PIECES[s].start : ints * PIECES[s].stop].rearrange("z q c -> q z c")
+                nc.sync.dma_start(out=x_scale[s][q:P:32, :, :].bitcast(I32), in_=src)
+
+        load_w(0)
+        nc.sync.dma_start(out=old_cols[:], in_=old[0:1, :].rearrange("o (p b) -> (o p) b", b=BLOCKS))
+        nc.sync.dma_start(out=row_stage[:], in_=new[0:1, :].rearrange("o (b n) -> (o b) n", n=P))
+        load_x_scales(0)
+        load_w(1)
         nc.sync.dma_start(offs[:], slot)
-        for t in LOADS:
+        load_x_words(0)
+        for t in range(PACK):
             nc.sync.dma_start(out=window[t][:], in_=plane_rows(mem, ORDER[t]))
-            if t > 0 and t < LAST:
-                load_x(t - 1)
+            if t == 0:
+                load_x_scales(1)
+                load_x_words(1)
 
-        for q in range(QUADRANTS):
-            nc.vector.tensor_copy(x_scale[32 * q : 32 * q + 4, :].bitcast(I32), scale_stage[32 * q : 32 * q + 4, :])
-
-        nc.scalar.copy(weight_rows[0 : 2 * BLOCKS, :], row_stage[:])
-        cols_bank = ps_tr.tile([P, BANK], F32, name="tr")
-        nc.tensor.transpose(cols_bank[:, 0:P], weight_rows[:], ident[:])
-        weight_cols = keep.tile([P, 2 * BLOCKS], F32, name="weight_cols")
-        nc.scalar.copy(weight_cols[:], cols_bank[:, 0 : 2 * BLOCKS])
         old_all = keep.tile([P, T], F32, name="old_all")
         for s in range(2):
             bank = ps_tr.tile([P, BANK], F32, name="tr")
             for i, b in enumerate(blocks(s)):
-                nc.tensor.transpose(bank[:, P * i : P * (i + 1)], weight_cols[:, b : b + 1].to_broadcast([P, P]), ident[:])
-            nc.scalar.copy(old_all[:, half(s)], bank[:])
+                nc.tensor.transpose(bank[:, P * i : P * (i + 1)], old_cols[:, b : b + 1].to_broadcast([P, P]), ident[:])
+            nc.scalar.copy(
+                old_all[:].rearrange("m (p s i) -> m s p i", s=2, i=HALF_BLOCKS)[:, s],
+                bank[:].rearrange("m (i p) -> m p i", i=HALF_BLOCKS),
+            )
+        nc.scalar.copy(weight_rows[0:BLOCKS, :], row_stage[:])
+        cols_bank = ps_tr.tile([P, BANK], F32, name="tr")
+        nc.tensor.transpose(cols_bank[:, 0:P], weight_rows[:], ident[:])
+        new_cols = keep.tile([P, BLOCKS], F32, name="new_cols")
+        nc.scalar.copy(new_cols[:], cols_bank[:, 0:BLOCKS])
 
         w_mx = []
         for z in range(PASSES):
             w_grouped = keep.tile([P, PACK * N], BF16, name="w_grouped%d" % z, align_bytes=64)
-            nc.vector.tensor_copy(
-                w_grouped[:].rearrange("p (r l i) -> p l i r", r=PACK, i=PACK),
-                w_raw[z][:].rearrange("p i (l r) -> p l i r", r=PACK),
-            )
+            dealt = w_grouped[:].rearrange("p (r l i) -> p l i r", r=PACK, i=PACK)
+            raw = w_raw[z][:].rearrange("p i (l r) -> p l i r", r=PACK)
+            nc.vector.tensor_copy(dealt[:, 0:W_VECTOR], raw[:, 0:W_VECTOR])
+            nc.scalar.copy(dealt[:, W_VECTOR:P], raw[:, W_VECTOR:P])
             codes = keep.tile([P, N], U32, name="w_codes%d" % z, align_bytes=64)
             scales = keep.tile([P, N], U8, name="w_scales%d" % z, align_bytes=64)
             nc.vector.quantize_mx(out=codes[:].bitcast(FP8X4), scales=scales[:], in_=w_grouped[:])
@@ -127,11 +131,12 @@ def tile_picked_wema_none_lo_kernel(tc, x_words, x_scales, mem, w1, old, new, sl
 
         def mx_pass(out, b, r, z):
             codes, scales = w_mx[z]
-            s, i = divmod(b, HALF_BLOCKS)
+            s = 0 if b < EARLY else 1
+            i = b - PIECES[s].start
             nc.tensor.matmul_mx(
                 out=out,
                 lhsT=x_word[s][:, z, 2 * P * i : 2 * P * (i + 1)].bitcast(FP4X4),
-                lhsT_scale=x_scale[:, T * z + P * b : T * z + P * (b + 1)],
+                lhsT_scale=x_scale[s][:, z, P * i : P * (i + 1)],
                 rhs=codes[:, P * r : P * (r + 1)].bitcast(FP8X4),
                 rhs_scale=scales[:, P * r : P * (r + 1)],
                 start=(z == 0),
@@ -139,24 +144,23 @@ def tile_picked_wema_none_lo_kernel(tc, x_words, x_scales, mem, w1, old, new, sl
             )
 
         def new_of(b):
-            return weight_cols[:, BLOCKS + b : BLOCKS + b + 1]
+            return new_cols[:, b : b + 1]
 
         def turn(sources):
             bank = ps_tr.tile([P, BANK], F32, name="tr")
-            for i in range(HALF_BLOCKS):
-                nc.tensor.transpose(bank[:, P * i : P * (i + 1)], sources[i], ident[:])
-            return bank
+            for i, source in enumerate(sources):
+                nc.tensor.transpose(bank[:, P * i : P * (i + 1)], source, ident[:])
+            return bank[:, 0 : P * len(sources)]
 
         new_y = [keep.tile([P, T], F32, name="new_y%d" % t) for t in range(PACK)]
-        for s in range(2):
-            banks = [ps_mx.tile([P, BANK], F32, name="mx") for b in blocks(s)]
-            for i, b in enumerate(blocks(s)):
+        y_first = keep.tile([P, BLOCKS, P], F32, name="y_first")
+        for run in (range(0, EARLY), range(EARLY, EARLY + HALF_BLOCKS), range(EARLY + HALF_BLOCKS, BLOCKS)):
+            for b in run:
+                bank = ps_mx.tile([P, BANK], F32, name="mx")
                 for z in range(PASSES):
-                    mx_pass(banks[i][:, 0:P], b, ORDER[0], z)
-            y_first = keep.tile([P, HALF_BLOCKS, P], F32, name="y_first%d" % s)
-            for i, b in enumerate(blocks(s)):
-                nc.scalar.activation(y_first[:, i, :], banks[i][:, 0:P], COPY, scale=new_of(b))
-            nc.scalar.copy(new_y[0][:, half(s)], turn([y_first[:, i, :] for i in range(HALF_BLOCKS)])[:])
+                    mx_pass(bank[:, 0:P], b, ORDER[0], z)
+                nc.scalar.activation(y_first[:, b, :], bank[:, 0:P], COPY, scale=new_of(b))
+            nc.scalar.copy(new_y[0][:, P * run.start : P * run.stop], turn([y_first[:, b, :] for b in run]))
 
         y_rest = keep.tile([P, BLOCKS, LAST, P], F32, name="y_rest", tag="y_rest", align_bytes=64)
         for b in range(BLOCKS):
@@ -167,7 +171,7 @@ def tile_picked_wema_none_lo_kernel(tc, x_words, x_scales, mem, w1, old, new, sl
             nc.scalar.activation(y_rest[:, b, :, :].rearrange("p t l -> p (t l)"), bank[:, 0 : P * LAST], COPY, scale=new_of(b))
         for t in range(1, PACK):
             for s in range(2):
-                nc.scalar.copy(new_y[t][:, half(s)], turn([y_rest[:, b, t - 1, :] for b in blocks(s)])[:])
+                nc.scalar.copy(new_y[t][:, half(s)], turn([y_rest[:, b, t - 1, :] for b in blocks(s)]))
 
         def gather(t, tag):
             old_mem = keep.tile([P, T], F32, name="old_mem%d" % t, tag=tag)
@@ -182,13 +186,12 @@ def tile_picked_wema_none_lo_kernel(tc, x_words, x_scales, mem, w1, old, new, sl
                 copy = nc.vector.tensor_copy if t == LAST and c < VECTOR_CHUNKS else nc.scalar.copy
                 copy(grouped[:, chunk(c), ORDER[t]], window[t][:, chunk(c)])
 
-        second = gather(1, "old_mem1")
-        old_mem = [gather(0, "old_mem0"), second]
-        nc.vector.tensor_tensor(window[0][:].indirect(offs[:, 0:LIST_HALF]), old_mem[0][:, half(0)], new_y[0][:, half(0)], ADD)
-        old_mem.append(gather(2, "old_mem2"))
-        nc.vector.tensor_tensor(
-            window[0][:].indirect(offs[:, LIST_HALF : 2 * LIST_HALF]), old_mem[0][:, half(1)], new_y[0][:, half(1)], ADD
-        )
+        old_mem = [gather(0, "old_mem0")]
+        for s, piece in enumerate(PIECES):
+            entries = slice(P * piece.start, P * piece.stop)
+            names = offs[:, P // 16 * piece.start : P // 16 * piece.stop]
+            nc.vector.tensor_tensor(window[0][:].indirect(names), old_mem[0][:, entries], new_y[0][:, entries], ADD)
+            old_mem.append(gather(s + 1, "old_mem%d" % (s + 1)))
         finish(0)
         for t in range(1, LAST):
             nc.vector.tensor_tensor(window[t][:].indirect(offs[:]), old_mem[t][:], new_y[t][:], ADD)
@@ -211,4 +214,4 @@ def tile_picked_wema_none_lo_kernel(tc, x_words, x_scales, mem, w1, old, new, sl
         scales_dram = out_2[0].bitcast(I32)
         for q in range(QUADRANTS):
             queue = nc.scalar if q % 2 == 0 else nc.sync
-            queue.dma_start(out=scales_dram[4 * q : 4 * q + 4, :], in_=out_scale[32 * q : 32 * q + 4, :].bitcast(I32))
+            queue.dma_start(out=scales_dram[q:16:4, :], in_=out_scale[q:P:32, :].bitcast(I32))

@@ -32,9 +32,9 @@ PIECES = (range(0, EARLY), range(EARLY, BLOCKS))
 CHUNKS = 4
 CHUNK = U // CHUNKS
 VECTOR_CHUNKS = 2
-ORDER = (2, 0, 1, 3)
+ORDER = (0, 2, 3, 1)
 LAST = PACK - 1
-W_VECTOR = 96
+W_VECTOR = (64, 96)
 
 
 def tile_picked_wema_none_lo_kernel(tc, x_words, x_scales, mem, w1, old, new, slot, out_0, out_1, out_2):
@@ -89,18 +89,22 @@ def tile_picked_wema_none_lo_kernel(tc, x_words, x_scales, mem, w1, old, new, sl
                 src = xs_dram[:, q:16:4, ints * PIECES[s].start : ints * PIECES[s].stop].rearrange("z q c -> q z c")
                 nc.sync.dma_start(out=x_scale[s][q:P:32, :, :].bitcast(I32), in_=src)
 
-        load_w(0)
+        def load_window(t):
+            nc.sync.dma_start(out=window[t][:], in_=plane_rows(mem, ORDER[t]))
+
         nc.sync.dma_start(out=old_cols[:], in_=old[0:1, :].rearrange("o (p b) -> (o p) b", b=BLOCKS))
         nc.sync.dma_start(out=row_stage[:], in_=new[0:1, :].rearrange("o (b n) -> (o b) n", n=P))
-        load_x_scales(0)
-        load_w(1)
+        load_window(0)
         nc.sync.dma_start(offs[:], slot)
+        load_x_scales(0)
+        load_w(0)
         load_x_words(0)
-        for t in range(PACK):
-            nc.sync.dma_start(out=window[t][:], in_=plane_rows(mem, ORDER[t]))
-            if t == 0:
-                load_x_scales(1)
-                load_x_words(1)
+        load_w(1)
+        load_window(1)
+        load_x_words(1)
+        load_x_scales(1)
+        load_window(2)
+        load_window(LAST)
 
         old_all = keep.tile([P, T], F32, name="old_all")
         for s in range(2):
@@ -117,16 +121,28 @@ def tile_picked_wema_none_lo_kernel(tc, x_words, x_scales, mem, w1, old, new, sl
         new_cols = keep.tile([P, BLOCKS], F32, name="new_cols")
         nc.scalar.copy(new_cols[:], cols_bank[:, 0:BLOCKS])
 
+        def gather(t, tag):
+            old_mem = keep.tile([P, T], F32, name="old_mem%d" % t, tag=tag)
+            nc.vector.tensor_tensor(old_mem[:], window[t][:].indirect(offs[:]), old_all[:], MULT)
+            return old_mem
+
+        old_mem = [gather(0, "old_mem0")]
+
         w_mx = []
         for z in range(PASSES):
             w_grouped = keep.tile([P, PACK * N], BF16, name="w_grouped%d" % z, align_bytes=64)
             dealt = w_grouped[:].rearrange("p (r l i) -> p l i r", r=PACK, i=PACK)
             raw = w_raw[z][:].rearrange("p i (l r) -> p l i r", r=PACK)
-            nc.vector.tensor_copy(dealt[:, 0:W_VECTOR], raw[:, 0:W_VECTOR])
-            nc.scalar.copy(dealt[:, W_VECTOR:P], raw[:, W_VECTOR:P])
+            nc.vector.tensor_copy(dealt[:, 0 : W_VECTOR[z]], raw[:, 0 : W_VECTOR[z]])
+            nc.scalar.copy(dealt[:, W_VECTOR[z] : P], raw[:, W_VECTOR[z] : P])
             codes = keep.tile([P, N], U32, name="w_codes%d" % z, align_bytes=64)
             scales = keep.tile([P, N], U8, name="w_scales%d" % z, align_bytes=64)
-            nc.vector.quantize_mx(out=codes[:].bitcast(FP8X4), scales=scales[:], in_=w_grouped[:])
+            for lo, hi in ((0, PACK),) if z == 0 else ((0, 1), (1, 2), (2, PACK)):
+                nc.vector.quantize_mx(
+                    out=codes[:, P * lo : P * hi].bitcast(FP8X4),
+                    scales=scales[:, P * lo : P * hi],
+                    in_=w_grouped[:, PACK * P * lo : PACK * P * hi],
+                )
             w_mx.append((codes, scales))
 
         def mx_pass(out, b, r, z):
@@ -155,11 +171,11 @@ def tile_picked_wema_none_lo_kernel(tc, x_words, x_scales, mem, w1, old, new, sl
         new_y = [keep.tile([P, T], F32, name="new_y%d" % t) for t in range(PACK)]
         y_first = keep.tile([P, BLOCKS, P], F32, name="y_first")
         for run in (range(0, EARLY), range(EARLY, EARLY + HALF_BLOCKS), range(EARLY + HALF_BLOCKS, BLOCKS)):
+            banks = {b: ps_mx.tile([P, BANK], F32, name="mx") for b in run}
             for b in run:
-                bank = ps_mx.tile([P, BANK], F32, name="mx")
                 for z in range(PASSES):
-                    mx_pass(bank[:, 0:P], b, ORDER[0], z)
-                nc.scalar.activation(y_first[:, b, :], bank[:, 0:P], COPY, scale=new_of(b))
+                    mx_pass(banks[b][:, 0:P], b, ORDER[0], z)
+                nc.scalar.activation(y_first[:, b, :], banks[b][:, 0:P], COPY, scale=new_of(b))
             nc.scalar.copy(new_y[0][:, P * run.start : P * run.stop], turn([y_first[:, b, :] for b in run]))
 
         y_rest = keep.tile([P, BLOCKS, LAST, P], F32, name="y_rest", tag="y_rest", align_bytes=64)
@@ -173,11 +189,6 @@ def tile_picked_wema_none_lo_kernel(tc, x_words, x_scales, mem, w1, old, new, sl
             for s in range(2):
                 nc.scalar.copy(new_y[t][:, half(s)], turn([y_rest[:, b, t - 1, :] for b in blocks(s)]))
 
-        def gather(t, tag):
-            old_mem = keep.tile([P, T], F32, name="old_mem%d" % t, tag=tag)
-            nc.vector.tensor_tensor(old_mem[:], window[t][:].indirect(offs[:]), old_all[:], MULT)
-            return old_mem
-
         grouped = keep.tile([P, U, PACK], BF16, name="grouped", tag="y_rest", align_bytes=64)
 
         def finish(t):
@@ -186,12 +197,13 @@ def tile_picked_wema_none_lo_kernel(tc, x_words, x_scales, mem, w1, old, new, sl
                 copy = nc.vector.tensor_copy if t == LAST and c < VECTOR_CHUNKS else nc.scalar.copy
                 copy(grouped[:, chunk(c), ORDER[t]], window[t][:, chunk(c)])
 
-        old_mem = [gather(0, "old_mem0")]
+        old_mem.append(gather(1, "old_mem1"))
         for s, piece in enumerate(PIECES):
             entries = slice(P * piece.start, P * piece.stop)
             names = offs[:, P // 16 * piece.start : P // 16 * piece.stop]
             nc.vector.tensor_tensor(window[0][:].indirect(names), old_mem[0][:, entries], new_y[0][:, entries], ADD)
-            old_mem.append(gather(s + 1, "old_mem%d" % (s + 1)))
+            if s == 0:
+                old_mem.append(gather(2, "old_mem2"))
         finish(0)
         for t in range(1, LAST):
             nc.vector.tensor_tensor(window[t][:].indirect(offs[:]), old_mem[t][:], new_y[t][:], ADD)

@@ -22,19 +22,21 @@ P = 128
 PACK = 4
 K_PASS = P * PACK
 PASSES = K // K_PASS
-QUADRANTS = 4
+QUADRANT = 32
+SCALE_ROWS = 16
 BANK = 512
 BLOCKS = T // P
 HALF_BLOCKS = BLOCKS // 2
 HALF_T = T // 2
 EARLY = 2
 PIECES = (range(0, EARLY), range(EARLY, BLOCKS))
-CHUNKS = 4
-CHUNK = U // CHUNKS
+EDGES = (0, 512, 1024, 1536, 1792, 2048)
+CHUNKS = len(EDGES) - 1
 VECTOR_CHUNKS = 2
+CHUNK_ORDER = (0, VECTOR_CHUNKS, 1) + tuple(range(VECTOR_CHUNKS + 1, CHUNKS))
 ORDER = (0, 2, 3, 1)
 LAST = PACK - 1
-W_VECTOR = (64, 96)
+W_VECTOR = (32, 96)
 
 
 def tile_picked_wema_none_lo_kernel(tc, x_words, x_scales, mem, w1, old, new, slot, out_0, out_1, out_2):
@@ -50,7 +52,7 @@ def tile_picked_wema_none_lo_kernel(tc, x_words, x_scales, mem, w1, old, new, sl
         return range(HALF_BLOCKS * s, HALF_BLOCKS * (s + 1))
 
     def chunk(c):
-        return slice(CHUNK * c, CHUNK * (c + 1))
+        return slice(EDGES[c], EDGES[c + 1])
 
     with ExitStack() as ctx:
         keep = ctx.enter_context(tc.tile_pool(name="keep", bufs=1))
@@ -59,8 +61,8 @@ def tile_picked_wema_none_lo_kernel(tc, x_words, x_scales, mem, w1, old, new, sl
 
         offs = keep.tile([P, T // 16], U16, name="offs")
         ident = keep.tile([P, P], F32, name="ident")
-        weight_rows = keep.tile([P, P], F32, name="weight_rows")
-        nc.gpsimd.memset(weight_rows[:], 0.0)
+        new_rows = keep.tile([P, P], F32, name="new_rows")
+        nc.gpsimd.memset(new_rows[:], 0.0)
         make_identity(nc, ident[:])
 
         xw_dram = x_words.bitcast(I32)
@@ -85,9 +87,9 @@ def tile_picked_wema_none_lo_kernel(tc, x_words, x_scales, mem, w1, old, new, sl
 
         def load_x_scales(s):
             ints = P // 4
-            for q in range(QUADRANTS):
-                src = xs_dram[:, q:16:4, ints * PIECES[s].start : ints * PIECES[s].stop].rearrange("z q c -> q z c")
-                nc.sync.dma_start(out=x_scale[s][q:P:32, :, :].bitcast(I32), in_=src)
+            for q in range(PACK):
+                src = xs_dram[:, q:SCALE_ROWS:PACK, ints * PIECES[s].start : ints * PIECES[s].stop].rearrange("z q c -> q z c")
+                nc.sync.dma_start(out=x_scale[s][q:P:QUADRANT, :, :].bitcast(I32), in_=src)
 
         def load_window(t):
             nc.sync.dma_start(out=window[t][:], in_=plane_rows(mem, ORDER[t]))
@@ -115,9 +117,9 @@ def tile_picked_wema_none_lo_kernel(tc, x_words, x_scales, mem, w1, old, new, sl
                 old_all[:].rearrange("m (p s i) -> m s p i", s=2, i=HALF_BLOCKS)[:, s],
                 bank[:].rearrange("m (i p) -> m p i", i=HALF_BLOCKS),
             )
-        nc.scalar.copy(weight_rows[0:BLOCKS, :], row_stage[:])
+        nc.scalar.copy(new_rows[0:BLOCKS, :], row_stage[:])
         cols_bank = ps_tr.tile([P, BANK], F32, name="tr")
-        nc.tensor.transpose(cols_bank[:, 0:P], weight_rows[:], ident[:])
+        nc.tensor.transpose(cols_bank[:, 0:P], new_rows[:], ident[:])
         new_cols = keep.tile([P, BLOCKS], F32, name="new_cols")
         nc.scalar.copy(new_cols[:], cols_bank[:, 0:BLOCKS])
 
@@ -193,9 +195,12 @@ def tile_picked_wema_none_lo_kernel(tc, x_words, x_scales, mem, w1, old, new, sl
 
         def finish(t):
             nc.sync.dma_start(out=plane_rows(out_0, ORDER[t]), in_=window[t][:])
-            for c in range(CHUNKS):
-                copy = nc.vector.tensor_copy if t == LAST and c < VECTOR_CHUNKS else nc.scalar.copy
-                copy(grouped[:, chunk(c), ORDER[t]], window[t][:, chunk(c)])
+            if t < LAST:
+                nc.scalar.copy(grouped[:, :, ORDER[t]], window[t][:])
+            else:
+                for c in range(CHUNKS):
+                    copy = nc.vector.tensor_copy if c < VECTOR_CHUNKS else nc.scalar.copy
+                    copy(grouped[:, chunk(c), ORDER[t]], window[t][:, chunk(c)])
 
         old_mem.append(gather(1, "old_mem1"))
         for s, piece in enumerate(PIECES):
@@ -214,16 +219,15 @@ def tile_picked_wema_none_lo_kernel(tc, x_words, x_scales, mem, w1, old, new, sl
 
         out_scale = keep.tile([P, U], U8, name="out_scale", align_bytes=64)
         words_dram = out_1[0].rearrange("p c r -> p (c r)").bitcast(I32)
-        for first in range(VECTOR_CHUNKS):
-            for c in (first, VECTOR_CHUNKS + first):
-                words = keep.tile([P, CHUNK], U32, name="words%d" % c, align_bytes=64)
-                nc.vector.quantize_mx(
-                    out=words[:].bitcast(FP8X4),
-                    scales=out_scale[:, chunk(c)],
-                    in_=grouped[:, chunk(c), :].rearrange("p c r -> p (c r)"),
-                )
-                nc.sync.dma_start(out=words_dram[:, chunk(c)], in_=words[:].bitcast(I32))
+        for c in CHUNK_ORDER:
+            words = keep.tile([P, EDGES[c + 1] - EDGES[c]], U32, name="words%d" % c, align_bytes=64)
+            nc.vector.quantize_mx(
+                out=words[:].bitcast(FP8X4),
+                scales=out_scale[:, chunk(c)],
+                in_=grouped[:, chunk(c), :].rearrange("p c r -> p (c r)"),
+            )
+            nc.sync.dma_start(out=words_dram[:, chunk(c)], in_=words[:].bitcast(I32))
         scales_dram = out_2[0].bitcast(I32)
-        for q in range(QUADRANTS):
+        for q in range(PACK):
             queue = nc.scalar if q % 2 == 0 else nc.sync
-            queue.dma_start(out=scales_dram[q:16:4, :], in_=out_scale[q:P:32, :].bitcast(I32))
+            queue.dma_start(out=scales_dram[q:SCALE_ROWS:PACK, :], in_=out_scale[q:P:QUADRANT, :].bitcast(I32))

@@ -78,7 +78,7 @@ def tile_picked_wema_none_lo_kernel(tc, x_words, x_scales, mem, w1, old, new, sl
 
         x_word = [keep.tile([P, PASSES, 2 * P * len(PIECES[s])], U8, name="x_word%d" % s, align_bytes=64) for s in range(2)]
         x_scale = [keep.tile([P, PASSES, P * len(PIECES[s])], U8, name="x_scale%d" % s, align_bytes=64) for s in range(2)]
-        window = [keep.tile([P, U], F32, name="window%d" % t, tag="window%d" % t) for t in range(PACK)]
+        window = [keep.tile([P, U], F32, name="window%d" % t) for t in range(PACK)]
 
         def load_x_words(s):
             ints = P // 2
@@ -123,12 +123,12 @@ def tile_picked_wema_none_lo_kernel(tc, x_words, x_scales, mem, w1, old, new, sl
         new_cols = keep.tile([P, BLOCKS], F32, name="new_cols")
         nc.scalar.copy(new_cols[:], cols_bank[:, 0:BLOCKS])
 
-        def gather(t, tag):
-            old_mem = keep.tile([P, T], F32, name="old_mem%d" % t, tag=tag)
+        def gather(t):
+            old_mem = keep.tile([P, T], F32, name="old_mem%d" % t)
             nc.vector.tensor_tensor(old_mem[:], window[t][:].indirect(offs[:]), old_all[:], MULT)
             return old_mem
 
-        old_mem = [gather(0, "old_mem0")]
+        old_mem = [gather(0)]
 
         w_mx = []
         for z in range(PASSES):
@@ -195,27 +195,27 @@ def tile_picked_wema_none_lo_kernel(tc, x_words, x_scales, mem, w1, old, new, sl
 
         def finish(t):
             nc.sync.dma_start(out=plane_rows(out_0, ORDER[t]), in_=window[t][:])
-            if t < LAST:
+            if t == 0:
+                nc.scalar.copy(grouped[:, :, 0:2], window[t][:].unsqueeze(2).to_broadcast([P, U, 2]))
+            elif t < LAST:
                 nc.scalar.copy(grouped[:, :, ORDER[t]], window[t][:])
             else:
                 for c in range(CHUNKS):
                     copy = nc.vector.tensor_copy if c < VECTOR_CHUNKS else nc.scalar.copy
                     copy(grouped[:, chunk(c), ORDER[t]], window[t][:, chunk(c)])
 
-        old_mem.append(gather(1, "old_mem1"))
+        old_mem.append(gather(1))
         for s, piece in enumerate(PIECES):
             entries = slice(P * piece.start, P * piece.stop)
             names = offs[:, P // 16 * piece.start : P // 16 * piece.stop]
             nc.vector.tensor_tensor(window[0][:].indirect(names), old_mem[0][:, entries], new_y[0][:, entries], ADD)
             if s == 0:
-                old_mem.append(gather(2, "old_mem2"))
+                old_mem.append(gather(2))
+        old_mem.append(gather(LAST))
         finish(0)
-        for t in range(1, LAST):
+        for t in range(1, PACK):
             nc.vector.tensor_tensor(window[t][:].indirect(offs[:]), old_mem[t][:], new_y[t][:], ADD)
             finish(t)
-        old_mem.append(gather(LAST, "window0"))
-        nc.vector.tensor_tensor(window[LAST][:].indirect(offs[:]), old_mem[LAST][:], new_y[LAST][:], ADD)
-        finish(LAST)
 
         out_scale = keep.tile([P, U], U8, name="out_scale", align_bytes=64)
         words_dram = out_1[0].rearrange("p c r -> p (c r)").bitcast(I32)

@@ -23,27 +23,23 @@ PACK = 4
 K_PASS = P * PACK
 PASSES = K // K_PASS
 QUADRANT = 32
+QUADRANTS = P // QUADRANT
 SCALE_ROWS = 16
 BANK = 512
 BLOCKS = T // P
 HALF_BLOCKS = BLOCKS // 2
 HALF_T = T // 2
-EARLY = 2
+WINDOWS = N // P
+LAST = WINDOWS - 1
+STRETCH = U // QUADRANTS
+CHUNKS = STRETCH // P
+EARLY = 3
 PIECES = (range(0, EARLY), range(EARLY, BLOCKS))
-EDGES = (0, 512, 1024, 1536, 1792, 2048)
-CHUNKS = len(EDGES) - 1
-VECTOR_CHUNKS = 2
-CHUNK_ORDER = (0, VECTOR_CHUNKS, 1) + tuple(range(VECTOR_CHUNKS + 1, CHUNKS))
-ORDER = (0, 2, 3, 1)
-LAST = PACK - 1
-W_VECTOR = (32, 96)
+W_GROUPS = (range(0, 1), range(1, 2), range(2, WINDOWS))
 
 
 def tile_picked_wema_none_lo_kernel(tc, x_words, x_scales, mem, w1, old, new, slot, out_0, out_1, out_2):
     nc = tc.nc
-
-    def plane_rows(ap, r):
-        return ap.rearrange("(p r) c -> r p c", r=PACK)[r]
 
     def half(s):
         return slice(HALF_T * s, HALF_T * (s + 1))
@@ -51,13 +47,22 @@ def tile_picked_wema_none_lo_kernel(tc, x_words, x_scales, mem, w1, old, new, sl
     def blocks(s):
         return range(HALF_BLOCKS * s, HALF_BLOCKS * (s + 1))
 
-    def chunk(c):
-        return slice(EDGES[c], EDGES[c + 1])
-
     with ExitStack() as ctx:
         keep = ctx.enter_context(tc.tile_pool(name="keep", bufs=1))
-        ps_mx = ctx.enter_context(tc.psum_pool(name="ps_mx", bufs=4))
-        ps_tr = ctx.enter_context(tc.psum_pool(name="ps_tr", bufs=4))
+        psum = ctx.enter_context(tc.psum_pool(name="psum", bufs=1))
+        taken = {"mx": 0, "tr": 0}
+
+        def next_bank(kind):
+            place = taken[kind] % 4 + (4 if kind == "tr" else 0)
+            taken[kind] = taken[kind] + 1
+            return psum.tile([P, BANK], F32, name="%s%d" % (kind, taken[kind]), offset=4 * BANK * place)
+
+        shared = ctx.enter_context(tc.tile_pool(name="shared", bufs=1))
+        places = {}
+
+        def shared_tile(shape, dtype, name, tag, skip=0):
+            places.setdefault(tag, 4 * T * len(places))
+            return shared.tile(shape, dtype, name=name, offset=places[tag] + skip, align_bytes=64)
 
         offs = keep.tile([P, T // 16], U16, name="offs")
         ident = keep.tile([P, P], F32, name="ident")
@@ -70,15 +75,17 @@ def tile_picked_wema_none_lo_kernel(tc, x_words, x_scales, mem, w1, old, new, sl
 
         row_stage = keep.tile([BLOCKS, P], F32, name="row_stage")
         old_cols = keep.tile([P, BLOCKS], F32, name="old_cols")
-        w_raw = [keep.tile([P, PACK, N], F32, name="w_raw%d" % z) for z in range(PASSES)]
+        w_raw = [[keep.tile([P, PACK, P * len(group)], F32, name="w_raw%d_%d" % (g, z)) for z in range(PASSES)] for g, group in enumerate(W_GROUPS)]
 
-        def load_w(z):
-            rows = w1[K_PASS * z : K_PASS * (z + 1), :]
-            nc.sync.dma_start(out=w_raw[z][:], in_=rows.rearrange("(p i) n -> p i n", i=PACK))
+        def load_w(g):
+            cols = slice(P * W_GROUPS[g].start, P * W_GROUPS[g].stop)
+            for z in range(PASSES):
+                rows = w1[K_PASS * z : K_PASS * (z + 1), cols]
+                nc.sync.dma_start(out=w_raw[g][z][:], in_=rows.rearrange("(p i) n -> p i n", i=PACK))
 
         x_word = [keep.tile([P, PASSES, 2 * P * len(PIECES[s])], U8, name="x_word%d" % s, align_bytes=64) for s in range(2)]
         x_scale = [keep.tile([P, PASSES, P * len(PIECES[s])], U8, name="x_scale%d" % s, align_bytes=64) for s in range(2)]
-        window = [keep.tile([P, U], F32, name="window%d" % t) for t in range(PACK)]
+        window = [keep.tile([P, U], F32, name="window%d" % t) for t in range(WINDOWS)]
 
         def load_x_words(s):
             ints = P // 2
@@ -92,25 +99,26 @@ def tile_picked_wema_none_lo_kernel(tc, x_words, x_scales, mem, w1, old, new, sl
                 nc.sync.dma_start(out=x_scale[s][q:P:QUADRANT, :, :].bitcast(I32), in_=src)
 
         def load_window(t):
-            nc.sync.dma_start(out=window[t][:], in_=plane_rows(mem, ORDER[t]))
+            nc.sync.dma_start(out=window[t][:], in_=mem[P * t : P * (t + 1), :])
 
         nc.sync.dma_start(out=old_cols[:], in_=old[0:1, :].rearrange("o (p b) -> (o p) b", b=BLOCKS))
         nc.sync.dma_start(out=row_stage[:], in_=new[0:1, :].rearrange("o (b n) -> (o b) n", n=P))
-        load_window(0)
-        nc.sync.dma_start(offs[:], slot)
-        load_x_scales(0)
         load_w(0)
-        load_x_words(0)
-        load_w(1)
+        nc.sync.dma_start(offs[:], slot)
         load_window(1)
+        load_x_scales(0)
+        load_x_words(0)
+        load_window(0)
         load_x_words(1)
         load_x_scales(1)
+        load_w(1)
         load_window(2)
+        load_w(2)
         load_window(LAST)
 
         old_all = keep.tile([P, T], F32, name="old_all")
         for s in range(2):
-            bank = ps_tr.tile([P, BANK], F32, name="tr")
+            bank = next_bank("tr")
             for i, b in enumerate(blocks(s)):
                 nc.tensor.transpose(bank[:, P * i : P * (i + 1)], old_cols[:, b : b + 1].to_broadcast([P, P]), ident[:])
             nc.scalar.copy(
@@ -118,116 +126,172 @@ def tile_picked_wema_none_lo_kernel(tc, x_words, x_scales, mem, w1, old, new, sl
                 bank[:].rearrange("m (i p) -> m p i", i=HALF_BLOCKS),
             )
         nc.scalar.copy(new_rows[0:BLOCKS, :], row_stage[:])
-        cols_bank = ps_tr.tile([P, BANK], F32, name="tr")
+        cols_bank = next_bank("tr")
         nc.tensor.transpose(cols_bank[:, 0:P], new_rows[:], ident[:])
         new_cols = keep.tile([P, BLOCKS], F32, name="new_cols")
         nc.scalar.copy(new_cols[:], cols_bank[:, 0:BLOCKS])
 
-        def gather(t):
-            old_mem = keep.tile([P, T], F32, name="old_mem%d" % t)
-            nc.vector.tensor_tensor(old_mem[:], window[t][:].indirect(offs[:]), old_all[:], MULT)
-            return old_mem
+        def entries(piece):
+            return slice(P * piece.start, P * piece.stop)
 
-        old_mem = [gather(0)]
+        def names(piece):
+            return offs[:, P // 16 * piece.start : P // 16 * piece.stop]
 
-        w_mx = []
-        for z in range(PASSES):
-            w_grouped = keep.tile([P, PACK * N], BF16, name="w_grouped%d" % z, align_bytes=64)
-            dealt = w_grouped[:].rearrange("p (r l i) -> p l i r", r=PACK, i=PACK)
-            raw = w_raw[z][:].rearrange("p i (l r) -> p l i r", r=PACK)
-            nc.vector.tensor_copy(dealt[:, 0 : W_VECTOR[z]], raw[:, 0 : W_VECTOR[z]])
-            nc.scalar.copy(dealt[:, W_VECTOR[z] : P], raw[:, W_VECTOR[z] : P])
-            codes = keep.tile([P, N], U32, name="w_codes%d" % z, align_bytes=64)
-            scales = keep.tile([P, N], U8, name="w_scales%d" % z, align_bytes=64)
-            for lo, hi in ((0, PACK),) if z == 0 else ((0, 1), (1, 2), (2, PACK)):
-                nc.vector.quantize_mx(
-                    out=codes[:, P * lo : P * hi].bitcast(FP8X4),
-                    scales=scales[:, P * lo : P * hi],
-                    in_=w_grouped[:, PACK * P * lo : PACK * P * hi],
-                )
-            w_mx.append((codes, scales))
+        def gather(t, pieces, tag):
+            looked_up = shared_tile([P, T], F32, "old_mem%d" % t, tag)
+            for piece in pieces:
+                nc.vector.tensor_tensor(looked_up[:, entries(piece)], window[t][:].indirect(names(piece)), old_all[:, entries(piece)], MULT)
+            return looked_up
 
-        def mx_pass(out, b, r, z):
-            codes, scales = w_mx[z]
+        w_mx = {}
+
+        def quantise_w(g, copy, tag):
+            group = W_GROUPS[g]
+            width = len(group) * PASSES * P
+            grouped = shared_tile([P, width * PACK], BF16, "w_grouped%d" % g, "w_grouped%d" % g)
+            laid = grouped[:].rearrange("p (t z c k i) -> p z t c i k", z=PASSES, c=P // 4, k=4, i=PACK)
+            for z in range(PASSES):
+                for i, t in enumerate(group):
+                    copy(laid[:, z, i], w_raw[g][z][:, :, P * i : P * (i + 1)].rearrange("p i (c k) -> p c i k", k=4))
+            codes = shared_tile([P, width], U32, "w_codes%d" % g, tag)
+            scales = keep.tile([P, width], U8, name="w_scales%d" % g, align_bytes=64)
+            nc.vector.quantize_mx(out=codes[:].bitcast(FP8X4), scales=scales[:], in_=grouped[:])
+            for i, t in enumerate(group):
+                for z in range(PASSES):
+                    cols = slice(P * (PASSES * i + z), P * (PASSES * i + z + 1))
+                    w_mx[(t, z)] = (codes[:, cols], scales[:, cols])
+
+        def mx_pass(out, b, t, z):
+            codes, scales = w_mx[(t, z)]
             s = 0 if b < EARLY else 1
             i = b - PIECES[s].start
             nc.tensor.matmul_mx(
                 out=out,
                 lhsT=x_word[s][:, z, 2 * P * i : 2 * P * (i + 1)].bitcast(FP4X4),
                 lhsT_scale=x_scale[s][:, z, P * i : P * (i + 1)],
-                rhs=codes[:, P * r : P * (r + 1)].bitcast(FP8X4),
-                rhs_scale=scales[:, P * r : P * (r + 1)],
+                rhs=codes.bitcast(FP8X4),
+                rhs_scale=scales,
                 start=(z == 0),
                 stop=(z == PASSES - 1),
             )
 
-        def new_of(b):
-            return new_cols[:, b : b + 1]
-
         def turn(sources):
-            bank = ps_tr.tile([P, BANK], F32, name="tr")
+            bank = next_bank("tr")
             for i, source in enumerate(sources):
                 nc.tensor.transpose(bank[:, P * i : P * (i + 1)], source, ident[:])
             return bank[:, 0 : P * len(sources)]
 
-        new_y = [keep.tile([P, T], F32, name="new_y%d" % t) for t in range(PACK)]
-        y_first = keep.tile([P, BLOCKS, P], F32, name="y_first")
-        for run in (range(0, EARLY), range(EARLY, EARLY + HALF_BLOCKS), range(EARLY + HALF_BLOCKS, BLOCKS)):
-            banks = {b: ps_mx.tile([P, BANK], F32, name="mx") for b in run}
-            for b in run:
-                for z in range(PASSES):
-                    mx_pass(banks[b][:, 0:P], b, ORDER[0], z)
-                nc.scalar.activation(y_first[:, b, :], banks[b][:, 0:P], COPY, scale=new_of(b))
-            nc.scalar.copy(new_y[0][:, P * run.start : P * run.stop], turn([y_first[:, b, :] for b in run]))
+        new_y = {}
 
-        y_rest = keep.tile([P, BLOCKS, LAST, P], F32, name="y_rest", tag="y_rest", align_bytes=64)
-        for b in range(BLOCKS):
-            bank = ps_mx.tile([P, BANK], F32, name="mx")
-            for t in range(1, PACK):
-                for z in range(PASSES):
-                    mx_pass(bank[:, P * (t - 1) : P * t], b, ORDER[t], z)
-            nc.scalar.activation(y_rest[:, b, :, :].rearrange("p t l -> p (t l)"), bank[:, 0 : P * LAST], COPY, scale=new_of(b))
-        for t in range(1, PACK):
-            for s in range(2):
-                nc.scalar.copy(new_y[t][:, half(s)], turn([y_rest[:, b, t - 1, :] for b in blocks(s)]))
+        def read_out(g, runs):
+            group = W_GROUPS[g]
+            made = []
+            for run in runs:
+                y = keep.tile([P, len(run), len(group), P], F32, name="y%d_%d" % (g, run.start))
+                for j, b in enumerate(run):
+                    bank = next_bank("mx")
+                    for i, t in enumerate(group):
+                        for z in range(PASSES):
+                            mx_pass(bank[:, P * i : P * (i + 1)], b, t, z)
+                    nc.scalar.activation(y[:, j].rearrange("p t l -> p (t l)"), bank[:, 0 : P * len(group)], COPY, scale=new_cols[:, b : b + 1])
+                made.append((run, y))
+            return made
 
-        grouped = keep.tile([P, U, PACK], BF16, name="grouped", tag="y_rest", align_bytes=64)
+        def turn_back(t, i, made):
+            if True:
+                for run, y in made:
+                    nc.scalar.copy(new_y[t][:, P * run.start : P * run.stop], turn([y[:, j, i, :] for j in range(len(run))]))
 
-        def finish(t):
-            nc.sync.dma_start(out=plane_rows(out_0, ORDER[t]), in_=window[t][:])
-            if t == 0:
-                nc.scalar.copy(grouped[:, :, 0:2], window[t][:].unsqueeze(2).to_broadcast([P, U, 2]))
-            elif t < LAST:
-                nc.scalar.copy(grouped[:, :, ORDER[t]], window[t][:])
-            else:
-                for c in range(CHUNKS):
-                    copy = nc.vector.tensor_copy if c < VECTOR_CHUNKS else nc.scalar.copy
-                    copy(grouped[:, chunk(c), ORDER[t]], window[t][:, chunk(c)])
+        old_mem = {}
 
-        old_mem.append(gather(1))
-        for s, piece in enumerate(PIECES):
-            entries = slice(P * piece.start, P * piece.stop)
-            names = offs[:, P // 16 * piece.start : P // 16 * piece.stop]
-            nc.vector.tensor_tensor(window[0][:].indirect(names), old_mem[0][:, entries], new_y[0][:, entries], ADD)
-            if s == 0:
-                old_mem.append(gather(2))
-        old_mem.append(gather(LAST))
-        finish(0)
-        for t in range(1, PACK):
-            nc.vector.tensor_tensor(window[t][:].indirect(offs[:]), old_mem[t][:], new_y[t][:], ADD)
-            finish(t)
+        def scatter(t, piece):
+            nc.vector.tensor_tensor(window[t][:].indirect(names(piece)), old_mem[t][:, entries(piece)], new_y[t][:, entries(piece)], ADD)
 
-        out_scale = keep.tile([P, U], U8, name="out_scale", align_bytes=64)
+        out_scale = keep.tile([P, STRETCH], U8, name="out_scale", align_bytes=64)
         words_dram = out_1[0].rearrange("p c r -> p (c r)").bitcast(I32)
-        for c in CHUNK_ORDER:
-            words = keep.tile([P, EDGES[c + 1] - EDGES[c]], U32, name="words%d" % c, align_bytes=64)
-            nc.vector.quantize_mx(
-                out=words[:].bitcast(FP8X4),
-                scales=out_scale[:, chunk(c)],
-                in_=grouped[:, chunk(c), :].rearrange("p c r -> p (c r)"),
-            )
-            nc.sync.dma_start(out=words_dram[:, chunk(c)], in_=words[:].bitcast(I32))
+
+        def store(t):
+            nc.sync.dma_start(out=out_0[P * t : P * (t + 1), :], in_=window[t][:])
+
+        def regroup(t, copies, calls):
+            turned = []
+            for j in range(CHUNKS):
+                bank = turn([window[t][:, STRETCH * q + P * j : STRETCH * q + P * (j + 1)] for q in range(QUADRANTS)])
+                pairs = keep.tile([P, BANK], BF16, name="turned%d_%d" % (t, j))
+                copies[j % len(copies)](
+                    pairs[:].rearrange("c (u l e) -> c u l e", u=2, e=2), bank.rearrange("c (l u e) -> c u l e", u=2, e=2)
+                )
+                turned.append(pairs)
+            per_call = CHUNKS // calls
+            per_bank = min(per_call, 2)
+            grouped = []
+            for call in range(calls):
+                tile = shared_tile([P, per_call * P * PACK], BF16, "grouped%d_%d" % (t, call), "grouped%d_%d" % (t, call))
+                for first in range(0, per_call, per_bank):
+                    bank = next_bank("mx")
+                    for jj in range(per_bank):
+                        j = per_call * call + first + jj
+                        for u in range(2):
+                            nc.tensor.transpose(bank[:, P * (2 * jj + u) : P * (2 * jj + u + 1)], turned[j][:].bitcast(F32)[:, P * u : P * (u + 1)], ident[:])
+                    copies[call % len(copies)](
+                        tile[:].bitcast(F32)[:, 2 * P * first : 2 * P * (first + per_bank)].rearrange("p (j c u) -> p j c u", c=P, u=2),
+                        bank[:, 0 : 2 * P * per_bank].rearrange("p (j u c) -> p j c u", c=P, u=2),
+                    )
+                grouped.append(tile)
+            return grouped
+
+        def quantise_out(ts, tag, skip=0):
+            words = shared_tile([P, len(ts), STRETCH], U32, "words%d" % ts.start, tag, skip)
+            for i, t in enumerate(ts):
+                width = STRETCH // len(grouped[t])
+                for call, tile in enumerate(grouped[t]):
+                    cols = slice(width * call, width * (call + 1))
+                    nc.vector.quantize_mx(out=words[:, i, cols].bitcast(FP8X4), scales=out_scale[PACK * t : P, cols], in_=tile[:])
+            rows = words_dram[QUADRANT * ts.start : QUADRANT * ts.stop, :].rearrange("(t l) c -> l t c", l=QUADRANT)
+            for q in range(QUADRANTS):
+                queue = nc.scalar if ts.start == LAST and q % 2 == 1 else nc.sync
+                queue.dma_start(out=rows[:, :, STRETCH * q : STRETCH * (q + 1)], in_=words[QUADRANT * q : QUADRANT * (q + 1)].bitcast(I32))
+
+        everything = range(0, BLOCKS)
+
+        def y_tile(t, tag):
+            new_y[t] = shared_tile([P, T], F32, "new_y%d" % t, tag)
+
+        for t in (0, LAST, 2):
+            y_tile(t, "new_y%d" % t)
+        quantise_w(0, nc.vector.tensor_copy, "w_codes0")
+        old_mem[1] = gather(1, (everything,), "old_mem1")
+        turn_back(0, 0, read_out(0, (PIECES[0],)))
+        old_mem[0] = gather(0, PIECES, "old_mem0")
+        scatter(0, PIECES[0])
+        turn_back(0, 0, read_out(0, (range(EARLY, EARLY + HALF_BLOCKS), range(EARLY + HALF_BLOCKS, BLOCKS))))
+        quantise_w(1, nc.scalar.copy, "w_codes1")
+        old_mem[2] = gather(2, (everything,), "old_mem2")
+        made = read_out(1, (blocks(0), blocks(1)))
+        scatter(0, PIECES[1])
+        store(0)
+        quantise_w(2, nc.scalar.copy, "w_codes2")
+        y_tile(1, "w_grouped2")
+        turn_back(1, 0, made)
+        old_mem[LAST] = gather(LAST, (everything,), "old_mem3")
+        made = read_out(2, (blocks(0), blocks(1)))
+        turn_back(2, 0, made)
+        turn_back(LAST, 1, made)
+        grouped = {0: regroup(0, (nc.scalar.copy,), 1)}
+        scatter(1, everything)
+        store(1)
+        grouped[1] = regroup(1, (nc.scalar.copy,), 1)
+        scatter(2, everything)
+        store(2)
+        grouped[2] = regroup(2, (nc.scalar.copy,), 1)
+        scatter(LAST, everything)
+        store(LAST)
+        quantise_out(range(0, LAST), "new_y3")
+        grouped[LAST] = regroup(LAST, (nc.scalar.copy, nc.vector.tensor_copy), CHUNKS)
+        quantise_out(range(LAST, WINDOWS), "words3")
+
         scales_dram = out_2[0].bitcast(I32)
-        for q in range(PACK):
+        ints = STRETCH // 4
+        for q in range(QUADRANTS):
             queue = nc.scalar if q % 2 == 0 else nc.sync
-            queue.dma_start(out=scales_dram[q:SCALE_ROWS:PACK, :], in_=out_scale[q:P:QUADRANT, :].bitcast(I32))
+            queue.dma_start(out=scales_dram[:, ints * q : ints * (q + 1)], in_=out_scale[QUADRANT * q : QUADRANT * q + SCALE_ROWS, :].bitcast(I32))

@@ -249,7 +249,7 @@ def tile_picked_wema_none_lo_kernel(tc, x_words, x_scales, mem, w1, old, new, sl
                     nc.vector.quantize_mx(out=words[:, i, cols].bitcast(FP8X4), scales=out_scale[PACK * t : P, cols], in_=tile[:])
             rows = words_dram[QUADRANT * ts.start : QUADRANT * ts.stop, :].rearrange("(t l) c -> l t c", l=QUADRANT)
             for q in range(QUADRANTS):
-                queue = nc.scalar if ts.start == LAST and q % 2 == 1 else nc.sync
+                queue = nc.scalar if q >= QUADRANTS // 2 else nc.sync
                 queue.dma_start(out=rows[:, :, STRETCH * q : STRETCH * (q + 1)], in_=words[QUADRANT * q : QUADRANT * (q + 1)].bitcast(I32))
 
         everything = range(0, BLOCKS)
@@ -293,5 +293,5 @@ def tile_picked_wema_none_lo_kernel(tc, x_words, x_scales, mem, w1, old, new, sl
         scales_dram = out_2[0].bitcast(I32)
         ints = STRETCH // 4
         for q in range(QUADRANTS):
-            queue = nc.scalar if q % 2 == 0 else nc.sync
+            queue = nc.scalar if q >= QUADRANTS // 2 else nc.sync
             queue.dma_start(out=scales_dram[:, ints * q : ints * (q + 1)], in_=out_scale[QUADRANT * q : QUADRANT * q + SCALE_ROWS, :].bitcast(I32))

@@ -52,7 +52,9 @@ def tile_picked_wema_none_lo_kernel(tc, x_words, x_scales, mem, w1, old, new, sl
         psum = ctx.enter_context(tc.psum_pool(name="psum", bufs=1))
         taken = {"mx": 0, "tr": 0}
 
-        def next_bank(kind):
+        def next_bank(kind, again=None):
+            if again is not None:
+                taken[kind] = taken[kind] + (again - taken[kind]) % 4
             place = taken[kind] % 4 + (4 if kind == "tr" else 0)
             taken[kind] = taken[kind] + 1
             return psum.tile([P, BANK], F32, name="%s%d" % (kind, taken[kind]), offset=4 * BANK * place)
@@ -175,8 +177,8 @@ def tile_picked_wema_none_lo_kernel(tc, x_words, x_scales, mem, w1, old, new, sl
                 stop=(z == PASSES - 1),
             )
 
-        def turn(sources):
-            bank = next_bank("tr")
+        def turn(sources, kind="tr"):
+            bank = next_bank(kind)
             for i, source in enumerate(sources):
                 nc.tensor.transpose(bank[:, P * i : P * (i + 1)], source, ident[:])
             return bank[:, 0 : P * len(sources)]
@@ -215,20 +217,21 @@ def tile_picked_wema_none_lo_kernel(tc, x_words, x_scales, mem, w1, old, new, sl
 
         def regroup(t, copies, calls):
             turned = []
+            kinds = ("tr", "mx") if t % 2 == 0 else ("mx", "tr")
             for j in range(CHUNKS):
-                bank = turn([window[t][:, STRETCH * q + P * j : STRETCH * q + P * (j + 1)] for q in range(QUADRANTS)])
+                bank = turn([window[t][:, STRETCH * q + P * j : STRETCH * q + P * (j + 1)] for q in range(QUADRANTS)], kinds[0])
                 pairs = keep.tile([P, BANK], BF16, name="turned%d_%d" % (t, j))
                 copies[j % len(copies)](
                     pairs[:].rearrange("c (u l e) -> c u l e", u=2, e=2), bank.rearrange("c (l u e) -> c u l e", u=2, e=2)
                 )
                 turned.append(pairs)
             per_call = CHUNKS // calls
-            per_bank = min(per_call, 2)
+            per_bank = 1
             grouped = []
             for call in range(calls):
                 tile = shared_tile([P, per_call * P * PACK], BF16, "grouped%d_%d" % (t, call), "grouped%d_%d" % (t, call))
                 for first in range(0, per_call, per_bank):
-                    bank = next_bank("mx")
+                    bank = next_bank(kinds[1])
                     for jj in range(per_bank):
                         j = per_call * call + first + jj
                         for u in range(2):
@@ -238,6 +241,23 @@ def tile_picked_wema_none_lo_kernel(tc, x_words, x_scales, mem, w1, old, new, sl
                         bank[:, 0 : 2 * P * per_bank].rearrange("p (j u c) -> p j c u", c=P, u=2),
                     )
                 grouped.append(tile)
+            return grouped
+
+        def regroup_last(t):
+            act, dve = nc.scalar.copy, nc.vector.tensor_copy
+            turned = [keep.tile([P, BANK], BF16, name="turned%d_%d" % (t, j)) for j in range(CHUNKS)]
+            for j, quadrants, copy in ((0, range(0, 4), act), (1, range(0, 4), act), (2, range(0, 4), dve), (3, range(0, 2), act), (3, range(2, 4), dve)):
+                bank = turn([window[t][:, STRETCH * q + P * j : STRETCH * q + P * (j + 1)] for q in quadrants], "mx")
+                quads = slice(QUADRANT * quadrants.start, QUADRANT * quadrants.stop)
+                copy(turned[j][:].rearrange("c (u l e) -> c u l e", u=2, e=2)[:, :, quads], bank.rearrange("c (l u e) -> c u l e", u=2, e=2))
+            grouped = [keep.tile([P, 2 * P * PACK], BF16, name="grouped%d_%d" % (t, call), align_bytes=64) for call in range(2)]
+            for chunks, copy in ((range(0, 2), act), (range(2, 3), dve), (range(3, 4), act)):
+                bank = turn([turned[j][:].bitcast(F32)[:, P * u : P * (u + 1)] for j in chunks for u in range(2)], "tr")
+                first = chunks.start % 2
+                copy(
+                    grouped[chunks.start // 2][:].bitcast(F32)[:, 2 * P * first : 2 * P * (first + len(chunks))].rearrange("p (j c u) -> p j c u", c=P, u=2),
+                    bank.rearrange("p (j u c) -> p j c u", c=P, u=2),
+                )
             return grouped
 
         def quantise_out(ts, tag, skip=0):
@@ -286,9 +306,9 @@ def tile_picked_wema_none_lo_kernel(tc, x_words, x_scales, mem, w1, old, new, sl
         grouped[2] = regroup(2, (nc.scalar.copy,), 1)
         scatter(LAST, everything)
         store(LAST)
-        quantise_out(range(0, LAST), "new_y3")
-        grouped[LAST] = regroup(LAST, (nc.scalar.copy, nc.vector.tensor_copy), CHUNKS)
-        quantise_out(range(LAST, WINDOWS), "words3")
+        quantise_out(range(0, LAST), "words0")
+        grouped[LAST] = regroup_last(LAST)
+        quantise_out(range(LAST, WINDOWS), "words3", 2 * T)
 
         scales_dram = out_2[0].bitcast(I32)
         ints = STRETCH // 4

@@ -79,9 +79,9 @@ def tile_picked_wema_none_lo_kernel(tc, x_words, x_scales, mem, w1, old, new, sl
         old_cols = keep.tile([P, BLOCKS], F32, name="old_cols")
         w_raw = [[keep.tile([P, PACK, P * len(group)], F32, name="w_raw%d_%d" % (g, z)) for z in range(PASSES)] for g, group in enumerate(W_GROUPS)]
 
-        def load_w(g):
+        def load_w(g, passes=range(PASSES)):
             cols = slice(P * W_GROUPS[g].start, P * W_GROUPS[g].stop)
-            for z in range(PASSES):
+            for z in passes:
                 rows = w1[K_PASS * z : K_PASS * (z + 1), cols]
                 nc.sync.dma_start(out=w_raw[g][z][:], in_=rows.rearrange("(p i) n -> p i n", i=PACK))
 
@@ -103,9 +103,10 @@ def tile_picked_wema_none_lo_kernel(tc, x_words, x_scales, mem, w1, old, new, sl
         def load_window(t):
             nc.sync.dma_start(out=window[t][:], in_=mem[P * t : P * (t + 1), :])
 
+        load_w(0, (0,))
         nc.sync.dma_start(out=old_cols[:], in_=old[0:1, :].rearrange("o (p b) -> (o p) b", b=BLOCKS))
         nc.sync.dma_start(out=row_stage[:], in_=new[0:1, :].rearrange("o (b n) -> (o b) n", n=P))
-        load_w(0)
+        load_w(0, (1,))
         nc.sync.dma_start(offs[:], slot)
         load_window(1)
         load_x_scales(0)
@@ -250,22 +251,21 @@ def tile_picked_wema_none_lo_kernel(tc, x_words, x_scales, mem, w1, old, new, sl
                 bank = turn([window[t][:, STRETCH * q + P * j : STRETCH * q + P * (j + 1)] for q in quadrants], "mx")
                 quads = slice(QUADRANT * quadrants.start, QUADRANT * quadrants.stop)
                 copy(turned[j][:].rearrange("c (u l e) -> c u l e", u=2, e=2)[:, :, quads], bank.rearrange("c (l u e) -> c u l e", u=2, e=2))
-            grouped = [keep.tile([P, 2 * P * PACK], BF16, name="grouped%d_%d" % (t, call), align_bytes=64) for call in range(2)]
+            grouped = []
             for chunks, copy in ((range(0, 2), act), (range(2, 3), dve), (range(3, 4), act)):
                 bank = turn([turned[j][:].bitcast(F32)[:, P * u : P * (u + 1)] for j in chunks for u in range(2)], "tr")
-                first = chunks.start % 2
-                copy(
-                    grouped[chunks.start // 2][:].bitcast(F32)[:, 2 * P * first : 2 * P * (first + len(chunks))].rearrange("p (j c u) -> p j c u", c=P, u=2),
-                    bank.rearrange("p (j u c) -> p j c u", c=P, u=2),
-                )
+                tile = keep.tile([P, len(chunks) * P * PACK], BF16, name="grouped%d_%d" % (t, chunks.start), align_bytes=64)
+                copy(tile[:].bitcast(F32).rearrange("p (j c u) -> p j c u", c=P, u=2), bank.rearrange("p (j u c) -> p j c u", c=P, u=2))
+                grouped.append(tile)
             return grouped
 
         def quantise_out(ts, tag, skip=0):
             words = shared_tile([P, len(ts), STRETCH], U32, "words%d" % ts.start, tag, skip)
             for i, t in enumerate(ts):
-                width = STRETCH // len(grouped[t])
-                for call, tile in enumerate(grouped[t]):
-                    cols = slice(width * call, width * (call + 1))
+                done = 0
+                for tile in grouped[t]:
+                    cols = slice(done, done + tile.shape[1] // PACK)
+                    done = cols.stop
                     nc.vector.quantize_mx(out=words[:, i, cols].bitcast(FP8X4), scales=out_scale[PACK * t : P, cols], in_=tile[:])
             rows = words_dram[QUADRANT * ts.start : QUADRANT * ts.stop, :].rearrange("(t l) c -> l t c", l=QUADRANT)
             for q in range(QUADRANTS):

@@ -76,7 +76,7 @@ def tile_picked_wema_none_lo_kernel(tc, x_words, x_scales, mem, w1, old, new, sl
         xs_dram = x_scales.bitcast(I32)
 
         row_stage = keep.tile([BLOCKS, P], F32, name="row_stage")
-        old_cols = keep.tile([P, BLOCKS], F32, name="old_cols")
+        old_cols = shared_tile([P, BLOCKS], F32, "old_cols", "w_grouped0")
         w_raw = [[keep.tile([P, PACK, P * len(group)], F32, name="w_raw%d_%d" % (g, z)) for z in range(PASSES)] for g, group in enumerate(W_GROUPS)]
 
         def load_w(g, passes=range(PASSES)):
@@ -106,16 +106,16 @@ def tile_picked_wema_none_lo_kernel(tc, x_words, x_scales, mem, w1, old, new, sl
         load_w(0, (0,))
         nc.sync.dma_start(out=old_cols[:], in_=old[0:1, :].rearrange("o (p b) -> (o p) b", b=BLOCKS))
         nc.sync.dma_start(out=row_stage[:], in_=new[0:1, :].rearrange("o (b n) -> (o b) n", n=P))
-        load_w(0, (1,))
         nc.sync.dma_start(offs[:], slot)
         load_window(1)
         load_x_scales(0)
+        load_w(0, (1,))
+        load_window(2)
         load_x_words(0)
         load_window(0)
         load_x_words(1)
         load_x_scales(1)
         load_w(1)
-        load_window(2)
         load_w(2)
         load_window(LAST)
 
@@ -124,7 +124,7 @@ def tile_picked_wema_none_lo_kernel(tc, x_words, x_scales, mem, w1, old, new, sl
             bank = next_bank("tr")
             for i, b in enumerate(blocks(s)):
                 nc.tensor.transpose(bank[:, P * i : P * (i + 1)], old_cols[:, b : b + 1].to_broadcast([P, P]), ident[:])
-            nc.scalar.copy(
+            (nc.scalar.copy, nc.vector.tensor_copy)[s](
                 old_all[:].rearrange("m (p s i) -> m s p i", s=2, i=HALF_BLOCKS)[:, s],
                 bank[:].rearrange("m (i p) -> m p i", i=HALF_BLOCKS),
             )
@@ -155,7 +155,7 @@ def tile_picked_wema_none_lo_kernel(tc, x_words, x_scales, mem, w1, old, new, sl
             laid = grouped[:].rearrange("p (t z c k i) -> p z t c i k", z=PASSES, c=P // 4, k=4, i=PACK)
             for z in range(PASSES):
                 for i, t in enumerate(group):
-                    copy(laid[:, z, i], w_raw[g][z][:, :, P * i : P * (i + 1)].rearrange("p i (c k) -> p c i k", k=4))
+                    copy[z](laid[:, z, i], w_raw[g][z][:, :, P * i : P * (i + 1)].rearrange("p i (c k) -> p c i k", k=4))
             codes = shared_tile([P, width], U32, "w_codes%d" % g, tag)
             scales = keep.tile([P, width], U8, name="w_scales%d" % g, align_bytes=64)
             nc.vector.quantize_mx(out=codes[:].bitcast(FP8X4), scales=scales[:], in_=grouped[:])
@@ -279,20 +279,19 @@ def tile_picked_wema_none_lo_kernel(tc, x_words, x_scales, mem, w1, old, new, sl
 
         for t in (0, LAST, 2):
             y_tile(t, "new_y%d" % t)
-        quantise_w(0, nc.vector.tensor_copy, "w_codes0")
         old_mem[1] = gather(1, (everything,), "old_mem1")
+        quantise_w(0, (nc.scalar.copy, nc.scalar.copy), "w_codes0")
+        old_mem[2] = gather(2, (everything,), "old_mem2")
         turn_back(0, 0, read_out(0, (PIECES[0],)))
         old_mem[0] = gather(0, PIECES, "old_mem0")
         scatter(0, PIECES[0])
         turn_back(0, 0, read_out(0, (range(EARLY, EARLY + HALF_BLOCKS), range(EARLY + HALF_BLOCKS, BLOCKS))))
-        quantise_w(1, nc.scalar.copy, "w_codes1")
-        old_mem[2] = gather(2, (everything,), "old_mem2")
-        made = read_out(1, (blocks(0), blocks(1)))
+        quantise_w(1, (nc.scalar.copy, nc.scalar.copy), "w_codes1")
         scatter(0, PIECES[1])
         store(0)
-        quantise_w(2, nc.scalar.copy, "w_codes2")
-        y_tile(1, "w_grouped2")
-        turn_back(1, 0, made)
+        quantise_w(2, (nc.scalar.copy, nc.scalar.copy), "w_codes2")
+        y_tile(1, "new_y1")
+        turn_back(1, 0, read_out(1, (blocks(0), blocks(1))))
         old_mem[LAST] = gather(LAST, (everything,), "old_mem3")
         made = read_out(2, (blocks(0), blocks(1)))
         turn_back(2, 0, made)

@@ -23,294 +23,242 @@ PACK = 4
 K_PASS = P * PACK
 PASSES = K // K_PASS
 QUADRANT = 32
-QUADRANTS = P // QUADRANT
 SCALE_ROWS = 16
 BANK = 512
-BLOCKS = T // P
-HALF_BLOCKS = BLOCKS // 2
-HALF_T = T // 2
-WINDOWS = N // P
-LAST = WINDOWS - 1
-STRETCH = U // QUADRANTS
-CHUNKS = STRETCH // P
-EARLY = 3
-PIECES = (range(0, EARLY), range(EARLY, BLOCKS))
-W_GROUPS = (range(0, 1), range(1, 2), range(2, WINDOWS))
+HALVES = T // BANK
+LAST = PACK - 1
+KIB = 1024
+HEAD = slice(0, 384)
+TAIL = slice(384, T)
+PIECES = (HEAD, slice(384, 704), slice(704, T))
+W_VECTOR = 88
+SIDES = (slice(0, 1024), slice(1024, U))
+CHUNKS = ((slice(0, 512), slice(512, 768), slice(768, 1024)), (slice(1024, 1536), slice(1536, U)))
 
 
 def tile_picked_wema_none_lo_kernel(tc, x_words, x_scales, mem, w1, old, new, slot, out_0, out_1, out_2):
     nc = tc.nc
+    act, dve = nc.scalar.copy, nc.vector.tensor_copy
 
     def half(s):
-        return slice(HALF_T * s, HALF_T * (s + 1))
+        return slice(BANK * s, BANK * (s + 1))
 
-    def blocks(s):
-        return range(HALF_BLOCKS * s, HALF_BLOCKS * (s + 1))
+    def width(piece):
+        return piece.stop - piece.start
 
     with ExitStack() as ctx:
         keep = ctx.enter_context(tc.tile_pool(name="keep", bufs=1))
-        psum = ctx.enter_context(tc.psum_pool(name="psum", bufs=1))
-        taken = {"mx": 0, "tr": 0}
-
-        def next_bank(kind, again=None):
-            if again is not None:
-                taken[kind] = taken[kind] + (again - taken[kind]) % 4
-            place = taken[kind] % 4 + (4 if kind == "tr" else 0)
-            taken[kind] = taken[kind] + 1
-            return psum.tile([P, BANK], F32, name="%s%d" % (kind, taken[kind]), offset=4 * BANK * place)
-
         shared = ctx.enter_context(tc.tile_pool(name="shared", bufs=1))
-        places = {}
+        psum = ctx.enter_context(tc.psum_pool(name="psum", bufs=1))
 
-        def shared_tile(shape, dtype, name, tag, skip=0):
-            places.setdefault(tag, 4 * T * len(places))
-            return shared.tile(shape, dtype, name=name, offset=places[tag] + skip, align_bytes=64)
+        def bank_tile(place, name):
+            return psum.tile([P, BANK], F32, name=name, offset=4 * BANK * place)
+
+        def placed(name, kib, columns, room=None):
+            tile = shared.tile([P, room or columns], F32, name=name, offset=KIB * kib, align_bytes=64)
+            return tile[:, 0:columns]
 
         offs = keep.tile([P, T // 16], U16, name="offs")
         ident = keep.tile([P, P], F32, name="ident")
-        new_rows = keep.tile([P, P], F32, name="new_rows")
-        nc.gpsimd.memset(new_rows[:], 0.0)
         make_identity(nc, ident[:])
 
         xw_dram = x_words.bitcast(I32)
         xs_dram = x_scales.bitcast(I32)
+        mem_planes = mem.rearrange("(p r) u -> r p u", r=PACK)
+        out_planes = out_0.rearrange("(p r) u -> r p u", r=PACK)
+        old_cols = keep.tile([P, HALVES, PACK], F32, name="old_cols")
+        new_cols = keep.tile([P, HALVES, PACK], F32, name="new_cols")
+        w_raw = [keep.tile([P, PACK, N], F32, name="w_raw%d" % z) for z in range(PASSES)]
+        x_word = [keep.tile([P, PASSES, 2 * BANK], U8, name="x_word%d" % s, align_bytes=64) for s in range(HALVES)]
+        x_scale = keep.tile([P, PASSES, T], U8, name="x_scale", align_bytes=64)
+        window = [keep.tile([P, U], F32, name="window%d" % t) for t in range(PACK)]
 
-        row_stage = keep.tile([BLOCKS, P], F32, name="row_stage")
-        old_cols = shared_tile([P, BLOCKS], F32, "old_cols", "w_grouped0")
-        w_raw = [[keep.tile([P, PACK, P * len(group)], F32, name="w_raw%d_%d" % (g, z)) for z in range(PASSES)] for g, group in enumerate(W_GROUPS)]
+        def load_w(z):
+            nc.sync.dma_start(out=w_raw[z][:], in_=w1[K_PASS * z : K_PASS * (z + 1), :].rearrange("(p i) n -> p i n", i=PACK))
 
-        def load_w(g, passes=range(PASSES)):
-            cols = slice(P * W_GROUPS[g].start, P * W_GROUPS[g].stop)
-            for z in passes:
-                rows = w1[K_PASS * z : K_PASS * (z + 1), cols]
-                nc.sync.dma_start(out=w_raw[g][z][:], in_=rows.rearrange("(p i) n -> p i n", i=PACK))
+        def load_x(s):
+            ints = BANK // 2
+            nc.sync.dma_start(out=x_word[s][:].bitcast(I32), in_=xw_dram[:, :, ints * s : ints * (s + 1)].rearrange("z p c -> p z c"))
 
-        x_word = [keep.tile([P, PASSES, 2 * P * len(PIECES[s])], U8, name="x_word%d" % s, align_bytes=64) for s in range(2)]
-        x_scale = [keep.tile([P, PASSES, P * len(PIECES[s])], U8, name="x_scale%d" % s, align_bytes=64) for s in range(2)]
-        window = [keep.tile([P, U], F32, name="window%d" % t) for t in range(WINDOWS)]
+        def load_row(cols, row):
+            nc.sync.dma_start(out=cols[:], in_=row[0:1, :].rearrange("o (s p b) -> (o p) s b", p=P, b=PACK))
 
-        def load_x_words(s):
-            ints = P // 2
-            src = xw_dram[:, :, ints * PIECES[s].start : ints * PIECES[s].stop].rearrange("z p c -> p z c")
-            nc.sync.dma_start(out=x_word[s][:].bitcast(I32), in_=src)
-
-        def load_x_scales(s):
-            ints = P // 4
-            for q in range(PACK):
-                src = xs_dram[:, q:SCALE_ROWS:PACK, ints * PIECES[s].start : ints * PIECES[s].stop].rearrange("z q c -> q z c")
-                nc.sync.dma_start(out=x_scale[s][q:P:QUADRANT, :, :].bitcast(I32), in_=src)
-
-        def load_window(t):
-            nc.sync.dma_start(out=window[t][:], in_=mem[P * t : P * (t + 1), :])
-
-        load_w(0, (0,))
-        nc.sync.dma_start(out=old_cols[:], in_=old[0:1, :].rearrange("o (p b) -> (o p) b", b=BLOCKS))
-        nc.sync.dma_start(out=row_stage[:], in_=new[0:1, :].rearrange("o (b n) -> (o b) n", n=P))
+        load_row(old_cols, old)
+        load_row(new_cols, new)
+        load_w(0)
         nc.sync.dma_start(offs[:], slot)
-        load_window(1)
-        load_x_scales(0)
-        load_w(0, (1,))
-        load_window(2)
-        load_x_words(0)
-        load_window(0)
-        load_x_words(1)
-        load_x_scales(1)
+        for r in range(PACK):
+            nc.sync.dma_start(out=x_scale[r:P:QUADRANT, :, :].bitcast(I32), in_=xs_dram[:, r:SCALE_ROWS:PACK, :].rearrange("z q c -> q z c"))
         load_w(1)
-        load_w(2)
-        load_window(LAST)
+        load_x(0)
+        nc.sync.dma_start(out=window[0][:], in_=mem_planes[0])
+        load_x(1)
+        for t in range(1, PACK):
+            nc.sync.dma_start(out=window[t][:], in_=mem_planes[t])
 
         old_all = keep.tile([P, T], F32, name="old_all")
-        for s in range(2):
-            bank = next_bank("tr")
-            for i, b in enumerate(blocks(s)):
-                nc.tensor.transpose(bank[:, P * i : P * (i + 1)], old_cols[:, b : b + 1].to_broadcast([P, P]), ident[:])
-            (nc.scalar.copy, nc.vector.tensor_copy)[s](
-                old_all[:].rearrange("m (p s i) -> m s p i", s=2, i=HALF_BLOCKS)[:, s],
-                bank[:].rearrange("m (i p) -> m p i", i=HALF_BLOCKS),
-            )
-        nc.scalar.copy(new_rows[0:BLOCKS, :], row_stage[:])
-        cols_bank = next_bank("tr")
-        nc.tensor.transpose(cols_bank[:, 0:P], new_rows[:], ident[:])
-        new_cols = keep.tile([P, BLOCKS], F32, name="new_cols")
-        nc.scalar.copy(new_cols[:], cols_bank[:, 0:BLOCKS])
+        new_all = keep.tile([P, T], F32, name="new_all")
 
-        def entries(piece):
-            return slice(P * piece.start, P * piece.stop)
+        def spread(cols, whole, s, place):
+            bank = bank_tile(place, "spread%d" % place)
+            for i in range(PACK):
+                nc.tensor.transpose(bank[:, P * i : P * (i + 1)], cols[:, s, i : i + 1].to_broadcast([P, P]), ident[:])
+            act(whole[:, half(s)].rearrange("m (p i) -> m p i", i=PACK), bank[:].rearrange("m (i p) -> m p i", i=PACK))
 
-        def names(piece):
-            return offs[:, P // 16 * piece.start : P // 16 * piece.stop]
-
-        def gather(t, pieces, tag):
-            looked_up = shared_tile([P, T], F32, "old_mem%d" % t, tag)
-            for piece in pieces:
-                nc.vector.tensor_tensor(looked_up[:, entries(piece)], window[t][:].indirect(names(piece)), old_all[:, entries(piece)], MULT)
-            return looked_up
+        spread(old_cols, old_all, 0, 0)
+        spread(new_cols, new_all, 0, 1)
 
         w_mx = {}
 
-        def quantise_w(g, copy, tag):
-            group = W_GROUPS[g]
-            width = len(group) * PASSES * P
-            grouped = shared_tile([P, width * PACK], BF16, "w_grouped%d" % g, "w_grouped%d" % g)
-            laid = grouped[:].rearrange("p (t z c k i) -> p z t c i k", z=PASSES, c=P // 4, k=4, i=PACK)
-            for z in range(PASSES):
+        def quantise_w(z, shares, groups):
+            grouped = keep.tile([P, N * PACK], BF16, name="w_grouped%d" % z, align_bytes=64)
+            laid = grouped[:].rearrange("p (t m i) -> p m i t", t=PACK, i=PACK)
+            raw = w_raw[z][:].rearrange("p i (m t) -> p m i t", t=PACK)
+            for copy, ms in shares:
+                copy(laid[:, ms], raw[:, ms])
+            for group in groups:
+                cols = P * len(group)
+                codes = keep.tile([P, cols], U32, name="w_codes%d_%d" % (z, group.start), align_bytes=64)
+                scales = keep.tile([P, cols], U8, name="w_scales%d_%d" % (z, group.start), align_bytes=64)
+                nc.vector.quantize_mx(out=codes[:].bitcast(FP8X4), scales=scales[:], in_=grouped[:, K_PASS * group.start : K_PASS * group.stop])
                 for i, t in enumerate(group):
-                    copy[z](laid[:, z, i], w_raw[g][z][:, :, P * i : P * (i + 1)].rearrange("p i (c k) -> p c i k", k=4))
-            codes = shared_tile([P, width], U32, "w_codes%d" % g, tag)
-            scales = keep.tile([P, width], U8, name="w_scales%d" % g, align_bytes=64)
-            nc.vector.quantize_mx(out=codes[:].bitcast(FP8X4), scales=scales[:], in_=grouped[:])
-            for i, t in enumerate(group):
-                for z in range(PASSES):
-                    cols = slice(P * (PASSES * i + z), P * (PASSES * i + z + 1))
-                    w_mx[(t, z)] = (codes[:, cols], scales[:, cols])
+                    w_mx[(t, z)] = (codes[:, P * i : P * (i + 1)], scales[:, P * i : P * (i + 1)])
 
-        def mx_pass(out, b, t, z):
-            codes, scales = w_mx[(t, z)]
-            s = 0 if b < EARLY else 1
-            i = b - PIECES[s].start
-            nc.tensor.matmul_mx(
-                out=out,
-                lhsT=x_word[s][:, z, 2 * P * i : 2 * P * (i + 1)].bitcast(FP4X4),
-                lhsT_scale=x_scale[s][:, z, P * i : P * (i + 1)],
-                rhs=codes.bitcast(FP8X4),
-                rhs_scale=scales,
-                start=(z == 0),
-                stop=(z == PASSES - 1),
-            )
-
-        def turn(sources, kind="tr"):
-            bank = next_bank(kind)
-            for i, source in enumerate(sources):
-                nc.tensor.transpose(bank[:, P * i : P * (i + 1)], source, ident[:])
-            return bank[:, 0 : P * len(sources)]
-
-        new_y = {}
-
-        def read_out(g, runs):
-            group = W_GROUPS[g]
-            made = []
-            for run in runs:
-                y = keep.tile([P, len(run), len(group), P], F32, name="y%d_%d" % (g, run.start))
-                for j, b in enumerate(run):
-                    bank = next_bank("mx")
-                    for i, t in enumerate(group):
-                        for z in range(PASSES):
-                            mx_pass(bank[:, P * i : P * (i + 1)], b, t, z)
-                    nc.scalar.activation(y[:, j].rearrange("p t l -> p (t l)"), bank[:, 0 : P * len(group)], COPY, scale=new_cols[:, b : b + 1])
-                made.append((run, y))
-            return made
-
-        def turn_back(t, i, made):
-            if True:
-                for run, y in made:
-                    nc.scalar.copy(new_y[t][:, P * run.start : P * run.stop], turn([y[:, j, i, :] for j in range(len(run))]))
-
-        old_mem = {}
-
-        def scatter(t, piece):
-            nc.vector.tensor_tensor(window[t][:].indirect(names(piece)), old_mem[t][:, entries(piece)], new_y[t][:, entries(piece)], ADD)
-
-        out_scale = keep.tile([P, STRETCH], U8, name="out_scale", align_bytes=64)
-        words_dram = out_1[0].rearrange("p c r -> p (c r)").bitcast(I32)
-
-        def store(t):
-            nc.sync.dma_start(out=out_0[P * t : P * (t + 1), :], in_=window[t][:])
-
-        def regroup(t, copies, calls):
-            turned = []
-            kinds = ("tr", "mx") if t % 2 == 0 else ("mx", "tr")
-            for j in range(CHUNKS):
-                bank = turn([window[t][:, STRETCH * q + P * j : STRETCH * q + P * (j + 1)] for q in range(QUADRANTS)], kinds[0])
-                pairs = keep.tile([P, BANK], BF16, name="turned%d_%d" % (t, j))
-                copies[j % len(copies)](
-                    pairs[:].rearrange("c (u l e) -> c u l e", u=2, e=2), bank.rearrange("c (l u e) -> c u l e", u=2, e=2)
+        def project(t, piece, place):
+            s, first = divmod(piece.start, BANK)
+            bank = bank_tile(place, "y%d_%d" % (t, piece.start))
+            for z in range(PASSES):
+                codes, scales = w_mx[(t, z)]
+                nc.tensor.matmul_mx(
+                    out=bank[:, 0 : width(piece)],
+                    lhsT=codes.bitcast(FP8X4),
+                    lhsT_scale=scales,
+                    rhs=x_word[s][:, z, 2 * first : 2 * (first + width(piece))].bitcast(FP4X4),
+                    rhs_scale=x_scale[:, z, piece],
+                    start=(z == 0),
+                    stop=(z == PASSES - 1),
                 )
-                turned.append(pairs)
-            per_call = CHUNKS // calls
-            per_bank = 1
-            grouped = []
-            for call in range(calls):
-                tile = shared_tile([P, per_call * P * PACK], BF16, "grouped%d_%d" % (t, call), "grouped%d_%d" % (t, call))
-                for first in range(0, per_call, per_bank):
-                    bank = next_bank(kinds[1])
-                    for jj in range(per_bank):
-                        j = per_call * call + first + jj
-                        for u in range(2):
-                            nc.tensor.transpose(bank[:, P * (2 * jj + u) : P * (2 * jj + u + 1)], turned[j][:].bitcast(F32)[:, P * u : P * (u + 1)], ident[:])
-                    copies[call % len(copies)](
-                        tile[:].bitcast(F32)[:, 2 * P * first : 2 * P * (first + per_bank)].rearrange("p (j c u) -> p j c u", c=P, u=2),
-                        bank[:, 0 : 2 * P * per_bank].rearrange("p (j u c) -> p j c u", c=P, u=2),
-                    )
-                grouped.append(tile)
-            return grouped
+            return bank[:, 0 : width(piece)]
 
-        def regroup_last(t):
-            act, dve = nc.scalar.copy, nc.vector.tensor_copy
-            turned = [keep.tile([P, BANK], BF16, name="turned%d_%d" % (t, j)) for j in range(CHUNKS)]
-            for j, quadrants, copy in ((0, range(0, 4), act), (1, range(0, 4), act), (2, range(0, 4), dve), (3, range(0, 2), act), (3, range(2, 4), dve)):
-                bank = turn([window[t][:, STRETCH * q + P * j : STRETCH * q + P * (j + 1)] for q in quadrants], "mx")
-                quads = slice(QUADRANT * quadrants.start, QUADRANT * quadrants.stop)
-                copy(turned[j][:].rearrange("c (u l e) -> c u l e", u=2, e=2)[:, :, quads], bank.rearrange("c (l u e) -> c u l e", u=2, e=2))
-            grouped = []
-            for chunks, copy in ((range(0, 2), act), (range(2, 3), dve), (range(3, 4), act)):
-                bank = turn([turned[j][:].bitcast(F32)[:, P * u : P * (u + 1)] for j in chunks for u in range(2)], "tr")
-                tile = keep.tile([P, len(chunks) * P * PACK], BF16, name="grouped%d_%d" % (t, chunks.start), align_bytes=64)
-                copy(tile[:].bitcast(F32).rearrange("p (j c u) -> p j c u", c=P, u=2), bank.rearrange("p (j u c) -> p j c u", c=P, u=2))
-                grouped.append(tile)
-            return grouped
+        def names(piece):
+            return offs[:, piece.start // 16 : piece.stop // 16]
 
-        def quantise_out(ts, tag, skip=0):
-            words = shared_tile([P, len(ts), STRETCH], U32, "words%d" % ts.start, tag, skip)
-            for i, t in enumerate(ts):
-                done = 0
-                for tile in grouped[t]:
-                    cols = slice(done, done + tile.shape[1] // PACK)
-                    done = cols.stop
-                    nc.vector.quantize_mx(out=words[:, i, cols].bitcast(FP8X4), scales=out_scale[PACK * t : P, cols], in_=tile[:])
-            rows = words_dram[QUADRANT * ts.start : QUADRANT * ts.stop, :].rearrange("(t l) c -> l t c", l=QUADRANT)
-            for q in range(QUADRANTS):
-                queue = nc.scalar if q >= QUADRANTS // 2 else nc.sync
-                queue.dma_start(out=rows[:, :, STRETCH * q : STRETCH * (q + 1)], in_=words[QUADRANT * q : QUADRANT * (q + 1)].bitcast(I32))
+        def weigh(into, piece, bank):
+            nc.vector.tensor_tensor(into, bank, new_all[:, piece], MULT)
 
-        everything = range(0, BLOCKS)
+        def gather(into, t, piece):
+            nc.vector.tensor_tensor(into, window[t][:].indirect(names(piece)), old_all[:, piece], MULT)
 
-        def y_tile(t, tag):
-            new_y[t] = shared_tile([P, T], F32, "new_y%d" % t, tag)
+        def mix(into, kept, weighed):
+            nc.vector.tensor_tensor(into, kept, weighed, ADD)
 
-        for t in (0, LAST, 2):
-            y_tile(t, "new_y%d" % t)
-        old_mem[1] = gather(1, (everything,), "old_mem1")
-        quantise_w(0, (nc.scalar.copy, nc.scalar.copy), "w_codes0")
-        old_mem[2] = gather(2, (everything,), "old_mem2")
-        turn_back(0, 0, read_out(0, (PIECES[0],)))
-        old_mem[0] = gather(0, PIECES, "old_mem0")
-        scatter(0, PIECES[0])
-        turn_back(0, 0, read_out(0, (range(EARLY, EARLY + HALF_BLOCKS), range(EARLY + HALF_BLOCKS, BLOCKS))))
-        quantise_w(1, (nc.scalar.copy, nc.scalar.copy), "w_codes1")
-        scatter(0, PIECES[1])
-        store(0)
-        quantise_w(2, (nc.scalar.copy, nc.scalar.copy), "w_codes2")
-        y_tile(1, "new_y1")
-        turn_back(1, 0, read_out(1, (blocks(0), blocks(1))))
-        old_mem[LAST] = gather(LAST, (everything,), "old_mem3")
-        made = read_out(2, (blocks(0), blocks(1)))
-        turn_back(2, 0, made)
-        turn_back(LAST, 1, made)
-        grouped = {0: regroup(0, (nc.scalar.copy,), 1)}
-        scatter(1, everything)
-        store(1)
-        grouped[1] = regroup(1, (nc.scalar.copy,), 1)
-        scatter(2, everything)
-        store(2)
-        grouped[2] = regroup(2, (nc.scalar.copy,), 1)
-        scatter(LAST, everything)
-        store(LAST)
-        quantise_out(range(0, LAST), "words0")
-        grouped[LAST] = regroup_last(LAST)
-        quantise_out(range(LAST, WINDOWS), "words3", 2 * T)
+        def scatter(t, piece, total):
+            nc.scalar.activation(window[t][:].indirect(names(piece)), total, COPY)
 
+        quantise_w(0, ((dve, slice(0, P)),), (range(0, PACK),))
+        quantise_w(1, ((dve, slice(0, W_VECTOR)), (act, slice(W_VECTOR, P))), (range(0, 1), range(1, PACK)))
+
+        spread(new_cols, new_all, 1, 2)
+        spread(old_cols, old_all, 1, 3)
+
+        front, middle, back = PIECES
+
+        def within(piece, whole):
+            return slice(piece.start - whole.start, piece.stop - whole.start)
+
+        def finish(t, kib, kept, weighed):
+            total = placed("back%d" % t, kib, width(back))
+            mix(total, kept, weighed)
+            scatter(t, back, total)
+            nc.scalar.dma_start(out=out_planes[t], in_=window[t][:])
+
+        lower = placed("lower_y0", 0, BANK, 10 * KIB // 4)
+        for i in range(2):
+            quarter = slice(BANK // 2 * i, BANK // 2 * (i + 1))
+            weigh(lower[:, quarter], quarter, project(0, quarter, i))
+        first = placed("first", 40, width(front), 6 * KIB // 4)
+        gather(first, 0, front)
+        plain = keep.tile([P, width(TAIL)], F32, name="plain")
+        nc.scalar.activation(plain[:], window[0][:].indirect(names(TAIL)), COPY)
+        total = keep.tile([P, width(front)], F32, name="front0")
+        mix(total[:], first, lower[:, front])
+        scatter(0, front, total[:])
+        rest = placed("old_rest0", 44, width(TAIL), 10 * KIB // 4)
+        nc.vector.tensor_tensor(rest, plain[:], old_all[:, TAIL], MULT)
+        upper = placed("upper_y0", 42, BANK)
+        weigh(upper, half(1), project(0, half(1), 0))
+        total = keep.tile([P, width(middle)], F32, name="middle0")
+        rim = BANK - middle.start
+        mix(total[:, 0:rim], rest[:, 0:rim], lower[:, middle.start : BANK])
+        mix(total[:, rim:], rest[:, rim : width(middle)], upper[:, 0 : middle.stop - BANK])
+        scatter(0, middle, total[:])
+        behind = (rest[:, within(back, TAIL)], upper[:, within(back, half(1))])
+
+        for t, base in ((1, 2), (2, 47)):
+            weighed = placed("new_y%d" % t, base, T)
+            weigh(weighed[:, half(0)], half(0), project(t, half(0), 1))
+            first = placed("old_front%d" % t, base + 4, width(front))
+            gather(first, t, front)
+            rest = placed("old_rest%d" % t, base + 6, width(TAIL), (22, 3)[t - 1] * KIB // 4)
+            gather(rest, t, TAIL)
+            total = keep.tile([P, width(front)], F32, name="front%d" % t)
+            mix(total[:], first, weighed[:, front])
+            scatter(t, front, total[:])
+            weigh(weighed[:, half(1)], half(1), project(t, half(1), 0))
+            finish(t - 1, base + 4, *behind)
+            total = keep.tile([P, width(middle)], F32, name="middle%d" % t)
+            mix(total[:], rest[:, within(middle, TAIL)], weighed[:, middle])
+            scatter(t, middle, total[:])
+            behind = (rest[:, within(back, TAIL)], weighed[:, back])
+
+        pairs = {}
+
+        def round_plane(t, side, copy, both=False):
+            if side not in pairs:
+                pairs[side] = shared.tile([P, 2, width(SIDES[side]), 2], BF16, name="pairs%d" % side, offset=KIB * (20 + 9 * side), align_bytes=64)
+            source = window[t][:, SIDES[side]]
+            if both:
+                copy(pairs[side][:, t // 2], source.unsqueeze(2).to_broadcast([P, width(SIDES[side]), 2]))
+            else:
+                copy(pairs[side][:, t // 2, :, t % 2], source)
+
+        weighed = placed("new_y3", 11, T)
+        for s in range(HALVES):
+            weigh(weighed[:, half(s)], half(s), project(LAST, half(s), 1 - s))
+        rest = placed("old_rest3", 17, width(TAIL))
+        gather(rest, LAST, TAIL)
+        first = placed("old_front3", 15, width(front))
+        gather(first, LAST, front)
+        total = keep.tile([P, width(middle)], F32, name="middle3")
+        mix(total[:], rest[:, within(middle, TAIL)], weighed[:, middle])
+        nc.vector.tensor_tensor(window[LAST][:].indirect(names(front)), first, weighed[:, front], ADD)
+        scatter(LAST, middle, total[:])
+        round_plane(0, 0, dve)
+        finish(2, 15, *behind)
+        finish(LAST, 60, rest[:, within(back, TAIL)], weighed[:, back])
+        round_plane(0, 1, dve)
+        for side in range(2):
+            round_plane(1, side, dve)
+        round_plane(2, 0, dve, both=True)
+        round_plane(2, 1, dve)
+        round_plane(LAST, 0, act)
+        round_plane(LAST, 1, dve)
+
+        out_scale = keep.tile([P, U], U8, name="out_scale", align_bytes=64)
+        words_dram = out_1[0].rearrange("p c r -> p (c r)").bitcast(I32)
+        grouped = {}
+        for side, copy in ((1, dve), (0, act)):
+            words = pairs[side][:].rearrange("p u c e -> p u (c e)").bitcast(F32)
+            for chunk in CHUNKS[side]:
+                tile = keep.tile([P, width(chunk) * PACK], BF16, name="grouped%d" % chunk.start, align_bytes=64)
+                part = words[:, :, chunk.start - SIDES[side].start : chunk.stop - SIDES[side].start]
+                copy(tile[:].bitcast(F32).rearrange("p (c u) -> p c u", u=2), part.rearrange("p u c -> p c u"))
+                grouped[chunk.start] = tile
+        for chunk in CHUNKS[1] + CHUNKS[0]:
+            codes = keep.tile([P, width(chunk)], U32, name="codes%d" % chunk.start, align_bytes=64)
+            nc.vector.quantize_mx(out=codes[:].bitcast(FP8X4), scales=out_scale[:, chunk], in_=grouped[chunk.start][:])
+            nc.sync.dma_start(out=words_dram[:, chunk], in_=codes[:].bitcast(I32))
         scales_dram = out_2[0].bitcast(I32)
-        ints = STRETCH // 4
-        for q in range(QUADRANTS):
-            queue = nc.scalar if q >= QUADRANTS // 2 else nc.sync
-            queue.dma_start(out=scales_dram[:, ints * q : ints * (q + 1)], in_=out_scale[QUADRANT * q : QUADRANT * q + SCALE_ROWS, :].bitcast(I32))
+        for r in range(PACK):
+            queue = nc.scalar if r >= PACK // 2 else nc.sync
+            queue.dma_start(out=scales_dram[r:SCALE_ROWS:PACK, :], in_=out_scale[r:P:QUADRANT, :].bitcast(I32))

@@ -31,6 +31,7 @@ KIB = 1024
 HEAD = slice(0, 384)
 TAIL = slice(384, T)
 PIECES = (HEAD, slice(384, 704), slice(704, T))
+LAST_PIECES = (slice(0, 512), slice(512, 768), slice(768, T))
 W_VECTOR = 88
 SIDES = (slice(0, 1024), slice(1024, U))
 CHUNKS = ((slice(0, 512), slice(512, 768), slice(768, 1024)), (slice(1024, 1536), slice(1536, U)))
@@ -55,7 +56,7 @@ def tile_picked_wema_none_lo_kernel(tc, x_words, x_scales, mem, w1, old, new, sl
             return psum.tile([P, BANK], F32, name=name, offset=4 * BANK * place)
 
         def placed(name, kib, columns, room=None):
-            tile = shared.tile([P, room or columns], F32, name=name, offset=KIB * kib, align_bytes=64)
+            tile = shared.tile([P, room or columns], F32, name=name, offset=int(KIB * kib), align_bytes=64)
             return tile[:, 0:columns]
 
         offs = keep.tile([P, T // 16], U16, name="offs")
@@ -84,8 +85,8 @@ def tile_picked_wema_none_lo_kernel(tc, x_words, x_scales, mem, w1, old, new, sl
             nc.sync.dma_start(out=cols[:], in_=row[0:1, :].rearrange("o (s p b) -> (o p) s b", p=P, b=PACK))
 
         load_row(old_cols, old)
-        load_row(new_cols, new)
         load_w(0)
+        load_row(new_cols, new)
         nc.sync.dma_start(offs[:], slot)
         for r in range(PACK):
             nc.sync.dma_start(out=x_scale[r:P:QUADRANT, :, :].bitcast(I32), in_=xs_dram[:, r:SCALE_ROWS:PACK, :].rearrange("z q c -> q z c"))
@@ -105,8 +106,10 @@ def tile_picked_wema_none_lo_kernel(tc, x_words, x_scales, mem, w1, old, new, sl
                 nc.tensor.transpose(bank[:, P * i : P * (i + 1)], cols[:, s, i : i + 1].to_broadcast([P, P]), ident[:])
             act(whole[:, half(s)].rearrange("m (p i) -> m p i", i=PACK), bank[:].rearrange("m (i p) -> m p i", i=PACK))
 
-        spread(old_cols, old_all, 0, 0)
-        spread(new_cols, new_all, 0, 1)
+        spread(old_cols, old_all, 0, 2)
+        spread(old_cols, old_all, 1, 3)
+        spread(new_cols, new_all, 0, 0)
+        spread(new_cols, new_all, 1, 1)
 
         w_mx = {}
 
@@ -158,84 +161,85 @@ def tile_picked_wema_none_lo_kernel(tc, x_words, x_scales, mem, w1, old, new, sl
         quantise_w(0, ((dve, slice(0, P)),), (range(0, PACK),))
         quantise_w(1, ((dve, slice(0, W_VECTOR)), (act, slice(W_VECTOR, P))), (range(0, 1), range(1, PACK)))
 
-        spread(new_cols, new_all, 1, 2)
-        spread(old_cols, old_all, 1, 3)
-
         front, middle, back = PIECES
 
         def within(piece, whole):
             return slice(piece.start - whole.start, piece.stop - whole.start)
 
-        def finish(t, kib, kept, weighed):
-            total = placed("back%d" % t, kib, width(back))
-            mix(total, kept, weighed)
-            scatter(t, back, total)
-            nc.scalar.dma_start(out=out_planes[t], in_=window[t][:])
+        def finish(t, kib, piece, engine, kept, weighed):
+            total = placed("back%d" % t, kib, width(piece))
+            engine.tensor_tensor(total, kept, weighed, ADD)
+            scatter(t, piece, total)
+            nc.sync.dma_start(out=out_planes[t], in_=window[t][:])
 
-        lower = placed("lower_y0", 0, BANK, 10 * KIB // 4)
+        lower = placed("lower_y0", 30, BANK, 5 * KIB // 4)
         for i in range(2):
             quarter = slice(BANK // 2 * i, BANK // 2 * (i + 1))
             weigh(lower[:, quarter], quarter, project(0, quarter, i))
-        first = placed("first", 40, width(front), 6 * KIB // 4)
+        first = placed("first", 0, width(front), 11 * KIB // 4)
         gather(first, 0, front)
         plain = keep.tile([P, width(TAIL)], F32, name="plain")
         nc.scalar.activation(plain[:], window[0][:].indirect(names(TAIL)), COPY)
         total = keep.tile([P, width(front)], F32, name="front0")
         mix(total[:], first, lower[:, front])
         scatter(0, front, total[:])
-        rest = placed("old_rest0", 44, width(TAIL), 10 * KIB // 4)
-        nc.vector.tensor_tensor(rest, plain[:], old_all[:, TAIL], MULT)
-        upper = placed("upper_y0", 42, BANK)
+        rest = placed("old_rest0", 8, width(TAIL), 12 * KIB // 4)
+        nc.gpsimd.tensor_tensor(rest, plain[:], old_all[:, TAIL], MULT)
+        upper = placed("upper_y0", 2, BANK)
         weigh(upper, half(1), project(0, half(1), 0))
-        total = keep.tile([P, width(middle)], F32, name="middle0")
-        rim = BANK - middle.start
-        mix(total[:, 0:rim], rest[:, 0:rim], lower[:, middle.start : BANK])
-        mix(total[:, rim:], rest[:, rim : width(middle)], upper[:, 0 : middle.stop - BANK])
-        scatter(0, middle, total[:])
-        behind = (rest[:, within(back, TAIL)], upper[:, within(back, half(1))])
+        weighed = placed("new_y1", 4, T)
+        weigh(weighed[:, half(0)], half(0), project(1, half(0), 1))
+        second, ending = slice(front.stop, 2 * front.stop), slice(2 * front.stop, T)
+        total = keep.tile([P, width(second)], F32, name="middle0")
+        rim = BANK - second.start
+        mix(total[:, 0:rim], rest[:, 0:rim], lower[:, second.start : BANK])
+        mix(total[:, rim:], rest[:, rim : width(second)], upper[:, 0 : second.stop - BANK])
+        scatter(0, second, total[:])
+        behind = (rest[:, within(ending, TAIL)], upper[:, within(ending, half(1))])
 
-        for t, base in ((1, 2), (2, 47)):
-            weighed = placed("new_y%d" % t, base, T)
-            weigh(weighed[:, half(0)], half(0), project(t, half(0), 1))
-            first = placed("old_front%d" % t, base + 4, width(front))
+        for t, at_front, at_rest, room in ((1, 24, 32, 22), (2, 14, 11, 3)):
+            first = placed("old_front%d" % t, at_front, width(front), (13 if t == 1 else 12) * KIB // 8)
             gather(first, t, front)
-            rest = placed("old_rest%d" % t, base + 6, width(TAIL), (22, 3)[t - 1] * KIB // 4)
+            rest = placed("old_rest%d" % t, at_rest, width(TAIL), room * KIB // 4)
             gather(rest, t, TAIL)
             total = keep.tile([P, width(front)], F32, name="front%d" % t)
             mix(total[:], first, weighed[:, front])
             scatter(t, front, total[:])
+            finish(t - 1, at_front, ending if t == 1 else back, nc.gpsimd, *behind)
             weigh(weighed[:, half(1)], half(1), project(t, half(1), 0))
-            finish(t - 1, base + 4, *behind)
+            coming = placed("new_y%d" % (t + 1), at_front + 2, T)
+            weigh(coming[:, half(0)], half(0), project(t + 1, half(0), 1))
             total = keep.tile([P, width(middle)], F32, name="middle%d" % t)
             mix(total[:], rest[:, within(middle, TAIL)], weighed[:, middle])
             scatter(t, middle, total[:])
             behind = (rest[:, within(back, TAIL)], weighed[:, back])
+            weighed = coming
 
         pairs = {}
 
         def round_plane(t, side, copy, both=False):
             if side not in pairs:
-                pairs[side] = shared.tile([P, 2, width(SIDES[side]), 2], BF16, name="pairs%d" % side, offset=KIB * (20 + 9 * side), align_bytes=64)
+                pairs[side] = shared.tile([P, 2, width(SIDES[side]), 2], BF16, name="pairs%d" % side, offset=KIB * (40 + 8 * side), align_bytes=64)
             source = window[t][:, SIDES[side]]
             if both:
                 copy(pairs[side][:, t // 2], source.unsqueeze(2).to_broadcast([P, width(SIDES[side]), 2]))
             else:
                 copy(pairs[side][:, t // 2, :, t % 2], source)
 
-        weighed = placed("new_y3", 11, T)
-        for s in range(HALVES):
-            weigh(weighed[:, half(s)], half(s), project(LAST, half(s), 1 - s))
-        rest = placed("old_rest3", 17, width(TAIL))
-        gather(rest, LAST, TAIL)
-        first = placed("old_front3", 15, width(front))
-        gather(first, LAST, front)
-        total = keep.tile([P, width(middle)], F32, name="middle3")
-        mix(total[:], rest[:, within(middle, TAIL)], weighed[:, middle])
-        nc.vector.tensor_tensor(window[LAST][:].indirect(names(front)), first, weighed[:, front], ADD)
-        scatter(LAST, middle, total[:])
+        own, third, fourth = LAST_PIECES
+        others = slice(own.stop, T)
+        weigh(weighed[:, half(1)], half(1), project(LAST, half(1), 0))
+        rest = placed("old_rest3", 37.5, width(others))
+        gather(rest, LAST, others)
+        first = placed("old_front3", 35, width(own))
+        gather(first, LAST, own)
+        total = keep.tile([P, width(third)], F32, name="middle3")
+        mix(total[:], rest[:, within(third, others)], weighed[:, third])
+        nc.vector.tensor_tensor(window[LAST][:].indirect(names(own)), first, weighed[:, own], ADD)
+        scatter(LAST, third, total[:])
         round_plane(0, 0, dve)
-        finish(2, 15, *behind)
-        finish(LAST, 60, rest[:, within(back, TAIL)], weighed[:, back])
+        finish(2, 35, back, nc.vector, *behind)
+        finish(LAST, 60, fourth, nc.vector, rest[:, within(fourth, others)], weighed[:, fourth])
         round_plane(0, 1, dve)
         for side in range(2):
             round_plane(1, side, dve)

@@ -31,10 +31,10 @@ KIB = 1024
 HEAD = slice(0, 384)
 TAIL = slice(384, T)
 PIECES = (HEAD, slice(384, 704), slice(704, T))
-LAST_PIECES = (slice(0, 512), slice(512, 768), slice(768, T))
+LAST_PIECES = (slice(0, 640), slice(640, T))
 W_VECTOR = 88
-SIDES = (slice(0, 1024), slice(1024, U))
-CHUNKS = ((slice(0, 512), slice(512, 768), slice(768, 1024)), (slice(1024, 1536), slice(1536, U)))
+SIDES = (slice(0, 1152), slice(1152, U))
+CHUNKS = ((slice(0, 512), slice(512, 896), slice(896, 1152)), (slice(1152, 1664), slice(1664, U)))
 
 
 def tile_picked_wema_none_lo_kernel(tc, x_words, x_scales, mem, w1, old, new, slot, out_0, out_1, out_2):
@@ -197,7 +197,7 @@ def tile_picked_wema_none_lo_kernel(tc, x_words, x_scales, mem, w1, old, new, sl
         scatter(0, second, total[:])
         behind = (rest[:, within(ending, TAIL)], upper[:, within(ending, half(1))])
 
-        for t, at_front, at_rest, room in ((1, 24, 32, 22), (2, 14, 11, 3)):
+        for t, at_front, at_rest, room in ((1, 24, 32, 26), (2, 14, 11, 3)):
             first = placed("old_front%d" % t, at_front, width(front), (13 if t == 1 else 12) * KIB // 8)
             gather(first, t, front)
             rest = placed("old_rest%d" % t, at_rest, width(TAIL), room * KIB // 4)
@@ -209,41 +209,51 @@ def tile_picked_wema_none_lo_kernel(tc, x_words, x_scales, mem, w1, old, new, sl
             weigh(weighed[:, half(1)], half(1), project(t, half(1), 0))
             coming = placed("new_y%d" % (t + 1), at_front + 2, T)
             weigh(coming[:, half(0)], half(0), project(t + 1, half(0), 1))
-            total = keep.tile([P, width(middle)], F32, name="middle%d" % t)
-            mix(total[:], rest[:, within(middle, TAIL)], weighed[:, middle])
-            scatter(t, middle, total[:])
-            behind = (rest[:, within(back, TAIL)], weighed[:, back])
+            if t == 1:
+                total = keep.tile([P, width(middle)], F32, name="middle%d" % t)
+                mix(total[:], rest[:, within(middle, TAIL)], weighed[:, middle])
+                scatter(t, middle, total[:])
+                behind = (rest[:, within(back, TAIL)], weighed[:, back])
+            else:
+                total = keep.tile([P, width(TAIL)], F32, name="tail%d" % t)
+                mix(total[:], rest, weighed[:, TAIL])
+                for piece in (middle, back):
+                    scatter(t, piece, total[:, within(piece, TAIL)])
+                nc.sync.dma_start(out=out_planes[t], in_=window[t][:])
             weighed = coming
 
         pairs = {}
 
-        def round_plane(t, side, copy, both=False):
+        def round_plane(t, side, copy, edge=0):
             if side not in pairs:
-                pairs[side] = shared.tile([P, 2, width(SIDES[side]), 2], BF16, name="pairs%d" % side, offset=KIB * (40 + 8 * side), align_bytes=64)
+                pairs[side] = shared.tile([P, 2, width(SIDES[side]), 2], BF16, name="pairs%d" % side, offset=KIB * (40, 62)[side], align_bytes=64)
             source = window[t][:, SIDES[side]]
-            if both:
-                copy(pairs[side][:, t // 2], source.unsqueeze(2).to_broadcast([P, width(SIDES[side]), 2]))
-            else:
-                copy(pairs[side][:, t // 2, :, t % 2], source)
+            copy(pairs[side][:, t // 2, edge:, t % 2], source[:, edge:])
+            if edge:
+                copy(pairs[side][:, t // 2, 0:edge], source[:, 0:edge].unsqueeze(2).to_broadcast([P, edge, 2]))
 
-        own, third, fourth = LAST_PIECES
-        others = slice(own.stop, T)
+        own, others = LAST_PIECES
         weigh(weighed[:, half(1)], half(1), project(LAST, half(1), 0))
-        rest = placed("old_rest3", 37.5, width(others))
-        gather(rest, LAST, others)
-        first = placed("old_front3", 35, width(own))
+        first = placed("old_front3", 35, width(own), 6 * KIB // 4)
         gather(first, LAST, own)
-        total = keep.tile([P, width(third)], F32, name="middle3")
-        mix(total[:], rest[:, within(third, others)], weighed[:, third])
-        nc.vector.tensor_tensor(window[LAST][:].indirect(names(own)), first, weighed[:, own], ADD)
-        scatter(LAST, third, total[:])
-        round_plane(0, 0, dve)
-        finish(2, 35, back, nc.vector, *behind)
-        finish(LAST, 60, fourth, nc.vector, rest[:, within(fourth, others)], weighed[:, fourth])
-        round_plane(0, 1, dve)
-        for side in range(2):
-            round_plane(1, side, dve)
-        round_plane(2, 0, dve, both=True)
+        rest = placed("old_rest3", 57, width(others))
+        gather(rest, LAST, others)
+        mine = placed("front3", 60, width(own))
+        mix(mine, first, weighed[:, own])
+        total = keep.tile([P, width(others)], F32, name="back3")
+        mix(total[:], rest, weighed[:, others])
+        nc.vector.tensor_copy(window[LAST][:].indirect(names(own)), mine)
+        scatter(LAST, others, total[:])
+        nc.sync.dma_start(out=out_planes[LAST], in_=window[LAST][:])
+
+        def pool_round(out, source):
+            nc.gpsimd.tensor_scalar(out, source, 1.0, 0.0, MULT, ADD)
+
+        for t in range(2):
+            round_plane(t, 0, pool_round)
+        for t in range(2):
+            round_plane(t, 1, dve)
+        round_plane(2, 0, dve, edge=4)
         round_plane(2, 1, dve)
         round_plane(LAST, 0, act)
         round_plane(LAST, 1, dve)

@@ -31,10 +31,10 @@ KIB = 1024
 HEAD = slice(0, 384)
 TAIL = slice(384, T)
 PIECES = (HEAD, slice(384, 704), slice(704, T))
-LAST_PIECES = (slice(0, 640), slice(640, T))
+LAST_PIECES = (slice(0, 704), slice(704, T))
 W_VECTOR = 88
-SIDES = (slice(0, 1152), slice(1152, U))
-CHUNKS = ((slice(0, 512), slice(512, 896), slice(896, 1152)), (slice(1152, 1664), slice(1664, U)))
+SIDES = (slice(0, 1024), slice(1024, U))
+CHUNKS = ((slice(0, 512), slice(512, 768), slice(768, 1024)), (slice(1024, 1536), slice(1536, U)))
 
 
 def tile_picked_wema_none_lo_kernel(tc, x_words, x_scales, mem, w1, old, new, slot, out_0, out_1, out_2):
@@ -106,8 +106,8 @@ def tile_picked_wema_none_lo_kernel(tc, x_words, x_scales, mem, w1, old, new, sl
                 nc.tensor.transpose(bank[:, P * i : P * (i + 1)], cols[:, s, i : i + 1].to_broadcast([P, P]), ident[:])
             act(whole[:, half(s)].rearrange("m (p i) -> m p i", i=PACK), bank[:].rearrange("m (i p) -> m p i", i=PACK))
 
-        spread(old_cols, old_all, 0, 2)
-        spread(old_cols, old_all, 1, 3)
+        spread(old_cols, old_all, 0, 3)
+        spread(old_cols, old_all, 1, 2)
         spread(new_cols, new_all, 0, 0)
         spread(new_cols, new_all, 1, 1)
 
@@ -173,11 +173,13 @@ def tile_picked_wema_none_lo_kernel(tc, x_words, x_scales, mem, w1, old, new, sl
             nc.sync.dma_start(out=out_planes[t], in_=window[t][:])
 
         lower = placed("lower_y0", 30, BANK, 5 * KIB // 4)
+        parts = (slice(0, 2 * P), slice(2 * P, front.stop), slice(front.stop, BANK))
+        banks = [project(0, part, i) for i, part in enumerate(parts)]
         for i in range(2):
-            quarter = slice(BANK // 2 * i, BANK // 2 * (i + 1))
-            weigh(lower[:, quarter], quarter, project(0, quarter, i))
+            weigh(lower[:, parts[i]], parts[i], banks[i])
         first = placed("first", 0, width(front), 11 * KIB // 4)
         gather(first, 0, front)
+        weigh(lower[:, parts[2]], parts[2], banks[2])
         plain = keep.tile([P, width(TAIL)], F32, name="plain")
         nc.scalar.activation(plain[:], window[0][:].indirect(names(TAIL)), COPY)
         total = keep.tile([P, width(front)], F32, name="front0")
@@ -186,9 +188,10 @@ def tile_picked_wema_none_lo_kernel(tc, x_words, x_scales, mem, w1, old, new, sl
         rest = placed("old_rest0", 8, width(TAIL), 12 * KIB // 4)
         nc.gpsimd.tensor_tensor(rest, plain[:], old_all[:, TAIL], MULT)
         upper = placed("upper_y0", 2, BANK)
-        weigh(upper, half(1), project(0, half(1), 0))
         weighed = placed("new_y1", 4, T)
         weigh(weighed[:, half(0)], half(0), project(1, half(0), 1))
+        weigh(upper, half(1), project(0, half(1), 0))
+        weigh(weighed[:, half(1)], half(1), project(1, half(1), 2))
         second, ending = slice(front.stop, 2 * front.stop), slice(2 * front.stop, T)
         total = keep.tile([P, width(second)], F32, name="middle0")
         rim = BANK - second.start
@@ -206,9 +209,9 @@ def tile_picked_wema_none_lo_kernel(tc, x_words, x_scales, mem, w1, old, new, sl
             mix(total[:], first, weighed[:, front])
             scatter(t, front, total[:])
             finish(t - 1, at_front, ending if t == 1 else back, nc.gpsimd, *behind)
-            weigh(weighed[:, half(1)], half(1), project(t, half(1), 0))
             coming = placed("new_y%d" % (t + 1), at_front + 2, T)
-            weigh(coming[:, half(0)], half(0), project(t + 1, half(0), 1))
+            for s in range(HALVES):
+                weigh(coming[:, half(s)], half(s), project(t + 1, half(s), (2 * t + 2 + s) % 3))
             if t == 1:
                 total = keep.tile([P, width(middle)], F32, name="middle%d" % t)
                 mix(total[:], rest[:, within(middle, TAIL)], weighed[:, middle])
@@ -226,24 +229,23 @@ def tile_picked_wema_none_lo_kernel(tc, x_words, x_scales, mem, w1, old, new, sl
 
         def round_plane(t, side, copy, edge=0):
             if side not in pairs:
-                pairs[side] = shared.tile([P, 2, width(SIDES[side]), 2], BF16, name="pairs%d" % side, offset=KIB * (40, 62)[side], align_bytes=64)
+                pairs[side] = shared.tile([P, 2, width(SIDES[side]), 2], BF16, name="pairs%d" % side, offset=KIB * (40 + 9 * side), align_bytes=64)
             source = window[t][:, SIDES[side]]
             copy(pairs[side][:, t // 2, edge:, t % 2], source[:, edge:])
             if edge:
                 copy(pairs[side][:, t // 2, 0:edge], source[:, 0:edge].unsqueeze(2).to_broadcast([P, edge, 2]))
 
         own, others = LAST_PIECES
-        weigh(weighed[:, half(1)], half(1), project(LAST, half(1), 0))
-        first = placed("old_front3", 35, width(own), 6 * KIB // 4)
+        first = placed("old_front3", 35, width(own), 15 * KIB // 4)
         gather(first, LAST, own)
         rest = placed("old_rest3", 57, width(others))
         gather(rest, LAST, others)
-        mine = placed("front3", 60, width(own))
+        mine = placed("front3", 59.5, width(own))
         mix(mine, first, weighed[:, own])
-        total = keep.tile([P, width(others)], F32, name="back3")
-        mix(total[:], rest, weighed[:, others])
+        total = placed("back3", 38, width(others))
+        nc.gpsimd.tensor_tensor(total, rest, weighed[:, others], ADD)
         nc.vector.tensor_copy(window[LAST][:].indirect(names(own)), mine)
-        scatter(LAST, others, total[:])
+        scatter(LAST, others, total)
         nc.sync.dma_start(out=out_planes[LAST], in_=window[LAST][:])
 
         def pool_round(out, source):

@@ -242,10 +242,10 @@ def tile_picked_wema_none_lo_kernel(tc, x_words, x_scales, mem, w1, old, new, sl
         gather(rest, LAST, others)
         mine = placed("front3", 59.5, width(own))
         mix(mine, first, weighed[:, own])
-        total = placed("back3", 38, width(others))
-        nc.gpsimd.tensor_tensor(total, rest, weighed[:, others], ADD)
+        total = keep.tile([P, width(others)], F32, name="back3")
+        mix(total[:], rest, weighed[:, others])
         nc.vector.tensor_copy(window[LAST][:].indirect(names(own)), mine)
-        scatter(LAST, others, total)
+        scatter(LAST, others, total[:])
         nc.sync.dma_start(out=out_planes[LAST], in_=window[LAST][:])
 
         def pool_round(out, source):

@@ -31,7 +31,7 @@ KIB = 1024
 HEAD = slice(0, 384)
 TAIL = slice(384, T)
 PIECES = (HEAD, slice(384, 704), slice(704, T))
-LAST_PIECES = (slice(0, 704), slice(704, T))
+LAST_PIECES = (slice(0, 640), slice(640, T))
 W_VECTOR = 88
 SIDES = (slice(0, 1024), slice(1024, U))
 CHUNKS = ((slice(0, 512), slice(512, 768), slice(768, 1024)), (slice(1024, 1536), slice(1536, U)))
@@ -240,21 +240,15 @@ def tile_picked_wema_none_lo_kernel(tc, x_words, x_scales, mem, w1, old, new, sl
         gather(first, LAST, own)
         rest = placed("old_rest3", 57, width(others))
         gather(rest, LAST, others)
-        mine = placed("front3", 59.5, width(own))
-        mix(mine, first, weighed[:, own])
+        nc.vector.tensor_tensor(window[LAST][:].indirect(names(own)), first, weighed[:, own], ADD)
         total = keep.tile([P, width(others)], F32, name="back3")
         mix(total[:], rest, weighed[:, others])
-        nc.vector.tensor_copy(window[LAST][:].indirect(names(own)), mine)
         scatter(LAST, others, total[:])
         nc.sync.dma_start(out=out_planes[LAST], in_=window[LAST][:])
 
-        def pool_round(out, source):
-            nc.gpsimd.tensor_scalar(out, source, 1.0, 0.0, MULT, ADD)
-
         for t in range(2):
-            round_plane(t, 0, pool_round)
-        for t in range(2):
-            round_plane(t, 1, dve)
+            for side in range(2):
+                round_plane(t, side, dve)
         round_plane(2, 0, dve, edge=4)
         round_plane(2, 1, dve)
         round_plane(LAST, 0, act)

@@ -28,18 +28,23 @@ BANK = 512
 HALVES = T // BANK
 LAST = PACK - 1
 KIB = 1024
-HEAD = slice(0, 384)
-TAIL = slice(384, T)
-PIECES = (HEAD, slice(384, 704), slice(704, T))
-LAST_PIECES = (slice(0, 640), slice(640, T))
+STRIPE = 16
+
+FRONT = slice(0, 384)
+REST = slice(FRONT.stop, T)
+SECOND, ENDING = slice(384, 768), slice(768, T)
+MIDDLE, BACK = slice(384, 704), slice(704, T)
+OWN, OTHERS = slice(0, 640), slice(640, T)
+SPARE = slice(T - 192, T)
 W_VECTOR = 88
-SIDES = (slice(0, 1024), slice(1024, U))
+SIDES = (slice(0, U // 2), slice(U // 2, U))
 CHUNKS = ((slice(0, 512), slice(512, 768), slice(768, 1024)), (slice(1024, 1536), slice(1536, U)))
+EDGE = 4
 
 
 def tile_picked_wema_none_lo_kernel(tc, x_words, x_scales, mem, w1, old, new, slot, out_0, out_1, out_2):
     nc = tc.nc
-    act, dve = nc.scalar.copy, nc.vector.tensor_copy
+    scalar_copy, vector_copy = nc.scalar.copy, nc.vector.tensor_copy
 
     def half(s):
         return slice(BANK * s, BANK * (s + 1))
@@ -47,28 +52,32 @@ def tile_picked_wema_none_lo_kernel(tc, x_words, x_scales, mem, w1, old, new, sl
     def width(piece):
         return piece.stop - piece.start
 
+    def within(piece, whole):
+        return slice(piece.start - whole.start, piece.stop - whole.start)
+
     with ExitStack() as ctx:
         keep = ctx.enter_context(tc.tile_pool(name="keep", bufs=1))
         shared = ctx.enter_context(tc.tile_pool(name="shared", bufs=1))
         psum = ctx.enter_context(tc.psum_pool(name="psum", bufs=1))
 
-        def bank_tile(place, name):
-            return psum.tile([P, BANK], F32, name=name, offset=4 * BANK * place)
+        def bank_tile(bank, name):
+            return psum.tile([P, BANK], F32, name=name, offset=4 * BANK * bank)
 
-        def placed(name, kib, columns, room=None):
-            tile = shared.tile([P, room or columns], F32, name=name, offset=int(KIB * kib), align_bytes=64)
+        def placed(name, at, columns, until=None):
+            room = columns if until is None else int((until - at) * KIB) // 4
+            tile = shared.tile([P, room], F32, name=name, offset=int(KIB * at), align_bytes=64)
             return tile[:, 0:columns]
 
-        offs = keep.tile([P, T // 16], U16, name="offs")
+        offs = keep.tile([P, T // STRIPE], U16, name="offs")
         ident = keep.tile([P, P], F32, name="ident")
         make_identity(nc, ident[:])
 
         xw_dram = x_words.bitcast(I32)
         xs_dram = x_scales.bitcast(I32)
-        mem_planes = mem.rearrange("(p r) u -> r p u", r=PACK)
-        out_planes = out_0.rearrange("(p r) u -> r p u", r=PACK)
-        old_cols = keep.tile([P, HALVES, PACK], F32, name="old_cols")
-        new_cols = keep.tile([P, HALVES, PACK], F32, name="new_cols")
+        mem_rows = mem.rearrange("(p t) u -> t p u", t=PACK)
+        out_rows = out_0.rearrange("(p t) u -> t p u", t=PACK)
+        old_cols = keep.tile([P, HALVES * PACK], F32, name="old_cols")
+        new_cols = keep.tile([P, HALVES * PACK], F32, name="new_cols")
         w_raw = [keep.tile([P, PACK, N], F32, name="w_raw%d" % z) for z in range(PASSES)]
         x_word = [keep.tile([P, PASSES, 2 * BANK], U8, name="x_word%d" % s, align_bytes=64) for s in range(HALVES)]
         x_scale = keep.tile([P, PASSES, T], U8, name="x_scale", align_bytes=64)
@@ -81,8 +90,8 @@ def tile_picked_wema_none_lo_kernel(tc, x_words, x_scales, mem, w1, old, new, sl
             ints = BANK // 2
             nc.sync.dma_start(out=x_word[s][:].bitcast(I32), in_=xw_dram[:, :, ints * s : ints * (s + 1)].rearrange("z p c -> p z c"))
 
-        def load_row(cols, row):
-            nc.sync.dma_start(out=cols[:], in_=row[0:1, :].rearrange("o (s p b) -> (o p) s b", p=P, b=PACK))
+        def load_row(cols, rows):
+            nc.sync.dma_start(out=cols[:], in_=rows[0:1, :].rearrange("o (p b) -> (o p) b", p=P))
 
         load_row(old_cols, old)
         load_w(0)
@@ -92,19 +101,19 @@ def tile_picked_wema_none_lo_kernel(tc, x_words, x_scales, mem, w1, old, new, sl
             nc.sync.dma_start(out=x_scale[r:P:QUADRANT, :, :].bitcast(I32), in_=xs_dram[:, r:SCALE_ROWS:PACK, :].rearrange("z q c -> q z c"))
         load_w(1)
         load_x(0)
-        nc.sync.dma_start(out=window[0][:], in_=mem_planes[0])
+        nc.sync.dma_start(out=window[0][:], in_=mem_rows[0])
         load_x(1)
         for t in range(1, PACK):
-            nc.sync.dma_start(out=window[t][:], in_=mem_planes[t])
+            nc.sync.dma_start(out=window[t][:], in_=mem_rows[t])
 
         old_all = keep.tile([P, T], F32, name="old_all")
         new_all = keep.tile([P, T], F32, name="new_all")
 
-        def spread(cols, whole, s, place):
-            bank = bank_tile(place, "spread%d" % place)
+        def spread(cols, whole, s, bank):
+            turned = bank_tile(bank, "spread%d" % bank)
             for i in range(PACK):
-                nc.tensor.transpose(bank[:, P * i : P * (i + 1)], cols[:, s, i : i + 1].to_broadcast([P, P]), ident[:])
-            act(whole[:, half(s)].rearrange("m (p i) -> m p i", i=PACK), bank[:].rearrange("m (i p) -> m p i", i=PACK))
+                nc.tensor.transpose(turned[:, P * i : P * (i + 1)], cols[:, PACK * s + i : PACK * s + i + 1].to_broadcast([P, P]), ident[:])
+            scalar_copy(whole[:].rearrange("m (p s i) -> m s p i", s=HALVES, i=PACK)[:, s], turned[:].rearrange("m (i p) -> m p i", i=PACK))
 
         spread(old_cols, old_all, 0, 3)
         spread(old_cols, old_all, 1, 2)
@@ -127,27 +136,27 @@ def tile_picked_wema_none_lo_kernel(tc, x_words, x_scales, mem, w1, old, new, sl
                 for i, t in enumerate(group):
                     w_mx[(t, z)] = (codes[:, P * i : P * (i + 1)], scales[:, P * i : P * (i + 1)])
 
-        def project(t, piece, place):
-            s, first = divmod(piece.start, BANK)
-            bank = bank_tile(place, "y%d_%d" % (t, piece.start))
+        def project(t, piece, bank):
+            s, skip = divmod(piece.start, BANK)
+            y = bank_tile(bank, "y%d_%d" % (t, piece.start))
             for z in range(PASSES):
                 codes, scales = w_mx[(t, z)]
                 nc.tensor.matmul_mx(
-                    out=bank[:, 0 : width(piece)],
+                    out=y[:, 0 : width(piece)],
                     lhsT=codes.bitcast(FP8X4),
                     lhsT_scale=scales,
-                    rhs=x_word[s][:, z, 2 * first : 2 * (first + width(piece))].bitcast(FP4X4),
+                    rhs=x_word[s][:, z, 2 * skip : 2 * (skip + width(piece))].bitcast(FP4X4),
                     rhs_scale=x_scale[:, z, piece],
                     start=(z == 0),
                     stop=(z == PASSES - 1),
                 )
-            return bank[:, 0 : width(piece)]
+            return y[:, 0 : width(piece)]
 
         def names(piece):
-            return offs[:, piece.start // 16 : piece.stop // 16]
+            return offs[:, piece.start // STRIPE : piece.stop // STRIPE]
 
-        def weigh(into, piece, bank):
-            nc.vector.tensor_tensor(into, bank, new_all[:, piece], MULT)
+        def weigh(into, piece, y):
+            nc.vector.tensor_tensor(into, y, new_all[:, piece], MULT)
 
         def gather(into, t, piece):
             nc.vector.tensor_tensor(into, window[t][:].indirect(names(piece)), old_all[:, piece], MULT)
@@ -158,112 +167,106 @@ def tile_picked_wema_none_lo_kernel(tc, x_words, x_scales, mem, w1, old, new, sl
         def scatter(t, piece, total):
             nc.scalar.activation(window[t][:].indirect(names(piece)), total, COPY)
 
-        quantise_w(0, ((dve, slice(0, P)),), (range(0, PACK),))
-        quantise_w(1, ((dve, slice(0, W_VECTOR)), (act, slice(W_VECTOR, P))), (range(0, 1), range(1, PACK)))
+        def store(t):
+            nc.sync.dma_start(out=out_rows[t], in_=window[t][:])
 
-        front, middle, back = PIECES
+        quantise_w(0, ((vector_copy, slice(0, P)),), (range(0, PACK),))
+        quantise_w(1, ((vector_copy, slice(0, W_VECTOR)), (scalar_copy, slice(W_VECTOR, P))), (range(0, 1), range(1, PACK)))
 
-        def within(piece, whole):
-            return slice(piece.start - whole.start, piece.stop - whole.start)
-
-        def finish(t, kib, piece, engine, kept, weighed):
-            total = placed("back%d" % t, kib, width(piece))
-            engine.tensor_tensor(total, kept, weighed, ADD)
-            scatter(t, piece, total)
-            nc.sync.dma_start(out=out_planes[t], in_=window[t][:])
-
-        lower = placed("lower_y0", 30, BANK, 5 * KIB // 4)
-        parts = (slice(0, 2 * P), slice(2 * P, front.stop), slice(front.stop, BANK))
-        banks = [project(0, part, i) for i, part in enumerate(parts)]
+        lower = placed("lower_y0", 30, BANK, until=35)
+        parts = (slice(0, 2 * P), slice(2 * P, FRONT.stop), slice(FRONT.stop, BANK))
+        part_y = [project(0, part, bank) for bank, part in enumerate(parts)]
         for i in range(2):
-            weigh(lower[:, parts[i]], parts[i], banks[i])
-        first = placed("first", 0, width(front), 11 * KIB // 4)
-        gather(first, 0, front)
-        weigh(lower[:, parts[2]], parts[2], banks[2])
-        plain = keep.tile([P, width(TAIL)], F32, name="plain")
-        nc.scalar.activation(plain[:], window[0][:].indirect(names(TAIL)), COPY)
-        total = keep.tile([P, width(front)], F32, name="front0")
-        mix(total[:], first, lower[:, front])
-        scatter(0, front, total[:])
-        rest = placed("old_rest0", 8, width(TAIL), 12 * KIB // 4)
-        nc.gpsimd.tensor_tensor(rest, plain[:], old_all[:, TAIL], MULT)
-        upper = placed("upper_y0", 2, BANK)
-        weighed = placed("new_y1", 4, T)
+            weigh(lower[:, parts[i]], parts[i], part_y[i])
+        kept_front = placed("old_front0", 0, width(FRONT), until=11)
+        gather(kept_front, 0, FRONT)
+        weigh(lower[:, parts[2]], parts[2], part_y[2])
+        plain = keep.tile([P, width(REST)], F32, name="plain0")
+        nc.scalar.activation(plain[:], window[0][:].indirect(names(REST)), COPY)
+        total = keep.tile([P, width(FRONT)], F32, name="front0")
+        mix(total[:], kept_front, lower[:, FRONT])
+        scatter(0, FRONT, total[:])
+        ahead = placed("plain1", 1.5, width(SPARE))
+        nc.scalar.activation(ahead, window[1][:].indirect(names(SPARE)), COPY)
+        kept_rest = placed("old_rest0", 8.5, width(REST), until=20)
+        nc.gpsimd.tensor_tensor(kept_rest, plain[:], old_all[:, REST], MULT)
+        upper = placed("upper_y0", 2.5, BANK)
+        weighed = placed("new_y1", 4.5, T)
         weigh(weighed[:, half(0)], half(0), project(1, half(0), 1))
         weigh(upper, half(1), project(0, half(1), 0))
         weigh(weighed[:, half(1)], half(1), project(1, half(1), 2))
-        second, ending = slice(front.stop, 2 * front.stop), slice(2 * front.stop, T)
-        total = keep.tile([P, width(second)], F32, name="middle0")
-        rim = BANK - second.start
-        mix(total[:, 0:rim], rest[:, 0:rim], lower[:, second.start : BANK])
-        mix(total[:, rim:], rest[:, rim : width(second)], upper[:, 0 : second.stop - BANK])
-        scatter(0, second, total[:])
-        behind = (rest[:, within(ending, TAIL)], upper[:, within(ending, half(1))])
+        total = keep.tile([P, width(SECOND)], F32, name="middle0")
+        rim = BANK - SECOND.start
+        mix(total[:, 0:rim], kept_rest[:, 0:rim], lower[:, SECOND.start : BANK])
+        mix(total[:, rim:], kept_rest[:, rim : width(SECOND)], upper[:, 0 : SECOND.stop - BANK])
+        scatter(0, SECOND, total[:])
+        left, left_kept, left_weighed = ENDING, kept_rest[:, within(ENDING, REST)], upper[:, within(ENDING, half(1))]
 
-        for t, at_front, at_rest, room in ((1, 24, 32, 26), (2, 14, 11, 3)):
-            first = placed("old_front%d" % t, at_front, width(front), (13 if t == 1 else 12) * KIB // 8)
-            gather(first, t, front)
-            rest = placed("old_rest%d" % t, at_rest, width(TAIL), room * KIB // 4)
-            gather(rest, t, TAIL)
-            total = keep.tile([P, width(front)], F32, name="front%d" % t)
-            mix(total[:], first, weighed[:, front])
-            scatter(t, front, total[:])
-            finish(t - 1, at_front, ending if t == 1 else back, nc.gpsimd, *behind)
-            coming = placed("new_y%d" % (t + 1), at_front + 2, T)
-            for s in range(HALVES):
-                weigh(coming[:, half(s)], half(s), project(t + 1, half(s), (2 * t + 2 + s) % 3))
+        for t, front_at, front_until, rest_at, rest_until in ((1, 24, 30.5, 32, 58), (2, 14, 20, 11, 14)):
+            kept_front = placed("old_front%d" % t, front_at, width(FRONT), until=front_until)
+            gather(kept_front, t, FRONT)
+            kept_rest = placed("old_rest%d" % t, rest_at, width(REST), until=rest_until)
             if t == 1:
-                total = keep.tile([P, width(middle)], F32, name="middle%d" % t)
-                mix(total[:], rest[:, within(middle, TAIL)], weighed[:, middle])
-                scatter(t, middle, total[:])
-                behind = (rest[:, within(back, TAIL)], weighed[:, back])
+                gather(kept_rest[:, 0 : SPARE.start - REST.start], t, slice(REST.start, SPARE.start))
+                nc.vector.tensor_tensor(kept_rest[:, within(SPARE, REST)], ahead, old_all[:, SPARE], MULT)
             else:
-                total = keep.tile([P, width(TAIL)], F32, name="tail%d" % t)
-                mix(total[:], rest, weighed[:, TAIL])
-                for piece in (middle, back):
-                    scatter(t, piece, total[:, within(piece, TAIL)])
-                nc.sync.dma_start(out=out_planes[t], in_=window[t][:])
+                gather(kept_rest, t, REST)
+            total = keep.tile([P, width(FRONT)], F32, name="front%d" % t)
+            mix(total[:], kept_front, weighed[:, FRONT])
+            scatter(t, FRONT, total[:])
+            last_sum = placed("back%d" % (t - 1), front_at, width(left))
+            nc.gpsimd.tensor_tensor(last_sum, left_kept, left_weighed, ADD)
+            scatter(t - 1, left, last_sum)
+            store(t - 1)
+            coming = placed("new_y%d" % (t + 1), front_at + 2, T)
+            for s in range(HALVES):
+                weigh(coming[:, half(s)], half(s), project(t + 1, half(s), (HALVES * (t + 1) + s) % 3))
+            if t == 1:
+                total = keep.tile([P, width(MIDDLE)], F32, name="middle1")
+                mix(total[:], kept_rest[:, within(MIDDLE, REST)], weighed[:, MIDDLE])
+                scatter(t, MIDDLE, total[:])
+                left, left_kept, left_weighed = BACK, kept_rest[:, within(BACK, REST)], weighed[:, BACK]
+            else:
+                total = keep.tile([P, width(REST)], F32, name="rest2")
+                mix(total[:], kept_rest, weighed[:, REST])
+                for piece in (MIDDLE, BACK):
+                    scatter(t, piece, total[:, within(piece, REST)])
+                store(t)
             weighed = coming
 
-        pairs = {}
+        kept_own = placed("old_own3", 35, width(OWN), until=50)
+        gather(kept_own, LAST, OWN)
+        kept_others = placed("old_others3", 57, width(OTHERS))
+        gather(kept_others, LAST, OTHERS)
+        nc.vector.tensor_tensor(window[LAST][:].indirect(names(OWN)), kept_own, weighed[:, OWN], ADD)
+        total = keep.tile([P, width(OTHERS)], F32, name="others3")
+        mix(total[:], kept_others, weighed[:, OTHERS])
+        scatter(LAST, OTHERS, total[:])
+        store(LAST)
 
-        def round_plane(t, side, copy, edge=0):
-            if side not in pairs:
-                pairs[side] = shared.tile([P, 2, width(SIDES[side]), 2], BF16, name="pairs%d" % side, offset=KIB * (40 + 9 * side), align_bytes=64)
-            source = window[t][:, SIDES[side]]
-            copy(pairs[side][:, t // 2, edge:, t % 2], source[:, edge:])
-            if edge:
-                copy(pairs[side][:, t // 2, 0:edge], source[:, 0:edge].unsqueeze(2).to_broadcast([P, edge, 2]))
+        pairs = [shared.tile([P, 2, width(cols), 2], BF16, name="pairs%d" % side, offset=KIB * (40, 49)[side], align_bytes=64) for side, cols in enumerate(SIDES)]
 
-        own, others = LAST_PIECES
-        first = placed("old_front3", 35, width(own), 15 * KIB // 4)
-        gather(first, LAST, own)
-        rest = placed("old_rest3", 57, width(others))
-        gather(rest, LAST, others)
-        nc.vector.tensor_tensor(window[LAST][:].indirect(names(own)), first, weighed[:, own], ADD)
-        total = keep.tile([P, width(others)], F32, name="back3")
-        mix(total[:], rest, weighed[:, others])
-        scatter(LAST, others, total[:])
-        nc.sync.dma_start(out=out_planes[LAST], in_=window[LAST][:])
+        def round_window(t, side, copy, skip=0):
+            copy(pairs[side][:, t // 2, skip:, t % 2], window[t][:, SIDES[side]][:, skip:])
 
         for t in range(2):
             for side in range(2):
-                round_plane(t, side, dve)
-        round_plane(2, 0, dve, edge=4)
-        round_plane(2, 1, dve)
-        round_plane(LAST, 0, act)
-        round_plane(LAST, 1, dve)
+                round_window(t, side, vector_copy)
+        round_window(2, 0, vector_copy, skip=EDGE)
+        vector_copy(pairs[0][:, 1, 0:EDGE], window[2][:, 0:EDGE].unsqueeze(2).to_broadcast([P, EDGE, 2]))
+        round_window(2, 1, vector_copy)
+        round_window(LAST, 0, scalar_copy)
+        round_window(LAST, 1, vector_copy)
 
         out_scale = keep.tile([P, U], U8, name="out_scale", align_bytes=64)
         words_dram = out_1[0].rearrange("p c r -> p (c r)").bitcast(I32)
         grouped = {}
-        for side, copy in ((1, dve), (0, act)):
-            words = pairs[side][:].rearrange("p u c e -> p u (c e)").bitcast(F32)
+        for side, copy in ((1, vector_copy), (0, scalar_copy)):
+            pair_words = pairs[side][:].rearrange("p u c e -> p u (c e)").bitcast(F32)
             for chunk in CHUNKS[side]:
-                tile = keep.tile([P, width(chunk) * PACK], BF16, name="grouped%d" % chunk.start, align_bytes=64)
-                part = words[:, :, chunk.start - SIDES[side].start : chunk.stop - SIDES[side].start]
-                copy(tile[:].bitcast(F32).rearrange("p (c u) -> p c u", u=2), part.rearrange("p u c -> p c u"))
-                grouped[chunk.start] = tile
+                four = keep.tile([P, width(chunk) * PACK], BF16, name="grouped%d" % chunk.start, align_bytes=64)
+                copy(four[:].bitcast(F32).rearrange("p (c u) -> p c u", u=2), pair_words[:, :, within(chunk, SIDES[side])].rearrange("p u c -> p c u"))
+                grouped[chunk.start] = four
         for chunk in CHUNKS[1] + CHUNKS[0]:
             codes = keep.tile([P, width(chunk)], U32, name="codes%d" % chunk.start, align_bytes=64)
             nc.vector.quantize_mx(out=codes[:].bitcast(FP8X4), scales=out_scale[:, chunk], in_=grouped[chunk.start][:])

@@ -176,15 +176,17 @@ def tile_picked_wema_none_lo_kernel(tc, x_words, x_scales, mem, w1, old, new, sl
         lower = placed("lower_y0", 30, BANK, until=35)
         parts = (slice(0, 2 * P), slice(2 * P, FRONT.stop), slice(FRONT.stop, BANK))
         part_y = [project(0, part, bank) for bank, part in enumerate(parts)]
-        for i in range(2):
+        for i in range(3):
             weigh(lower[:, parts[i]], parts[i], part_y[i])
         kept_front = placed("old_front0", 0, width(FRONT), until=11)
-        gather(kept_front, 0, FRONT)
-        weigh(lower[:, parts[2]], parts[2], part_y[2])
+        front_halves = (slice(0, width(FRONT) // 2), slice(width(FRONT) // 2, FRONT.stop))
+        for piece in front_halves:
+            gather(kept_front[:, piece], 0, piece)
         plain = keep.tile([P, width(REST)], F32, name="plain0")
         nc.scalar.activation(plain[:], window[0][:].indirect(names(REST)), COPY)
         total = keep.tile([P, width(FRONT)], F32, name="front0")
-        mix(total[:], kept_front, lower[:, FRONT])
+        for piece in front_halves:
+            mix(total[:, piece], kept_front[:, piece], lower[:, piece])
         scatter(0, FRONT, total[:])
         ahead = placed("plain1", 1.5, width(SPARE))
         nc.scalar.activation(ahead, window[1][:].indirect(names(SPARE)), COPY)
@@ -227,45 +229,52 @@ def tile_picked_wema_none_lo_kernel(tc, x_words, x_scales, mem, w1, old, new, sl
                 scatter(t, MIDDLE, total[:])
                 left, left_kept, left_weighed = BACK, kept_rest[:, within(BACK, REST)], weighed[:, BACK]
             else:
-                total = keep.tile([P, width(REST)], F32, name="rest2")
-                mix(total[:], kept_rest, weighed[:, REST])
-                for piece in (MIDDLE, BACK):
-                    scatter(t, piece, total[:, within(piece, REST)])
-                store(t)
+                total = keep.tile([P, width(MIDDLE)], F32, name="middle2")
+                mix(total[:], kept_rest[:, within(MIDDLE, REST)], weighed[:, MIDDLE])
+                scatter(t, MIDDLE, total[:])
+                left, left_kept, left_weighed = BACK, kept_rest[:, within(BACK, REST)], weighed[:, BACK]
             weighed = coming
 
-        kept_own = placed("old_own3", 35, width(OWN), until=50)
-        gather(kept_own, LAST, OWN)
         kept_others = placed("old_others3", 57, width(OTHERS))
         gather(kept_others, LAST, OTHERS)
-        nc.vector.tensor_tensor(window[LAST][:].indirect(names(OWN)), kept_own, weighed[:, OWN], ADD)
+        kept_own = placed("old_own3", 35, width(OWN), until=50)
+        gather(kept_own, LAST, OWN)
         total = keep.tile([P, width(OTHERS)], F32, name="others3")
         mix(total[:], kept_others, weighed[:, OTHERS])
+        nc.vector.tensor_tensor(window[LAST][:].indirect(names(OWN)), kept_own, weighed[:, OWN], ADD)
         scatter(LAST, OTHERS, total[:])
         store(LAST)
+        total = keep.tile([P, width(left)], F32, name="back2")
+        mix(total[:], left_kept, left_weighed)
+        scatter(2, left, total[:])
+        store(2)
 
         pairs = [shared.tile([P, 2, width(cols), 2], BF16, name="pairs%d" % side, offset=KIB * (40, 49)[side], align_bytes=64) for side, cols in enumerate(SIDES)]
 
-        def round_window(t, side, copy, skip=0):
-            copy(pairs[side][:, t // 2, skip:, t % 2], window[t][:, SIDES[side]][:, skip:])
+        def round_window(t, side, copy, skip=0, stop=U // 2):
+            copy(pairs[side][:, t // 2, skip:stop, t % 2], window[t][:, SIDES[side]][:, skip:stop])
 
         for t in range(2):
             for side in range(2):
                 round_window(t, side, vector_copy)
-        round_window(2, 0, vector_copy, skip=EDGE)
-        vector_copy(pairs[0][:, 1, 0:EDGE], window[2][:, 0:EDGE].unsqueeze(2).to_broadcast([P, EDGE, 2]))
-        round_window(2, 1, vector_copy)
-        round_window(LAST, 0, scalar_copy)
+        round_window(LAST, 0, vector_copy, skip=EDGE)
+        vector_copy(pairs[0][:, 1, 0:EDGE], window[LAST][:, 0:EDGE].unsqueeze(2).to_broadcast([P, EDGE, 2]))
         round_window(LAST, 1, vector_copy)
+        round_window(2, 0, scalar_copy)
+        round_window(2, 1, vector_copy, stop=BANK)
+        round_window(2, 1, vector_copy, skip=BANK)
 
         out_scale = keep.tile([P, U], U8, name="out_scale", align_bytes=64)
         words_dram = out_1[0].rearrange("p c r -> p (c r)").bitcast(I32)
         grouped = {}
         for side, copy in ((1, vector_copy), (0, scalar_copy)):
-            pair_words = pairs[side][:].rearrange("p u c e -> p u (c e)").bitcast(F32)
             for chunk in CHUNKS[side]:
                 four = keep.tile([P, width(chunk) * PACK], BF16, name="grouped%d" % chunk.start, align_bytes=64)
-                copy(four[:].bitcast(F32).rearrange("p (c u) -> p c u", u=2), pair_words[:, :, within(chunk, SIDES[side])].rearrange("p u c -> p c u"))
+                if side == 1:
+                    copy(four[:].rearrange("p (c u e) -> p c u e", u=2, e=2), pairs[side][:, :, within(chunk, SIDES[side])].rearrange("p u c e -> p c u e"))
+                else:
+                    pair_words = pairs[side][:].rearrange("p u c e -> p u (c e)").bitcast(F32)
+                    copy(four[:].bitcast(F32).rearrange("p (c u) -> p c u", u=2), pair_words[:, :, within(chunk, SIDES[side])].rearrange("p u c -> p c u"))
                 grouped[chunk.start] = four
         for chunk in CHUNKS[1] + CHUNKS[0]:
             codes = keep.tile([P, width(chunk)], U32, name="codes%d" % chunk.start, align_bytes=64)

@@ -26,20 +26,19 @@ QUADRANT = 32
 SCALE_ROWS = 16
 BANK = 512
 HALVES = T // BANK
+BLOCKS = T // P
 LAST = PACK - 1
 KIB = 1024
 STRIPE = 16
 
-FRONT = slice(0, 384)
+FRONT, MIDDLE, BACK = slice(0, 384), slice(384, 768), slice(768, T)
 REST = slice(FRONT.stop, T)
-SECOND, ENDING = slice(384, 768), slice(768, T)
-MIDDLE, BACK = slice(384, 704), slice(704, T)
-OWN, OTHERS = slice(0, 640), slice(640, T)
-SPARE = slice(T - 192, T)
+OWN, OTHERS = slice(0, 704), slice(704, T)
 W_VECTOR = 88
 SIDES = (slice(0, U // 2), slice(U // 2, U))
 CHUNKS = ((slice(0, 512), slice(512, 768), slice(768, 1024)), (slice(1024, 1536), slice(1536, U)))
 EDGE = 4
+GPSIMD_SLOTS = 896
 
 
 def tile_picked_wema_none_lo_kernel(tc, x_words, x_scales, mem, w1, old, new, slot, out_0, out_1, out_2):
@@ -68,20 +67,25 @@ def tile_picked_wema_none_lo_kernel(tc, x_words, x_scales, mem, w1, old, new, sl
             tile = shared.tile([P, room], F32, name=name, offset=int(KIB * at), align_bytes=64)
             return tile[:, 0:columns]
 
+        def fresh(name, columns):
+            return keep.tile([P, columns], F32, name=name)[:]
+
         offs = keep.tile([P, T // STRIPE], U16, name="offs")
         ident = keep.tile([P, P], F32, name="ident")
         make_identity(nc, ident[:])
+
 
         xw_dram = x_words.bitcast(I32)
         xs_dram = x_scales.bitcast(I32)
         mem_rows = mem.rearrange("(p t) u -> t p u", t=PACK)
         out_rows = out_0.rearrange("(p t) u -> t p u", t=PACK)
-        old_cols = keep.tile([P, HALVES * PACK], F32, name="old_cols")
-        new_cols = keep.tile([P, HALVES * PACK], F32, name="new_cols")
+        old_cols = keep.tile([P, BLOCKS], F32, name="old_cols")
+        new_cols = keep.tile([P, BLOCKS], F32, name="new_cols")
         w_raw = [keep.tile([P, PACK, N], F32, name="w_raw%d" % z) for z in range(PASSES)]
         x_word = [keep.tile([P, PASSES, 2 * BANK], U8, name="x_word%d" % s, align_bytes=64) for s in range(HALVES)]
         x_scale = keep.tile([P, PASSES, T], U8, name="x_scale", align_bytes=64)
-        window = [keep.tile([P, U], F32, name="window%d" % t) for t in range(PACK)]
+        window = [shared.tile([P, U], F32, name="window0", offset=60 * KIB, align_bytes=64)]
+        window.extend(keep.tile([P, U], F32, name="window%d" % t) for t in range(1, PACK))
 
         def load_w(z):
             nc.sync.dma_start(out=w_raw[z][:], in_=w1[K_PASS * z : K_PASS * (z + 1), :].rearrange("(p i) n -> p i n", i=PACK))
@@ -93,9 +97,9 @@ def tile_picked_wema_none_lo_kernel(tc, x_words, x_scales, mem, w1, old, new, sl
         def load_row(cols, rows):
             nc.sync.dma_start(out=cols[:], in_=rows[0:1, :].rearrange("o (p b) -> (o p) b", p=P))
 
-        load_row(old_cols, old)
-        load_w(0)
         load_row(new_cols, new)
+        load_w(0)
+        load_row(old_cols, old)
         nc.sync.dma_start(offs[:], slot)
         for r in range(PACK):
             nc.sync.dma_start(out=x_scale[r:P:QUADRANT, :, :].bitcast(I32), in_=xs_dram[:, r:SCALE_ROWS:PACK, :].rearrange("z q c -> q z c"))
@@ -103,11 +107,12 @@ def tile_picked_wema_none_lo_kernel(tc, x_words, x_scales, mem, w1, old, new, sl
         load_x(0)
         nc.sync.dma_start(out=window[0][:], in_=mem_rows[0])
         load_x(1)
-        for t in range(1, PACK):
+        for t in (1, LAST, 2):
             nc.sync.dma_start(out=window[t][:], in_=mem_rows[t])
 
         old_all = keep.tile([P, T], F32, name="old_all")
         new_all = keep.tile([P, T], F32, name="new_all")
+        new_by_block = keep.tile([P, BLOCKS], F32, name="new_by_block")
 
         def spread(cols, whole, s, bank):
             turned = bank_tile(bank, "spread%d" % bank)
@@ -115,10 +120,19 @@ def tile_picked_wema_none_lo_kernel(tc, x_words, x_scales, mem, w1, old, new, sl
                 nc.tensor.transpose(turned[:, P * i : P * (i + 1)], cols[:, PACK * s + i : PACK * s + i + 1].to_broadcast([P, P]), ident[:])
             scalar_copy(whole[:].rearrange("m (p s i) -> m s p i", s=HALVES, i=PACK)[:, s], turned[:].rearrange("m (i p) -> m p i", i=PACK))
 
-        spread(old_cols, old_all, 0, 3)
-        spread(old_cols, old_all, 1, 2)
-        spread(new_cols, new_all, 0, 0)
-        spread(new_cols, new_all, 1, 1)
+        spread(new_cols, new_all, 0, 3)
+        spread(new_cols, new_all, 1, 2)
+
+        def new_on_partitions(s, bank):
+            turned = bank_tile(bank, "new_turned%d" % s)
+            for i in range(PACK):
+                nc.tensor.transpose(turned[:, P * i : P * (i + 1)], new_all[:, BANK * s + P * i : BANK * s + P * (i + 1)], ident[:])
+            scalar_copy(new_by_block[:, PACK * s : PACK * (s + 1)], turned[:, 0:BANK:P])
+
+        new_on_partitions(0, 4)
+        new_on_partitions(1, 5)
+        spread(old_cols, old_all, 0, 0)
+        spread(old_cols, old_all, 1, 1)
 
         w_mx = {}
 
@@ -134,23 +148,49 @@ def tile_picked_wema_none_lo_kernel(tc, x_words, x_scales, mem, w1, old, new, sl
                 scales = keep.tile([P, cols], U8, name="w_scales%d_%d" % (z, group.start), align_bytes=64)
                 nc.vector.quantize_mx(out=codes[:].bitcast(FP8X4), scales=scales[:], in_=grouped[:, K_PASS * group.start : K_PASS * group.stop])
                 for i, t in enumerate(group):
-                    w_mx[(t, z)] = (codes[:, P * i : P * (i + 1)], scales[:, P * i : P * (i + 1)])
+                    w_mx[(t, z)] = (codes, scales, P * i)
+
+        def w_operand(t, z, windows):
+            codes, scales, first = w_mx[(t, z)]
+            cols = slice(first, first + P * windows)
+            return codes[:, cols].bitcast(FP8X4), scales[:, cols]
+
+        def x_operand(piece, z):
+            s, skip = divmod(piece.start, BANK)
+            return x_word[s][:, z, 2 * skip : 2 * (skip + width(piece))].bitcast(FP4X4), x_scale[:, z, piece]
+
+        def multiply(out, stationary, moving):
+            for z in range(PASSES):
+                (lhs, lhs_scale), (rhs, rhs_scale) = stationary(z), moving(z)
+                nc.tensor.matmul_mx(out=out, lhsT=lhs, lhsT_scale=lhs_scale, rhs=rhs, rhs_scale=rhs_scale, start=(z == 0), stop=(z == PASSES - 1))
 
         def project(t, piece, bank):
-            s, skip = divmod(piece.start, BANK)
-            y = bank_tile(bank, "y%d_%d" % (t, piece.start))
-            for z in range(PASSES):
-                codes, scales = w_mx[(t, z)]
-                nc.tensor.matmul_mx(
-                    out=y[:, 0 : width(piece)],
-                    lhsT=codes.bitcast(FP8X4),
-                    lhsT_scale=scales,
-                    rhs=x_word[s][:, z, 2 * skip : 2 * (skip + width(piece))].bitcast(FP4X4),
-                    rhs_scale=x_scale[:, z, piece],
-                    start=(z == 0),
-                    stop=(z == PASSES - 1),
-                )
-            return y[:, 0 : width(piece)]
+            y = bank_tile(bank, "y%d_%d" % (t, piece.start))[:, 0 : width(piece)]
+            multiply(y, lambda z: w_operand(t, z, 1), lambda z: x_operand(piece, z))
+            return y
+
+        def project_blocks(first, bank):
+            both = bank_tile(bank, "y_blocks%d" % first)
+            for i in range(2):
+                block = slice(P * (first + i), P * (first + i + 1))
+                multiply(both[:, 2 * P * i : 2 * P * (i + 1)], lambda z: x_operand(block, z), lambda z: w_operand(1, z, 2))
+            return both[:, 0 : 2 * P], both[:, 2 * P : 4 * P]
+
+        weighed_block = {}
+
+        def weigh_block(b, y, at, on_scalar):
+            into = placed("new_y_block%d" % b, at, 2 * P)
+            if on_scalar:
+                nc.scalar.activation(into, y, COPY, scale=new_by_block[:, b : b + 1])
+            else:
+                nc.vector.tensor_scalar(into, y, new_by_block[:, b : b + 1], None, MULT)
+            weighed_block[b] = into
+
+        def turn_back(t, piece, bank):
+            back = bank_tile(bank, "turned%d_%d" % (t, piece.start))
+            for i, b in enumerate(range(piece.start // P, piece.stop // P)):
+                nc.tensor.transpose(back[:, P * i : P * (i + 1)], weighed_block[b][:, P * (t - 1) : P * t], ident[:])
+            return back[:, 0 : width(piece)]
 
         def names(piece):
             return offs[:, piece.start // STRIPE : piece.stop // STRIPE]
@@ -161,8 +201,9 @@ def tile_picked_wema_none_lo_kernel(tc, x_words, x_scales, mem, w1, old, new, sl
         def gather(into, t, piece):
             nc.vector.tensor_tensor(into, window[t][:].indirect(names(piece)), old_all[:, piece], MULT)
 
-        def mix(into, kept, weighed):
-            nc.vector.tensor_tensor(into, kept, weighed, ADD)
+        def mix(into, weighed, kept):
+            nc.vector.tensor_tensor(into, weighed, kept, ADD)
+            return into
 
         def scatter(t, piece, total):
             nc.scalar.activation(window[t][:].indirect(names(piece)), total, COPY)
@@ -173,90 +214,88 @@ def tile_picked_wema_none_lo_kernel(tc, x_words, x_scales, mem, w1, old, new, sl
         quantise_w(0, ((vector_copy, slice(0, P)),), (range(0, PACK),))
         quantise_w(1, ((vector_copy, slice(0, W_VECTOR)), (scalar_copy, slice(W_VECTOR, P))), (range(0, 1), range(1, PACK)))
 
-        lower = placed("lower_y0", 30, BANK, until=35)
+        lower = placed("lower_y0", 46, BANK, until=52)
         parts = (slice(0, 2 * P), slice(2 * P, FRONT.stop), slice(FRONT.stop, BANK))
         part_y = [project(0, part, bank) for bank, part in enumerate(parts)]
-        for i in range(3):
-            weigh(lower[:, parts[i]], parts[i], part_y[i])
-        kept_front = placed("old_front0", 0, width(FRONT), until=11)
+        for part, y in zip(parts, part_y):
+            weigh(lower[:, part], part, y)
+        y_block = list(project_blocks(0, 0) + project_blocks(2, 1))
+        kept_front = placed("old_front0", 20, width(FRONT), until=29.5)
         front_halves = (slice(0, width(FRONT) // 2), slice(width(FRONT) // 2, FRONT.stop))
         for piece in front_halves:
             gather(kept_front[:, piece], 0, piece)
-        plain = keep.tile([P, width(REST)], F32, name="plain0")
-        nc.scalar.activation(plain[:], window[0][:].indirect(names(REST)), COPY)
-        total = keep.tile([P, width(FRONT)], F32, name="front0")
+        plain = fresh("plain0", width(REST))
+        nc.scalar.activation(plain, window[0][:].indirect(names(REST)), COPY)
+        total = fresh("front0", width(FRONT))
         for piece in front_halves:
-            mix(total[:, piece], kept_front[:, piece], lower[:, piece])
-        scatter(0, FRONT, total[:])
-        ahead = placed("plain1", 1.5, width(SPARE))
-        nc.scalar.activation(ahead, window[1][:].indirect(names(SPARE)), COPY)
-        kept_rest = placed("old_rest0", 8.5, width(REST), until=20)
-        nc.gpsimd.tensor_tensor(kept_rest, plain[:], old_all[:, REST], MULT)
-        upper = placed("upper_y0", 2.5, BANK)
-        weighed = placed("new_y1", 4.5, T)
-        weigh(weighed[:, half(0)], half(0), project(1, half(0), 1))
-        weigh(upper, half(1), project(0, half(1), 0))
-        weigh(weighed[:, half(1)], half(1), project(1, half(1), 2))
-        total = keep.tile([P, width(SECOND)], F32, name="middle0")
-        rim = BANK - SECOND.start
-        mix(total[:, 0:rim], kept_rest[:, 0:rim], lower[:, SECOND.start : BANK])
-        mix(total[:, rim:], kept_rest[:, rim : width(SECOND)], upper[:, 0 : SECOND.stop - BANK])
-        scatter(0, SECOND, total[:])
-        left, left_kept, left_weighed = ENDING, kept_rest[:, within(ENDING, REST)], upper[:, within(ENDING, half(1))]
+            mix(total[:, piece], lower[:, piece], kept_front[:, piece])
+        scatter(0, FRONT, total)
+        kept_rest0 = placed("old_rest0", 12, width(REST), until=20.5)
+        nc.gpsimd.tensor_tensor(kept_rest0, plain, old_all[:, REST], MULT)
+        for b in range(2):
+            weigh_block(b, y_block[b], 22 + b, False)
+        for b in range(2, 4):
+            weigh_block(b, y_block[b], 22 + b, True)
+        upper = placed("upper_y0", 29, BANK, until=31.5)
+        weigh(upper, half(1), project(0, half(1), 2))
+        y_block.extend(project_blocks(4, 0))
+        weigh_block(4, y_block[4], 26, False)
+        total = fresh("middle0", width(MIDDLE))
+        rim = BANK - MIDDLE.start
+        mix(total[:, 0:rim], lower[:, MIDDLE.start : BANK], kept_rest0[:, 0:rim])
+        mix(total[:, rim:], upper[:, 0 : MIDDLE.stop - BANK], kept_rest0[:, rim : width(MIDDLE)])
+        scatter(0, MIDDLE, total)
 
-        for t, front_at, front_until, rest_at, rest_until in ((1, 24, 30.5, 32, 58), (2, 14, 20, 11, 14)):
-            kept_front = placed("old_front%d" % t, front_at, width(FRONT), until=front_until)
-            gather(kept_front, t, FRONT)
-            kept_rest = placed("old_rest%d" % t, rest_at, width(REST), until=rest_until)
-            if t == 1:
-                gather(kept_rest[:, 0 : SPARE.start - REST.start], t, slice(REST.start, SPARE.start))
-                nc.vector.tensor_tensor(kept_rest[:, within(SPARE, REST)], ahead, old_all[:, SPARE], MULT)
-            else:
-                gather(kept_rest, t, REST)
-            total = keep.tile([P, width(FRONT)], F32, name="front%d" % t)
-            mix(total[:], kept_front, weighed[:, FRONT])
-            scatter(t, FRONT, total[:])
-            last_sum = placed("back%d" % (t - 1), front_at, width(left))
-            nc.gpsimd.tensor_tensor(last_sum, left_kept, left_weighed, ADD)
-            scatter(t - 1, left, last_sum)
-            store(t - 1)
-            coming = placed("new_y%d" % (t + 1), front_at + 2, T)
-            for s in range(HALVES):
-                weigh(coming[:, half(s)], half(s), project(t + 1, half(s), (HALVES * (t + 1) + s) % 3))
-            if t == 1:
-                total = keep.tile([P, width(MIDDLE)], F32, name="middle1")
-                mix(total[:], kept_rest[:, within(MIDDLE, REST)], weighed[:, MIDDLE])
-                scatter(t, MIDDLE, total[:])
-                left, left_kept, left_weighed = BACK, kept_rest[:, within(BACK, REST)], weighed[:, BACK]
-            else:
-                total = keep.tile([P, width(MIDDLE)], F32, name="middle2")
-                mix(total[:], kept_rest[:, within(MIDDLE, REST)], weighed[:, MIDDLE])
-                scatter(t, MIDDLE, total[:])
-                left, left_kept, left_weighed = BACK, kept_rest[:, within(BACK, REST)], weighed[:, BACK]
-            weighed = coming
+        kept_front = placed("old_front1", 51, width(FRONT), until=58)
+        gather(kept_front, 1, FRONT)
+        kept_rest1 = placed("old_rest1", 46, width(REST), until=50.5)
+        gather(kept_rest1, 1, REST)
+        scatter(1, FRONT, mix(fresh("front1", width(FRONT)), turn_back(1, FRONT, 5), kept_front))
+        last_sum = placed("back0", 53.5, width(BACK))
+        nc.gpsimd.tensor_tensor(last_sum, kept_rest0[:, within(BACK, REST)], upper[:, within(BACK, half(1))], ADD)
+        scatter(0, BACK, last_sum)
+        store(0)
+        y_block.extend(project_blocks(6, 1))
+        for b in range(5, BLOCKS):
+            weigh_block(b, y_block[b], (52.5, 54.5, 55.5)[b - 5], False)
+        scatter(1, MIDDLE, mix(fresh("middle1", width(MIDDLE)), turn_back(1, MIDDLE, 6), kept_rest1[:, within(MIDDLE, REST)]))
 
-        kept_others = placed("old_others3", 57, width(OTHERS))
+        kept_others = placed("old_others3", 15, width(OTHERS))
         gather(kept_others, LAST, OTHERS)
-        kept_own = placed("old_own3", 35, width(OWN), until=50)
+        kept_own = placed("old_own3", 0, width(OWN), until=12.5)
         gather(kept_own, LAST, OWN)
-        total = keep.tile([P, width(OTHERS)], F32, name="others3")
-        mix(total[:], kept_others, weighed[:, OTHERS])
-        nc.vector.tensor_tensor(window[LAST][:].indirect(names(OWN)), kept_own, weighed[:, OWN], ADD)
-        scatter(LAST, OTHERS, total[:])
-        store(LAST)
-        total = keep.tile([P, width(left)], F32, name="back2")
-        mix(total[:], left_kept, left_weighed)
-        scatter(2, left, total[:])
-        store(2)
+        kept_front = placed("old_front2", 31, width(FRONT), until=46)
+        gather(kept_front, 2, FRONT)
+        kept_rest2 = placed("old_rest2", 12.5, width(REST))
+        gather(kept_rest2, 2, REST)
+        scatter(2, FRONT, mix(fresh("front2", width(FRONT)), turn_back(2, FRONT, 3), kept_front))
 
-        pairs = [shared.tile([P, 2, width(cols), 2], BF16, name="pairs%d" % side, offset=KIB * (40, 49)[side], align_bytes=64) for side, cols in enumerate(SIDES)]
+        pairs = [shared.tile([P, 2, width(cols), 2], BF16, name="pairs%d" % side, offset=KIB * (33, 3)[side], align_bytes=64) for side, cols in enumerate(SIDES)]
 
         def round_window(t, side, copy, skip=0, stop=U // 2):
             copy(pairs[side][:, t // 2, skip:stop, t % 2], window[t][:, SIDES[side]][:, skip:stop])
 
-        for t in range(2):
-            for side in range(2):
-                round_window(t, side, vector_copy)
+        def gpsimd_round(into, values):
+            nc.gpsimd.tensor_scalar(into, values, 1.0, -0.0, MULT, ADD)
+
+        round_window(0, 0, gpsimd_round, stop=GPSIMD_SLOTS)
+        weighed = placed("new_y3", 41, T)
+        for s in range(HALVES):
+            weigh(weighed[:, half(s)], half(s), project(LAST, half(s), s))
+        scatter(1, BACK, mix(placed("back1", 45, width(BACK)), turn_back(1, BACK, 5), kept_rest1[:, within(BACK, REST)]))
+        store(1)
+        scatter(2, MIDDLE, mix(placed("middle2", 49, width(MIDDLE)), turn_back(2, MIDDLE, 6), kept_rest2[:, within(MIDDLE, REST)]))
+
+        total = mix(fresh("others3", width(OTHERS)), weighed[:, OTHERS], kept_others)
+        nc.vector.tensor_tensor(window[LAST][:].indirect(names(OWN)), kept_own, weighed[:, OWN], ADD)
+        scatter(LAST, OTHERS, total)
+        store(LAST)
+        scatter(2, BACK, mix(placed("back2", 11, width(BACK)), turn_back(2, BACK, 7), kept_rest2[:, within(BACK, REST)]))
+        store(2)
+
+        round_window(0, 0, vector_copy, skip=GPSIMD_SLOTS - EDGE)
+        for t, side in ((0, 1), (1, 0), (1, 1)):
+            round_window(t, side, vector_copy)
         round_window(LAST, 0, vector_copy, skip=EDGE)
         vector_copy(pairs[0][:, 1, 0:EDGE], window[LAST][:, 0:EDGE].unsqueeze(2).to_broadcast([P, EDGE, 2]))
         round_window(LAST, 1, vector_copy)
@@ -267,14 +306,15 @@ def tile_picked_wema_none_lo_kernel(tc, x_words, x_scales, mem, w1, old, new, sl
         out_scale = keep.tile([P, U], U8, name="out_scale", align_bytes=64)
         words_dram = out_1[0].rearrange("p c r -> p (c r)").bitcast(I32)
         grouped = {}
-        for side, copy in ((1, vector_copy), (0, scalar_copy)):
+        for side in (1, 0):
             for chunk in CHUNKS[side]:
                 four = keep.tile([P, width(chunk) * PACK], BF16, name="grouped%d" % chunk.start, align_bytes=64)
+                cols = within(chunk, SIDES[side])
                 if side == 1:
-                    copy(four[:].rearrange("p (c u e) -> p c u e", u=2, e=2), pairs[side][:, :, within(chunk, SIDES[side])].rearrange("p u c e -> p c u e"))
+                    vector_copy(four[:].rearrange("p (c u e) -> p c u e", u=2, e=2), pairs[side][:, :, cols].rearrange("p u c e -> p c u e"))
                 else:
                     pair_words = pairs[side][:].rearrange("p u c e -> p u (c e)").bitcast(F32)
-                    copy(four[:].bitcast(F32).rearrange("p (c u) -> p c u", u=2), pair_words[:, :, within(chunk, SIDES[side])].rearrange("p u c -> p c u"))
+                    scalar_copy(four[:].bitcast(F32).rearrange("p (c u) -> p c u", u=2), pair_words[:, :, cols].rearrange("p u c -> p c u"))
                 grouped[chunk.start] = four
         for chunk in CHUNKS[1] + CHUNKS[0]:
             codes = keep.tile([P, width(chunk)], U32, name="codes%d" % chunk.start, align_bytes=64)

@@ -219,7 +219,7 @@ def tile_picked_wema_none_lo_kernel(tc, x_words, x_scales, mem, w1, old, new, sl
         part_y = [project(0, part, bank) for bank, part in enumerate(parts)]
         for part, y in zip(parts, part_y):
             weigh(lower[:, part], part, y)
-        y_block = list(project_blocks(0, 0) + project_blocks(2, 1))
+        y_block = dict(zip((0, 1), project_blocks(0, 0)))
         kept_front = placed("old_front0", 20, width(FRONT), until=29.5)
         front_halves = (slice(0, width(FRONT) // 2), slice(width(FRONT) // 2, FRONT.stop))
         for piece in front_halves:
@@ -234,12 +234,11 @@ def tile_picked_wema_none_lo_kernel(tc, x_words, x_scales, mem, w1, old, new, sl
         nc.gpsimd.tensor_tensor(kept_rest0, plain, old_all[:, REST], MULT)
         for b in range(2):
             weigh_block(b, y_block[b], 22 + b, False)
-        for b in range(2, 4):
-            weigh_block(b, y_block[b], 22 + b, True)
         upper = placed("upper_y0", 29, BANK, until=31.5)
         weigh(upper, half(1), project(0, half(1), 2))
-        y_block.extend(project_blocks(4, 0))
-        weigh_block(4, y_block[4], 26, False)
+        for first, bank, on_scalar in ((4, 1, False), (2, 0, True)):
+            for b, y in enumerate(project_blocks(first, bank), first):
+                weigh_block(b, y, 22 + b, on_scalar)
         total = fresh("middle0", width(MIDDLE))
         rim = BANK - MIDDLE.start
         mix(total[:, 0:rim], lower[:, MIDDLE.start : BANK], kept_rest0[:, 0:rim])
@@ -255,9 +254,8 @@ def tile_picked_wema_none_lo_kernel(tc, x_words, x_scales, mem, w1, old, new, sl
         nc.gpsimd.tensor_tensor(last_sum, kept_rest0[:, within(BACK, REST)], upper[:, within(BACK, half(1))], ADD)
         scatter(0, BACK, last_sum)
         store(0)
-        y_block.extend(project_blocks(6, 1))
-        for b in range(5, BLOCKS):
-            weigh_block(b, y_block[b], (52.5, 54.5, 55.5)[b - 5], False)
+        for b, y in enumerate(project_blocks(6, 1), 6):
+            weigh_block(b, y, 48.5 + b, False)
         scatter(1, MIDDLE, mix(fresh("middle1", width(MIDDLE)), turn_back(1, MIDDLE, 6), kept_rest1[:, within(MIDDLE, REST)]))
 
         kept_others = placed("old_others3", 15, width(OTHERS))

@@ -38,7 +38,8 @@ W_VECTOR = 88
 SIDES = (slice(0, U // 2), slice(U // 2, U))
 CHUNKS = ((slice(0, 512), slice(512, 768), slice(768, 1024)), (slice(1024, 1536), slice(1536, U)))
 EDGE = 4
-GPSIMD_SLOTS = 896
+SCALAR_ROUNDS = 896
+GPSIMD_SLOTS = 1152
 
 
 def tile_picked_wema_none_lo_kernel(tc, x_words, x_scales, mem, w1, old, new, slot, out_0, out_1, out_2):
@@ -110,7 +111,7 @@ def tile_picked_wema_none_lo_kernel(tc, x_words, x_scales, mem, w1, old, new, sl
         for t in (1, LAST, 2):
             nc.sync.dma_start(out=window[t][:], in_=mem_rows[t])
 
-        old_all = keep.tile([P, T], F32, name="old_all")
+        old_all = placed("old_all", 68, T, until=73)
         new_all = keep.tile([P, T], F32, name="new_all")
         new_by_block = keep.tile([P, BLOCKS], F32, name="new_by_block")
 
@@ -118,10 +119,10 @@ def tile_picked_wema_none_lo_kernel(tc, x_words, x_scales, mem, w1, old, new, sl
             turned = bank_tile(bank, "spread%d" % bank)
             for i in range(PACK):
                 nc.tensor.transpose(turned[:, P * i : P * (i + 1)], cols[:, PACK * s + i : PACK * s + i + 1].to_broadcast([P, P]), ident[:])
-            scalar_copy(whole[:].rearrange("m (p s i) -> m s p i", s=HALVES, i=PACK)[:, s], turned[:].rearrange("m (i p) -> m p i", i=PACK))
+            scalar_copy(whole.rearrange("m (p s i) -> m s p i", s=HALVES, i=PACK)[:, s], turned[:].rearrange("m (i p) -> m p i", i=PACK))
 
-        spread(new_cols, new_all, 0, 3)
-        spread(new_cols, new_all, 1, 2)
+        spread(new_cols, new_all[:], 0, 3)
+        spread(new_cols, new_all[:], 1, 2)
 
         def new_on_partitions(s, bank):
             turned = bank_tile(bank, "new_turned%d" % s)
@@ -268,15 +269,15 @@ def tile_picked_wema_none_lo_kernel(tc, x_words, x_scales, mem, w1, old, new, sl
         gather(kept_rest2, 2, REST)
         scatter(2, FRONT, mix(fresh("front2", width(FRONT)), turn_back(2, FRONT, 3), kept_front))
 
-        pairs = [shared.tile([P, 2, width(cols), 2], BF16, name="pairs%d" % side, offset=KIB * (33, 3)[side], align_bytes=64) for side, cols in enumerate(SIDES)]
+        pairs = shared.tile([P, 2, U, 2], BF16, name="pairs", offset=KIB * 72, align_bytes=64)
 
-        def round_window(t, side, copy, skip=0, stop=U // 2):
-            copy(pairs[side][:, t // 2, skip:stop, t % 2], window[t][:, SIDES[side]][:, skip:stop])
+        def round_window(t, slots, copy):
+            copy(pairs[:, t // 2, slots, t % 2], window[t][:, slots])
 
         def gpsimd_round(into, values):
             nc.gpsimd.tensor_scalar(into, values, 1.0, -0.0, MULT, ADD)
 
-        round_window(0, 0, gpsimd_round, stop=GPSIMD_SLOTS)
+        round_window(0, slice(0, GPSIMD_SLOTS), gpsimd_round)
         weighed = placed("new_y3", 41, T)
         for s in range(HALVES):
             weigh(weighed[:, half(s)], half(s), project(LAST, half(s), s))
@@ -291,15 +292,14 @@ def tile_picked_wema_none_lo_kernel(tc, x_words, x_scales, mem, w1, old, new, sl
         scatter(2, BACK, mix(placed("back2", 11, width(BACK)), turn_back(2, BACK, 7), kept_rest2[:, within(BACK, REST)]))
         store(2)
 
-        round_window(0, 0, vector_copy, skip=GPSIMD_SLOTS - EDGE)
-        for t, side in ((0, 1), (1, 0), (1, 1)):
-            round_window(t, side, vector_copy)
-        round_window(LAST, 0, vector_copy, skip=EDGE)
-        vector_copy(pairs[0][:, 1, 0:EDGE], window[LAST][:, 0:EDGE].unsqueeze(2).to_broadcast([P, EDGE, 2]))
-        round_window(LAST, 1, vector_copy)
-        round_window(2, 0, scalar_copy)
-        round_window(2, 1, vector_copy, stop=BANK)
-        round_window(2, 1, vector_copy, skip=BANK)
+        round_window(0, slice(GPSIMD_SLOTS - EDGE, U), vector_copy)
+        round_window(1, slice(0, U), vector_copy)
+        round_window(LAST, slice(EDGE, SIDES[0].stop), vector_copy)
+        vector_copy(pairs[:, 1, 0:EDGE], window[LAST][:, 0:EDGE].unsqueeze(2).to_broadcast([P, EDGE, 2]))
+        round_window(LAST, SIDES[1], vector_copy)
+        round_window(2, slice(0, SCALAR_ROUNDS), scalar_copy)
+        round_window(2, slice(SCALAR_ROUNDS, CHUNKS[1][0].stop), vector_copy)
+        round_window(2, CHUNKS[1][1], vector_copy)
 
         out_scale = keep.tile([P, U], U8, name="out_scale", align_bytes=64)
         words_dram = out_1[0].rearrange("p c r -> p (c r)").bitcast(I32)
@@ -307,12 +307,11 @@ def tile_picked_wema_none_lo_kernel(tc, x_words, x_scales, mem, w1, old, new, sl
         for side in (1, 0):
             for chunk in CHUNKS[side]:
                 four = keep.tile([P, width(chunk) * PACK], BF16, name="grouped%d" % chunk.start, align_bytes=64)
-                cols = within(chunk, SIDES[side])
                 if side == 1:
-                    vector_copy(four[:].rearrange("p (c u e) -> p c u e", u=2, e=2), pairs[side][:, :, cols].rearrange("p u c e -> p c u e"))
+                    vector_copy(four[:].rearrange("p (c u e) -> p c u e", u=2, e=2), pairs[:, :, chunk].rearrange("p u c e -> p c u e"))
                 else:
-                    pair_words = pairs[side][:].rearrange("p u c e -> p u (c e)").bitcast(F32)
-                    scalar_copy(four[:].bitcast(F32).rearrange("p (c u) -> p c u", u=2), pair_words[:, :, cols].rearrange("p u c -> p c u"))
+                    pair_words = pairs[:].rearrange("p u c e -> p u (c e)").bitcast(F32)
+                    scalar_copy(four[:].bitcast(F32).rearrange("p (c u) -> p c u", u=2), pair_words[:, :, chunk].rearrange("p u c -> p c u"))
                 grouped[chunk.start] = four
         for chunk in CHUNKS[1] + CHUNKS[0]:
             codes = keep.tile([P, width(chunk)], U32, name="codes%d" % chunk.start, align_bytes=64)

@@ -33,13 +33,14 @@ STRIPE = 16
 
 FRONT, MIDDLE, BACK = slice(0, 384), slice(384, 768), slice(768, T)
 REST = slice(FRONT.stop, T)
+ENTRIES = slice(0, T)
 OWN, OTHERS = slice(0, 704), slice(704, T)
 W_VECTOR = 88
 SIDES = (slice(0, U // 2), slice(U // 2, U))
 CHUNKS = ((slice(0, 512), slice(512, 768), slice(768, 1024)), (slice(1024, 1536), slice(1536, U)))
-EDGE = 4
 SCALAR_ROUNDS = 896
 GPSIMD_SLOTS = 1152
+EDGE = 4
 
 
 def tile_picked_wema_none_lo_kernel(tc, x_words, x_scales, mem, w1, old, new, slot, out_0, out_1, out_2):
@@ -75,7 +76,6 @@ def tile_picked_wema_none_lo_kernel(tc, x_words, x_scales, mem, w1, old, new, sl
         ident = keep.tile([P, P], F32, name="ident")
         make_identity(nc, ident[:])
 
-
         xw_dram = x_words.bitcast(I32)
         xs_dram = x_scales.bitcast(I32)
         mem_rows = mem.rearrange("(p t) u -> t p u", t=PACK)
@@ -85,8 +85,7 @@ def tile_picked_wema_none_lo_kernel(tc, x_words, x_scales, mem, w1, old, new, sl
         w_raw = [keep.tile([P, PACK, N], F32, name="w_raw%d" % z) for z in range(PASSES)]
         x_word = [keep.tile([P, PASSES, 2 * BANK], U8, name="x_word%d" % s, align_bytes=64) for s in range(HALVES)]
         x_scale = keep.tile([P, PASSES, T], U8, name="x_scale", align_bytes=64)
-        window = [shared.tile([P, U], F32, name="window0", offset=60 * KIB, align_bytes=64)]
-        window.extend(keep.tile([P, U], F32, name="window%d" % t) for t in range(1, PACK))
+        window = [keep.tile([P, U], F32, name="window%d" % t) for t in range(PACK)]
 
         def load_w(z):
             nc.sync.dma_start(out=w_raw[z][:], in_=w1[K_PASS * z : K_PASS * (z + 1), :].rearrange("(p i) n -> p i n", i=PACK))
@@ -108,10 +107,10 @@ def tile_picked_wema_none_lo_kernel(tc, x_words, x_scales, mem, w1, old, new, sl
         load_x(0)
         nc.sync.dma_start(out=window[0][:], in_=mem_rows[0])
         load_x(1)
-        for t in (1, LAST, 2):
+        for t in range(1, PACK):
             nc.sync.dma_start(out=window[t][:], in_=mem_rows[t])
 
-        old_all = placed("old_all", 68, T, until=73)
+        old_all = placed("old_all", 68, T, until=79)
         new_all = keep.tile([P, T], F32, name="new_all")
         new_by_block = keep.tile([P, BLOCKS], F32, name="new_by_block")
 
@@ -220,7 +219,7 @@ def tile_picked_wema_none_lo_kernel(tc, x_words, x_scales, mem, w1, old, new, sl
         part_y = [project(0, part, bank) for bank, part in enumerate(parts)]
         for part, y in zip(parts, part_y):
             weigh(lower[:, part], part, y)
-        y_block = dict(zip((0, 1), project_blocks(0, 0)))
+        first_blocks = project_blocks(0, 0)
         kept_front = placed("old_front0", 20, width(FRONT), until=29.5)
         front_halves = (slice(0, width(FRONT) // 2), slice(width(FRONT) // 2, FRONT.stop))
         for piece in front_halves:
@@ -233,9 +232,9 @@ def tile_picked_wema_none_lo_kernel(tc, x_words, x_scales, mem, w1, old, new, sl
         scatter(0, FRONT, total)
         kept_rest0 = placed("old_rest0", 12, width(REST), until=20.5)
         nc.gpsimd.tensor_tensor(kept_rest0, plain, old_all[:, REST], MULT)
-        for b in range(2):
-            weigh_block(b, y_block[b], 22 + b, False)
-        upper = placed("upper_y0", 29, BANK, until=31.5)
+        for b, y in enumerate(first_blocks):
+            weigh_block(b, y, 22 + b, False)
+        upper = placed("upper_y0", 29, BANK)
         weigh(upper, half(1), project(0, half(1), 2))
         for first, bank, on_scalar in ((4, 1, False), (2, 0, True)):
             for b, y in enumerate(project_blocks(first, bank), first):
@@ -259,17 +258,13 @@ def tile_picked_wema_none_lo_kernel(tc, x_words, x_scales, mem, w1, old, new, sl
             weigh_block(b, y, 48.5 + b, False)
         scatter(1, MIDDLE, mix(fresh("middle1", width(MIDDLE)), turn_back(1, MIDDLE, 6), kept_rest1[:, within(MIDDLE, REST)]))
 
-        kept_others = placed("old_others3", 15, width(OTHERS))
-        gather(kept_others, LAST, OTHERS)
-        kept_own = placed("old_own3", 0, width(OWN), until=12.5)
-        gather(kept_own, LAST, OWN)
-        kept_front = placed("old_front2", 31, width(FRONT), until=46)
-        gather(kept_front, 2, FRONT)
-        kept_rest2 = placed("old_rest2", 12.5, width(REST))
-        gather(kept_rest2, 2, REST)
-        scatter(2, FRONT, mix(fresh("front2", width(FRONT)), turn_back(2, FRONT, 3), kept_front))
+        kept2 = placed("old2", 12.5, T)
+        gather(kept2, 2, ENTRIES)
+        kept3 = placed("old3", 0, T, until=12.5)
+        gather(kept3, LAST, ENTRIES)
+        scatter(2, FRONT, mix(placed("front2", 72, width(FRONT)), turn_back(2, FRONT, 3), kept2[:, FRONT]))
 
-        pairs = shared.tile([P, 2, U, 2], BF16, name="pairs", offset=KIB * 72, align_bytes=64)
+        pairs = shared.tile([P, 2, U, 2], BF16, name="pairs", offset=int(KIB * 78.5), align_bytes=64)
 
         def round_window(t, slots, copy):
             copy(pairs[:, t // 2, slots, t % 2], window[t][:, slots])
@@ -278,18 +273,18 @@ def tile_picked_wema_none_lo_kernel(tc, x_words, x_scales, mem, w1, old, new, sl
             nc.gpsimd.tensor_scalar(into, values, 1.0, -0.0, MULT, ADD)
 
         round_window(0, slice(0, GPSIMD_SLOTS), gpsimd_round)
-        weighed = placed("new_y3", 41, T)
+        weighed = placed("new_y3", 73.5, T)
         for s in range(HALVES):
             weigh(weighed[:, half(s)], half(s), project(LAST, half(s), s))
-        scatter(1, BACK, mix(placed("back1", 45, width(BACK)), turn_back(1, BACK, 5), kept_rest1[:, within(BACK, REST)]))
+        scatter(1, BACK, mix(placed("back1", 77.5, width(BACK)), turn_back(1, BACK, 5), kept_rest1[:, within(BACK, REST)]))
         store(1)
-        scatter(2, MIDDLE, mix(placed("middle2", 49, width(MIDDLE)), turn_back(2, MIDDLE, 6), kept_rest2[:, within(MIDDLE, REST)]))
+        scatter(2, MIDDLE, mix(placed("middle2", 49, width(MIDDLE)), turn_back(2, MIDDLE, 6), kept2[:, MIDDLE]))
 
-        total = mix(fresh("others3", width(OTHERS)), weighed[:, OTHERS], kept_others)
-        nc.vector.tensor_tensor(window[LAST][:].indirect(names(OWN)), kept_own, weighed[:, OWN], ADD)
+        total = mix(fresh("others3", width(OTHERS)), weighed[:, OTHERS], kept3[:, OTHERS])
+        nc.vector.tensor_tensor(window[LAST][:].indirect(names(OWN)), kept3[:, OWN], weighed[:, OWN], ADD)
         scatter(LAST, OTHERS, total)
         store(LAST)
-        scatter(2, BACK, mix(placed("back2", 11, width(BACK)), turn_back(2, BACK, 7), kept_rest2[:, within(BACK, REST)]))
+        scatter(2, BACK, mix(placed("back2", 11, width(BACK)), turn_back(2, BACK, 7), kept2[:, BACK]))
         store(2)
 
         round_window(0, slice(GPSIMD_SLOTS - EDGE, U), vector_copy)

from contextlib import ExitStack

import concourse.mybir as mybir
from concourse.masks import make_identity

K, T, N, U = 1024, 1024, 512, 2048
FLOPS = 2 * K * N * T

F32 = mybir.dt.float32
BF16 = mybir.dt.bfloat16
I32 = mybir.dt.int32
U32 = mybir.dt.uint32
U16 = mybir.dt.uint16
U8 = mybir.dt.uint8
FP8X4 = mybir.dt.float8_e4m3fn_x4
FP4X4 = mybir.dt.float4_e2m1fn_x4
COPY = mybir.ActivationFunctionType.Copy
MULT = mybir.AluOpType.mult
ADD = mybir.AluOpType.add

P = 128
PACK = 4
K_PASS = P * PACK
PASSES = K // K_PASS
QUADRANT = 32
SCALE_ROWS = 16
BANK = 512
HALVES = T // BANK
BLOCKS = T // P
LAST = PACK - 1
KIB = 1024
STRIPE = 16

FRONT, MIDDLE, BACK = slice(0, 384), slice(384, 768), slice(768, T)
REST = slice(FRONT.stop, T)
ENTRIES = slice(0, T)
OWN, OTHERS = slice(0, 704), slice(704, T)
W_VECTOR = 88
SIDES = (slice(0, U // 2), slice(U // 2, U))
CHUNKS = ((slice(0, 512), slice(512, 768), slice(768, 1024)), (slice(1024, 1536), slice(1536, U)))
SCALAR_ROUNDS = 896
GPSIMD_SLOTS = 1152
EDGE = 4


def tile_picked_wema_none_lo_kernel(tc, x_words, x_scales, mem, w1, old, new, slot, out_0, out_1, out_2):
    nc = tc.nc
    scalar_copy, vector_copy = nc.scalar.copy, nc.vector.tensor_copy

    def half(s):
        return slice(BANK * s, BANK * (s + 1))

    def width(piece):
        return piece.stop - piece.start

    def within(piece, whole):
        return slice(piece.start - whole.start, piece.stop - whole.start)

    with ExitStack() as ctx:
        keep = ctx.enter_context(tc.tile_pool(name="keep", bufs=1))
        shared = ctx.enter_context(tc.tile_pool(name="shared", bufs=1))
        psum = ctx.enter_context(tc.psum_pool(name="psum", bufs=1))

        def bank_tile(bank, name):
            return psum.tile([P, BANK], F32, name=name, offset=4 * BANK * bank)

        def placed(name, at, columns, until=None):
            room = columns if until is None else int((until - at) * KIB) // 4
            tile = shared.tile([P, room], F32, name=name, offset=int(KIB * at), align_bytes=64)
            return tile[:, 0:columns]

        def fresh(name, columns):
            return keep.tile([P, columns], F32, name=name)[:]

        offs = keep.tile([P, T // STRIPE], U16, name="offs")
        ident = keep.tile([P, P], F32, name="ident")
        make_identity(nc, ident[:])

        xw_dram = x_words.bitcast(I32)
        xs_dram = x_scales.bitcast(I32)
        mem_rows = mem.rearrange("(p t) u -> t p u", t=PACK)
        out_rows = out_0.rearrange("(p t) u -> t p u", t=PACK)
        old_cols = keep.tile([P, BLOCKS], F32, name="old_cols")
        new_cols = keep.tile([P, BLOCKS], F32, name="new_cols")
        w_raw = [keep.tile([P, PACK, N], F32, name="w_raw%d" % z) for z in range(PASSES)]
        x_word = [keep.tile([P, PASSES, 2 * BANK], U8, name="x_word%d" % s, align_bytes=64) for s in range(HALVES)]
        x_scale = keep.tile([P, PASSES, T], U8, name="x_scale", align_bytes=64)
        window = [keep.tile([P, U], F32, name="window%d" % t) for t in range(PACK)]

        def load_w(z):
            nc.sync.dma_start(out=w_raw[z][:], in_=w1[K_PASS * z : K_PASS * (z + 1), :].rearrange("(p i) n -> p i n", i=PACK))

        def load_x(s):
            ints = BANK // 2
            nc.sync.dma_start(out=x_word[s][:].bitcast(I32), in_=xw_dram[:, :, ints * s : ints * (s + 1)].rearrange("z p c -> p z c"))

        def load_row(cols, rows):
            nc.sync.dma_start(out=cols[:], in_=rows[0:1, :].rearrange("o (p b) -> (o p) b", p=P))

        load_row(new_cols, new)
        load_w(0)
        load_row(old_cols, old)
        nc.sync.dma_start(offs[:], slot)
        for r in range(PACK):
            nc.sync.dma_start(out=x_scale[r:P:QUADRANT, :, :].bitcast(I32), in_=xs_dram[:, r:SCALE_ROWS:PACK, :].rearrange("z q c -> q z c"))
        load_w(1)
        load_x(0)
        nc.sync.dma_start(out=window[0][:], in_=mem_rows[0])
        load_x(1)
        for t in range(1, PACK):
            nc.sync.dma_start(out=window[t][:], in_=mem_rows[t])

        old_all = placed("old_all", 68, T, until=79)
        new_all = keep.tile([P, T], F32, name="new_all")
        new_by_block = keep.tile([P, BLOCKS], F32, name="new_by_block")

        def spread(cols, whole, s, bank):
            turned = bank_tile(bank, "spread%d" % bank)
            for i in range(PACK):
                nc.tensor.transpose(turned[:, P * i : P * (i + 1)], cols[:, PACK * s + i : PACK * s + i + 1].to_broadcast([P, P]), ident[:])
            scalar_copy(whole.rearrange("m (p s i) -> m s p i", s=HALVES, i=PACK)[:, s], turned[:].rearrange("m (i p) -> m p i", i=PACK))

        spread(new_cols, new_all[:], 0, 3)
        spread(new_cols, new_all[:], 1, 2)

        def new_on_partitions(s, bank):
            turned = bank_tile(bank, "new_turned%d" % s)
            for i in range(PACK):
                nc.tensor.transpose(turned[:, P * i : P * (i + 1)], new_all[:, BANK * s + P * i : BANK * s + P * (i + 1)], ident[:])
            scalar_copy(new_by_block[:, PACK * s : PACK * (s + 1)], turned[:, 0:BANK:P])

        new_on_partitions(0, 4)
        new_on_partitions(1, 5)
        spread(old_cols, old_all, 0, 0)
        spread(old_cols, old_all, 1, 1)

        w_mx = {}

        def quantise_w(z, shares, groups):
            grouped = keep.tile([P, N * PACK], BF16, name="w_grouped%d" % z, align_bytes=64)
            laid = grouped[:].rearrange("p (t m i) -> p m i t", t=PACK, i=PACK)
            raw = w_raw[z][:].rearrange("p i (m t) -> p m i t", t=PACK)
            for copy, ms in shares:
                copy(laid[:, ms], raw[:, ms])
            for group in groups:
                cols = P * len(group)
                codes = keep.tile([P, cols], U32, name="w_codes%d_%d" % (z, group.start), align_bytes=64)
                scales = keep.tile([P, cols], U8, name="w_scales%d_%d" % (z, group.start), align_bytes=64)
                nc.vector.quantize_mx(out=codes[:].bitcast(FP8X4), scales=scales[:], in_=grouped[:, K_PASS * group.start : K_PASS * group.stop])
                for i, t in enumerate(group):
                    w_mx[(t, z)] = (codes, scales, P * i)

        def w_operand(t, z, windows):
            codes, scales, first = w_mx[(t, z)]
            cols = slice(first, first + P * windows)
            return codes[:, cols].bitcast(FP8X4), scales[:, cols]

        def x_operand(piece, z):
            s, skip = divmod(piece.start, BANK)
            return x_word[s][:, z, 2 * skip : 2 * (skip + width(piece))].bitcast(FP4X4), x_scale[:, z, piece]

        def multiply(out, stationary, moving):
            for z in range(PASSES):
                (lhs, lhs_scale), (rhs, rhs_scale) = stationary(z), moving(z)
                nc.tensor.matmul_mx(out=out, lhsT=lhs, lhsT_scale=lhs_scale, rhs=rhs, rhs_scale=rhs_scale, start=(z == 0), stop=(z == PASSES - 1))

        def project(t, piece, bank):
            y = bank_tile(bank, "y%d_%d" % (t, piece.start))[:, 0 : width(piece)]
            multiply(y, lambda z: w_operand(t, z, 1), lambda z: x_operand(piece, z))
            return y

        def project_blocks(first, bank):
            both = bank_tile(bank, "y_blocks%d" % first)
            for i in range(2):
                block = slice(P * (first + i), P * (first + i + 1))
                multiply(both[:, 2 * P * i : 2 * P * (i + 1)], lambda z: x_operand(block, z), lambda z: w_operand(1, z, 2))
            return both[:, 0 : 2 * P], both[:, 2 * P : 4 * P]

        weighed_block = {}

        def weigh_block(b, y, at, on_scalar):
            into = placed("new_y_block%d" % b, at, 2 * P)
            if on_scalar:
                nc.scalar.activation(into, y, COPY, scale=new_by_block[:, b : b + 1])
            else:
                nc.vector.tensor_scalar(into, y, new_by_block[:, b : b + 1], None, MULT)
            weighed_block[b] = into

        def turn_back(t, piece, bank):
            back = bank_tile(bank, "turned%d_%d" % (t, piece.start))
            for i, b in enumerate(range(piece.start // P, piece.stop // P)):
                nc.tensor.transpose(back[:, P * i : P * (i + 1)], weighed_block[b][:, P * (t - 1) : P * t], ident[:])
            return back[:, 0 : width(piece)]

        def names(piece):
            return offs[:, piece.start // STRIPE : piece.stop // STRIPE]

        def weigh(into, piece, y):
            nc.vector.tensor_tensor(into, y, new_all[:, piece], MULT)

        def gather(into, t, piece):
            nc.vector.tensor_tensor(into, window[t][:].indirect(names(piece)), old_all[:, piece], MULT)

        def mix(into, weighed, kept):
            nc.vector.tensor_tensor(into, weighed, kept, ADD)
            return into

        def scatter(t, piece, total):
            nc.scalar.activation(window[t][:].indirect(names(piece)), total, COPY)

        def store(t):
            nc.sync.dma_start(out=out_rows[t], in_=window[t][:])

        quantise_w(0, ((vector_copy, slice(0, P)),), (range(0, PACK),))
        quantise_w(1, ((vector_copy, slice(0, W_VECTOR)), (scalar_copy, slice(W_VECTOR, P))), (range(0, 1), range(1, PACK)))

        lower = placed("lower_y0", 46, BANK, until=52)
        parts = (slice(0, 2 * P), slice(2 * P, FRONT.stop), slice(FRONT.stop, BANK))
        part_y = [project(0, part, bank) for bank, part in enumerate(parts)]
        for part, y in zip(parts, part_y):
            weigh(lower[:, part], part, y)
        first_blocks = project_blocks(0, 0)
        kept_front = placed("old_front0", 20, width(FRONT), until=29.5)
        front_halves = (slice(0, width(FRONT) // 2), slice(width(FRONT) // 2, FRONT.stop))
        for piece in front_halves:
            gather(kept_front[:, piece], 0, piece)
        plain = fresh("plain0", width(REST))
        nc.scalar.activation(plain, window[0][:].indirect(names(REST)), COPY)
        total = fresh("front0", width(FRONT))
        for piece in front_halves:
            mix(total[:, piece], lower[:, piece], kept_front[:, piece])
        scatter(0, FRONT, total)
        kept_rest0 = placed("old_rest0", 12, width(REST), until=20.5)
        nc.gpsimd.tensor_tensor(kept_rest0, plain, old_all[:, REST], MULT)
        for b, y in enumerate(first_blocks):
            weigh_block(b, y, 22 + b, False)
        upper = placed("upper_y0", 29, BANK)
        weigh(upper, half(1), project(0, half(1), 2))
        for first, bank, on_scalar in ((4, 1, False), (2, 0, True)):
            for b, y in enumerate(project_blocks(first, bank), first):
                weigh_block(b, y, 22 + b, on_scalar)
        total = fresh("middle0", width(MIDDLE))
        rim = BANK - MIDDLE.start
        mix(total[:, 0:rim], lower[:, MIDDLE.start : BANK], kept_rest0[:, 0:rim])
        mix(total[:, rim:], upper[:, 0 : MIDDLE.stop - BANK], kept_rest0[:, rim : width(MIDDLE)])
        scatter(0, MIDDLE, total)

        kept_front = placed("old_front1", 51, width(FRONT), until=58)
        gather(kept_front, 1, FRONT)
        kept_rest1 = placed("old_rest1", 46, width(REST), until=50.5)
        gather(kept_rest1, 1, REST)
        scatter(1, FRONT, mix(fresh("front1", width(FRONT)), turn_back(1, FRONT, 5), kept_front))
        last_sum = placed("back0", 53.5, width(BACK))
        nc.gpsimd.tensor_tensor(last_sum, kept_rest0[:, within(BACK, REST)], upper[:, within(BACK, half(1))], ADD)
        scatter(0, BACK, last_sum)
        store(0)
        for b, y in enumerate(project_blocks(6, 1), 6):
            weigh_block(b, y, 48.5 + b, False)
        scatter(1, MIDDLE, mix(fresh("middle1", width(MIDDLE)), turn_back(1, MIDDLE, 6), kept_rest1[:, within(MIDDLE, REST)]))

        kept2 = placed("old2", 12.5, T)
        gather(kept2, 2, ENTRIES)
        kept3 = placed("old3", 0, T, until=12.5)
        gather(kept3, LAST, ENTRIES)
        scatter(2, FRONT, mix(placed("front2", 72, width(FRONT)), turn_back(2, FRONT, 3), kept2[:, FRONT]))

        pairs = shared.tile([P, 2, U, 2], BF16, name="pairs", offset=int(KIB * 78.5), align_bytes=64)

        def round_window(t, slots, copy):
            copy(pairs[:, t // 2, slots, t % 2], window[t][:, slots])

        def gpsimd_round(into, values):
            nc.gpsimd.tensor_scalar(into, values, 1.0, -0.0, MULT, ADD)

        round_window(0, slice(0, GPSIMD_SLOTS), gpsimd_round)
        weighed = placed("new_y3", 73.5, T)
        for s in range(HALVES):
            weigh(weighed[:, half(s)], half(s), project(LAST, half(s), s))
        scatter(1, BACK, mix(placed("back1", 77.5, width(BACK)), turn_back(1, BACK, 5), kept_rest1[:, within(BACK, REST)]))
        store(1)
        scatter(2, MIDDLE, mix(placed("middle2", 49, width(MIDDLE)), turn_back(2, MIDDLE, 6), kept2[:, MIDDLE]))

        total = mix(fresh("others3", width(OTHERS)), weighed[:, OTHERS], kept3[:, OTHERS])
        nc.vector.tensor_tensor(window[LAST][:].indirect(names(OWN)), kept3[:, OWN], weighed[:, OWN], ADD)
        scatter(LAST, OTHERS, total)
        store(LAST)
        scatter(2, BACK, mix(placed("back2", 11, width(BACK)), turn_back(2, BACK, 7), kept2[:, BACK]))
        store(2)

        round_window(0, slice(GPSIMD_SLOTS - EDGE, U), vector_copy)
        round_window(1, slice(0, U), vector_copy)
        round_window(LAST, slice(EDGE, SIDES[0].stop), vector_copy)
        vector_copy(pairs[:, 1, 0:EDGE], window[LAST][:, 0:EDGE].unsqueeze(2).to_broadcast([P, EDGE, 2]))
        round_window(LAST, SIDES[1], vector_copy)
        round_window(2, slice(0, SCALAR_ROUNDS), scalar_copy)
        round_window(2, slice(SCALAR_ROUNDS, CHUNKS[1][0].stop), vector_copy)
        round_window(2, CHUNKS[1][1], vector_copy)

        out_scale = keep.tile([P, U], U8, name="out_scale", align_bytes=64)
        words_dram = out_1[0].rearrange("p c r -> p (c r)").bitcast(I32)
        grouped = {}
        for side in (1, 0):
            for chunk in CHUNKS[side]:
                four = keep.tile([P, width(chunk) * PACK], BF16, name="grouped%d" % chunk.start, align_bytes=64)
                if side == 1:
                    vector_copy(four[:].rearrange("p (c u e) -> p c u e", u=2, e=2), pairs[:, :, chunk].rearrange("p u c e -> p c u e"))
                else:
                    pair_words = pairs[:].rearrange("p u c e -> p u (c e)").bitcast(F32)
                    scalar_copy(four[:].bitcast(F32).rearrange("p (c u) -> p c u", u=2), pair_words[:, :, chunk].rearrange("p u c -> p c u"))
                grouped[chunk.start] = four
        for chunk in CHUNKS[1] + CHUNKS[0]:
            codes = keep.tile([P, width(chunk)], U32, name="codes%d" % chunk.start, align_bytes=64)
            nc.vector.quantize_mx(out=codes[:].bitcast(FP8X4), scales=out_scale[:, chunk], in_=grouped[chunk.start][:])
            nc.sync.dma_start(out=words_dram[:, chunk], in_=codes[:].bitcast(I32))
        scales_dram = out_2[0].bitcast(I32)
        for r in range(PACK):
            queue = nc.scalar if r >= PACK // 2 else nc.sync
            queue.dma_start(out=scales_dram[r:SCALE_ROWS:PACK, :], in_=out_scale[r:P:QUADRANT, :].bitcast(I32))
